import numpy as np
import ml_dtypes


def mxq(x, axis, fmt="e4m3"):
    dtype, down = {"e4m3": (ml_dtypes.float8_e4m3fn, 7), "e5m2": (ml_dtypes.float8_e5m2, 14)}[fmt]
    v = np.moveaxis(np.asarray(x, np.float32).astype(ml_dtypes.bfloat16).astype(np.float64), axis, -1)
    blocks = v.reshape(v.shape[:-1] + (-1, 32))
    amax = np.abs(blocks).max(-1, keepdims=True)
    byte = np.maximum(np.where(amax > 0, np.frexp(amax)[1] - 1 + 127, 0) - down, 1)
    scale = np.exp2(byte - 127.0)
    codes = (blocks / scale).astype(np.float32).astype(dtype).astype(np.float64)
    return np.moveaxis((codes * scale).reshape(v.shape), -1, axis)


WIDE = False


def mx_kscale(k):
    if not WIDE:
        return np.ones(k)
    levels = np.array([10, -10, 5, -5, 0])
    if k % 512:
        return np.exp2(np.random.permutation(np.resize(levels, k // 32))).repeat(32)
    a = np.empty((k // 512, 16))
    for p in range(k // 512):
        a[p, :8] = np.random.permutation(np.resize(levels, 8))
        for g in range(8):
            far = levels[np.abs(levels - a[p, g]) >= 10]
            a[p, g + 8] = far[np.random.randint(len(far))]
    return np.exp2(a.ravel()).repeat(32)


def f64(x):
    return np.asarray(x).astype(np.float64)


def striped(idx):
    return np.tile(np.asarray(idx).reshape(-1, 16).T, (8, 1)).astype(np.uint16)


def unstriped(offs):
    return offs[:16].T.reshape(-1).astype(np.int64)


E2M1 = np.array([0.0, 0.5, 1.0, 1.5, 2.0, 3.0, 4.0, 6.0, -0.0, -0.5, -1.0, -1.5, -2.0, -3.0, -4.0, -6.0])


def pack_weight(w, fmt):
    k, n = w.shape
    w = f64(np.asarray(w, np.float32).astype(ml_dtypes.bfloat16)).reshape(k // 32, 32, n)
    amax = np.abs(w).max(1)
    if fmt == "e4m3":
        byte = np.frexp(amax)[1] - 1 + 127 - 7
    else:
        mant, ex = np.frexp(amax / 6.0)
        byte = np.where(mant > 0.5, ex, ex - 1) + 127
    byte = np.clip(np.where(amax > 0, byte, 1), 1, 254)
    scaled = (w * np.exp2(127.0 - byte)[:, None, :]).reshape(k, n).astype(np.float32)
    by_word = np.ascontiguousarray(scaled.reshape(k // 512, 128, 4, n).transpose(0, 1, 3, 2))
    if fmt == "e4m3":
        words = by_word.astype(ml_dtypes.float8_e4m3fn).view(np.uint8)
    else:
        c = by_word.astype(ml_dtypes.float4_e2m1fn).view(np.uint8) & 0xF
        words = (c[..., 0::2] | (c[..., 1::2] << 4)).reshape(k // 512, 128, 2 * n)
    return np.ascontiguousarray(words), np.ascontiguousarray(byte.astype(np.uint8).reshape(k // 512, 16, n))


def unpack_weight(words, scales, fmt):
    g, _, n = scales.shape
    words = np.ascontiguousarray(words).reshape(g, 128, n, -1)
    if fmt == "e4m3":
        vals = words.view(ml_dtypes.float8_e4m3fn).astype(np.float64)
    else:
        nib = np.empty((g, 128, n, 4), np.uint8)
        nib[..., 0::2] = words & 0xF
        nib[..., 1::2] = words >> 4
        vals = E2M1[nib]
    vals = vals * np.repeat(np.exp2(scales.astype(np.float64) - 127.0), 8, axis=1)[..., None]
    return vals.transpose(0, 1, 3, 2).reshape(g * 512, n)


def sigmoid(v):
    return 1.0 / (1.0 + np.exp(-v))


def bf(x):
    return np.asarray(x, np.float32).astype(ml_dtypes.bfloat16)


def planes(Y):
    r, m = Y.shape
    b = f64(bf(Y)).reshape(r // 32, 32, m)
    amax = np.abs(b).max(1)
    byte = np.clip(np.where(amax > 0, np.frexp(amax)[1] - 1 + 127 - 7, 1), 1, 254)
    codes = (b * np.exp2(127.0 - byte)[:, None, :]).reshape(r, m).astype(np.float32).astype(ml_dtypes.float8_e4m3fn).view(np.uint8)
    words = codes.reshape(r // 512, 128, 4, m).transpose(0, 1, 3, 2)
    return np.ascontiguousarray(words), np.ascontiguousarray(byte.astype(np.uint8).reshape(r // 512, 16, m))


B, N, T, D, NQ = 1, 512, 2048, 1024, 512


def setup_inputs():
    n = np.random.standard_normal
    idx = np.random.permutation(T)[:B * N]
    s = mx_kscale(D)[:, None]
    kp = pack_weight(n((D, T)) / s, "e2m1")
    cp = pack_weight(n((D, T)) / s / 12, "e4m3")
    return {
        "qT": (n((B, D, NQ)) * s * (1.00 / np.sqrt(D))).astype(np.float32),
        "k_words": np.ascontiguousarray(kp[0].reshape(1, 2, 128, T, 2).transpose(0, 2, 3, 1, 4)).reshape(1, 128, T, 4),
        "k_scales": kp[1],
        "c_words": cp[0],
        "c_scales": cp[1],
        "th": (n((B, 1, NQ)) + 1).astype(np.float32),
        "offs": striped(idx),
    }


def reference(qT, k_words, k_scales, c_words, c_scales, th, offs):
    idx = unstriped(offs)
    pick = lambda x, which: x[:, which].reshape(x.shape[0], B, -1).transpose(1, 0, 2)
    k = unpack_weight(k_words.reshape(1, 128, T, 2, 2).transpose(0, 3, 1, 2, 4).reshape(2, 128, 2 * T), k_scales, "e2m1")
    kg = pick(k, idx)
    c = unpack_weight(c_words, c_scales, "e4m3")
    cg = pick(c, idx)
    qq = mxq(f64(qT), 1, "e4m3")
    a = (kg.transpose(0, 2, 1) @ qq) + (cg.transpose(0, 2, 1) @ qq)
    y = sigmoid(a - f64(th))
    Y = y[0]
    words, scales = planes(Y)
    return Y, words, scales

@@ -1,0 +1,194 @@
+from contextlib import ExitStack
+
+import concourse.mybir as mybir
+from concourse.masks import make_identity
+
+N, T, D, NQ = 512, 2048, 1024, 512
+FLOPS = 2 * 2 * N * D * NQ
+
+F32 = mybir.dt.float32
+BF16 = mybir.dt.bfloat16
+I32 = mybir.dt.int32
+U32 = mybir.dt.uint32
+U16 = mybir.dt.uint16
+U8 = mybir.dt.uint8
+FP8X4 = mybir.dt.float8_e4m3fn_x4
+FP4X4 = mybir.dt.float4_e2m1fn_x4
+SIGMOID = mybir.ActivationFunctionType.Sigmoid
+MULT = mybir.AluOpType.mult
+
+P = 128
+PACK = 4
+K_PASS = P * PACK
+PASSES = D // K_PASS
+BLOCKS = NQ // P
+C_PLANE = 4
+
+
+def weave(engine_copy, dst, src):
+    engine_copy(
+        dst.rearrange("p (c i) t -> p c t i", i=PACK),
+        src.rearrange("p t (c i) -> p c t i", i=PACK),
+    )
+
+
+def tile_attend_plw_residsig_topk_kernel(tc, qT, k_words, k_scales, c_words, c_scales, th, offs, out_0, out_1, out_2):
+    nc = tc.nc
+    with ExitStack() as ctx:
+        keep = ctx.enter_context(tc.tile_pool(name="keep", bufs=1))
+        psum = ctx.enter_context(tc.psum_pool(name="psum", bufs=1))
+
+        offsets = keep.tile([P, N // 16], U16, name="offsets")
+        kw_pool = keep.tile([P, T], I32, name="kw_pool")
+        nc.sync.dma_start(offsets[:], offs)
+        pieces = [(0, 0, 256), (1, 0, 256), (0, 256, 256), (1, 256, 128), (1, 384, 128)]
+        q_raw = [keep.tile([P, PACK, w], F32, name=f"q_raw{i}") for i, (o, q0, w) in enumerate(pieces)]
+
+        def load_q(i):
+            o, q0, w = pieces[i]
+            rows = qT[0, o * K_PASS : (o + 1) * K_PASS, q0 : q0 + w]
+            nc.sync.dma_start(q_raw[i][:], rows.rearrange("(p t) w -> p t w", t=PACK))
+
+        load_q(0)
+
+        ks_pool = keep.tile([P, PASSES * T], U8, name="ks_pool")
+        cs_pool = keep.tile([P, T], U8, name="cs_pool")
+        th_rows = keep.tile([P, P], F32, name="th_rows")
+        nc.vector.memset(ks_pool[:].bitcast(I32), 0)
+        nc.gpsimd.memset(cs_pool[:].bitcast(I32), 0)
+        warm = keep.tile([P, 1], F32, name="warm")
+        nc.vector.memset(warm[:], 0.0)
+        nc.vector.memset(th_rows[:], 0.0)
+
+        cw_pool = [keep.tile([P, T], I32, name=f"cw_pool{o}") for o in range(PASSES)]
+
+        def load_c(o):
+            nc.sync.dma_start(cw_pool[o][:], c_words[o].rearrange("p t b -> p (t b)").bitcast(I32))
+
+        for quad in range(4):
+            nc.sync.dma_start(
+                ks_pool[32 * quad : 32 * quad + 4, :].bitcast(I32).rearrange("r (o t) -> r o t", o=PASSES),
+                k_scales[:, 4 * quad : 4 * quad + 4, :].bitcast(I32).rearrange("o r t -> r o t"),
+            )
+        nc.sync.dma_start(kw_pool[:], k_words[0].rearrange("p t b -> p (t b)").bitcast(I32))
+        for quad in range(4):
+            nc.sync.dma_start(
+                cs_pool[32 * quad + C_PLANE : 32 * quad + C_PLANE + 4 * PASSES, :].bitcast(I32),
+                c_scales[:, 4 * quad : 4 * quad + 4, :].bitcast(I32),
+            )
+
+        ident = keep.tile([P, P], F32, name="ident")
+        make_identity(nc, ident[:])
+        nc.scalar.activation(warm[:], warm[:], SIGMOID)
+
+        load_c(0)
+        nc.sync.dma_start(th_rows[0:BLOCKS, :], th[0, 0].rearrange("(j p) -> j p", p=P))
+        load_q(1)
+        load_c(1)
+        load_q(2)
+        load_q(3)
+        load_q(4)
+
+        th_psum = psum.tile([P, PACK, P], F32, name="th_psum", tag="turned", bufs=3)
+        nc.tensor.transpose(th_psum[:, 0, :], th_rows[:], ident[:])
+        neg_th = keep.tile([P, BLOCKS], F32, name="neg_th")
+        nc.vector.tensor_scalar(neg_th[:], th_psum[:, 0, 0:BLOCKS], -1.0, None, MULT)
+
+        ks = [keep.tile([P, N], U8, name=f"ks{o}", align_bytes=64) for o in range(PASSES)]
+        cs = keep.tile([P, N], U8, name="cs", align_bytes=64)
+        kw_pair = keep.tile([P, N], U32, name="kw_pair", align_bytes=64)
+        kw = [keep.tile([P, 2 * N], U8, name=f"kw{o}", align_bytes=64) for o in range(PASSES)]
+        cw = [keep.tile([P, N], U32, name=f"cw{o}", align_bytes=64) for o in range(PASSES)]
+
+        q_bf = [keep.tile([P, w, PACK], BF16, name=f"q_bf{i}", align_bytes=64) for i, (o, q0, w) in enumerate(pieces)]
+        q_codes = [keep.tile([P, w], U32, name=f"q_codes{i}", align_bytes=64) for i, (o, q0, w) in enumerate(pieces)]
+        q_scales = [keep.tile([P, w], U8, name=f"q_scales{i}", align_bytes=64) for i, (o, q0, w) in enumerate(pieces)]
+
+        def cast_q(i, engine_copy):
+            weave(engine_copy, q_bf[i][:], q_raw[i][:])
+
+        def quant_q(i):
+            nc.vector.quantize_mx(q_codes[i][:].bitcast(FP8X4), q_scales[i][:], q_bf[i][:].rearrange("p c t -> p (c t)"))
+
+        def q_operand(o, j):
+            for i, (po, q0, w) in enumerate(pieces):
+                if po == o and q0 <= j * P < q0 + w:
+                    cols = slice(j * P - q0, (j + 1) * P - q0)
+                    return q_codes[i][:, cols].bitcast(FP8X4), q_scales[i][:, cols]
+
+        acc = [psum.tile([P, N], F32, name=f"acc{j}") for j in range(BLOCKS)]
+
+        def mm_k(j, o, start):
+            codes, scales = q_operand(o, j)
+            nc.tensor.matmul_mx(acc[j][:], codes, scales, kw[o][:].bitcast(FP4X4), ks[o][:], start=start, stop=False)
+
+        def mm_c(j, o, stop):
+            codes, scales = q_operand(o, j)
+            nc.tensor.matmul_mx(acc[j][:], codes, scales, cw[o][:].bitcast(FP8X4), cs[C_PLANE + 4 * o : P, :], start=False, stop=stop)
+
+        for o in range(PASSES):
+            nc.vector.tensor_copy(ks[o][:], ks_pool[:, o * T : (o + 1) * T].indirect(offsets[:]))
+        nc.vector.tensor_copy(kw_pair[:], kw_pool[:].bitcast(U32).indirect(offsets[:]))
+        for o in range(PASSES):
+            nc.vector.tensor_copy(kw[o][:].bitcast(U16), kw_pair[:].bitcast(U16)[:, o : 2 * N : 2])
+        cast_q(0, nc.scalar.copy)
+        quant_q(0)
+        for j in range(2):
+            mm_k(j, 0, True)
+        nc.vector.tensor_copy(cs[:], cs_pool[:].indirect(offsets[:]))
+        nc.vector.tensor_copy(cw[0][:], cw_pool[0][:].bitcast(U32).indirect(offsets[:]))
+        for j in range(2):
+            mm_c(j, 0, False)
+        cast_q(1, nc.scalar.copy)
+        quant_q(1)
+        for j in range(2):
+            mm_k(j, 1, False)
+        nc.vector.tensor_copy(cw[1][:], cw_pool[1][:].bitcast(U32).indirect(offsets[:]))
+        for j in range(2):
+            mm_c(j, 1, True)
+
+        y_scales = keep.tile([P, NQ], U8, name="y_scales", align_bytes=64)
+        words_out = out_1[0].rearrange("p q t -> p (q t)").bitcast(I32)
+
+        y_q = [keep.tile([P, PACK, P], F32, name=f"y_q{j}") for j in range(BLOCKS)]
+        y = [keep.tile([P, PACK, P], F32, name=f"y{j}") for j in range(BLOCKS)]
+        turned = {}
+
+        def sigmoid_and_turn(j):
+            nc.scalar.activation(y_q[j][:], acc[j][:].rearrange("q (p u) -> q u p", u=PACK), SIGMOID, bias=neg_th[:, j : j + 1])
+            turned[j] = psum.tile([P, PACK, P], F32, name=f"turned{j}", tag="turned", bufs=3)
+            for u in range(PACK):
+                nc.tensor.transpose(turned[j][:, u, :], y_q[j][:, u, :], ident[:])
+
+        def hand_out(j, engine_copy):
+            cols = slice(j * P, (j + 1) * P)
+            engine_copy(y[j][:], turned[j][:])
+            nc.sync.dma_start(out_0[:, cols].rearrange("(p u) q -> p u q", u=PACK), y[j][:])
+            y_bf = keep.tile([P, P, PACK], BF16, name=f"y_bf{j}", align_bytes=64)
+            weave(nc.vector.tensor_copy, y_bf[:], y[j][:])
+            y_words = keep.tile([P, P], I32, name=f"y_words{j}", align_bytes=64)
+            nc.vector.quantize_mx(y_words[:].bitcast(FP8X4), y_scales[:, cols], y_bf[:].rearrange("p q u -> p (q u)"))
+            nc.sync.dma_start(words_out[:, cols], y_words[:])
+
+        cast_q(2, nc.vector.tensor_copy)
+        quant_q(2)
+        for j in range(2, 4):
+            mm_k(j, 0, True)
+            mm_c(j, 0, False)
+        sigmoid_and_turn(0)
+        sigmoid_and_turn(1)
+        for j in range(2, 4):
+            cast_q(j + 1, nc.vector.tensor_copy)
+            quant_q(j + 1)
+            mm_k(j, 1, False)
+            mm_c(j, 1, True)
+        hand_out(0, nc.scalar.copy)
+        hand_out(1, nc.scalar.copy)
+        sigmoid_and_turn(2)
+        sigmoid_and_turn(3)
+        hand_out(2, nc.vector.tensor_copy)
+        hand_out(3, nc.scalar.copy)
+
+        for quad in range(4):
+            queue = nc.sync if quad % 2 == 0 else nc.scalar
+            queue.dma_start(out_2[0, 4 * quad : 4 * quad + 4, :].bitcast(I32), y_scales[32 * quad : 32 * quad + 4, :].bitcast(I32))

@@ -54,8 +54,8 @@ def tile_attend_plw_residsig_topk_kernel(tc, qT, k_words, k_scales, c_words, c_s
         ks_pool = keep.tile([P, PASSES * T], U8, name="ks_pool")
         cs_pool = keep.tile([P, T], U8, name="cs_pool")
         th_rows = keep.tile([P, P], F32, name="th_rows")
-        nc.vector.memset(ks_pool[:].bitcast(I32), 0)
-        nc.gpsimd.memset(cs_pool[:].bitcast(I32), 0)
+        nc.gpsimd.memset(ks_pool[:].bitcast(I32), 0)
+        nc.vector.memset(cs_pool[:].bitcast(I32), 0)
         warm = keep.tile([P, 1], F32, name="warm")
         nc.vector.memset(warm[:], 0.0)
         nc.vector.memset(th_rows[:], 0.0)
@@ -81,15 +81,15 @@ def tile_attend_plw_residsig_topk_kernel(tc, qT, k_words, k_scales, c_words, c_s
         make_identity(nc, ident[:])
         nc.scalar.activation(warm[:], warm[:], SIGMOID)
 
+        load_q(2)
         load_c(0)
         nc.sync.dma_start(th_rows[0:BLOCKS, :], th[0, 0].rearrange("(j p) -> j p", p=P))
         load_q(1)
         load_c(1)
-        load_q(2)
         load_q(3)
         load_q(4)
 
-        th_psum = psum.tile([P, PACK, P], F32, name="th_psum", tag="turned", bufs=3)
+        th_psum = psum.tile([P, PACK, P], F32, name="th_psum", tag="turned", bufs=4)
         nc.tensor.transpose(th_psum[:, 0, :], th_rows[:], ident[:])
         neg_th = keep.tile([P, BLOCKS], F32, name="neg_th")
         nc.vector.tensor_scalar(neg_th[:], th_psum[:, 0, 0:BLOCKS], -1.0, None, MULT)
@@ -97,7 +97,7 @@ def tile_attend_plw_residsig_topk_kernel(tc, qT, k_words, k_scales, c_words, c_s
         ks = [keep.tile([P, N], U8, name=f"ks{o}", align_bytes=64) for o in range(PASSES)]
         cs = keep.tile([P, N], U8, name="cs", align_bytes=64)
         kw_pair = keep.tile([P, N], U32, name="kw_pair", align_bytes=64)
-        kw = [keep.tile([P, 2 * N], U8, name=f"kw{o}", align_bytes=64) for o in range(PASSES)]
+        kw = keep.tile([P, PASSES * N], U16, name="kw", align_bytes=64)
         cw = [keep.tile([P, N], U32, name=f"cw{o}", align_bytes=64) for o in range(PASSES)]
 
         q_bf = [keep.tile([P, w, PACK], BF16, name=f"q_bf{i}", align_bytes=64) for i, (o, q0, w) in enumerate(pieces)]
@@ -120,7 +120,7 @@ def tile_attend_plw_residsig_topk_kernel(tc, qT, k_words, k_scales, c_words, c_s
 
         def mm_k(j, o, start):
             codes, scales = q_operand(o, j)
-            nc.tensor.matmul_mx(acc[j][:], codes, scales, kw[o][:].bitcast(FP4X4), ks[o][:], start=start, stop=False)
+            nc.tensor.matmul_mx(acc[j][:], codes, scales, kw[:, o * N : (o + 1) * N].bitcast(FP4X4), ks[o][:], start=start, stop=False)
 
         def mm_c(j, o, stop):
             codes, scales = q_operand(o, j)
@@ -129,22 +129,34 @@ def tile_attend_plw_residsig_topk_kernel(tc, qT, k_words, k_scales, c_words, c_s
         for o in range(PASSES):
             nc.vector.tensor_copy(ks[o][:], ks_pool[:, o * T : (o + 1) * T].indirect(offsets[:]))
         nc.vector.tensor_copy(kw_pair[:], kw_pool[:].bitcast(U32).indirect(offsets[:]))
-        for o in range(PASSES):
-            nc.vector.tensor_copy(kw[o][:].bitcast(U16), kw_pair[:].bitcast(U16)[:, o : 2 * N : 2])
+        nc.vector.tensor_copy(
+            kw[:].rearrange("p (o s) -> p o s", o=PASSES),
+            kw_pair[:].bitcast(U16).rearrange("p (s o) -> p o s", o=PASSES),
+        )
         cast_q(0, nc.scalar.copy)
         quant_q(0)
         for j in range(2):
             mm_k(j, 0, True)
         nc.vector.tensor_copy(cs[:], cs_pool[:].indirect(offsets[:]))
+        cast_q(2, nc.scalar.copy)
+        quant_q(2)
+        for j in range(2, 4):
+            mm_k(j, 0, True)
         nc.vector.tensor_copy(cw[0][:], cw_pool[0][:].bitcast(U32).indirect(offsets[:]))
-        for j in range(2):
+        for j in range(2, 4):
             mm_c(j, 0, False)
         cast_q(1, nc.scalar.copy)
         quant_q(1)
         for j in range(2):
             mm_k(j, 1, False)
+            mm_c(j, 0, False)
         nc.vector.tensor_copy(cw[1][:], cw_pool[1][:].bitcast(U32).indirect(offsets[:]))
         for j in range(2):
+            mm_c(j, 1, True)
+        for j in range(2, 4):
+            cast_q(j + 1, nc.scalar.copy if j == 2 else nc.vector.tensor_copy)
+            quant_q(j + 1)
+            mm_k(j, 1, False)
             mm_c(j, 1, True)
 
         y_scales = keep.tile([P, NQ], U8, name="y_scales", align_bytes=64)
@@ -156,7 +168,7 @@ def tile_attend_plw_residsig_topk_kernel(tc, qT, k_words, k_scales, c_words, c_s
 
         def sigmoid_and_turn(j):
             nc.scalar.activation(y_q[j][:], acc[j][:].rearrange("q (p u) -> q u p", u=PACK), SIGMOID, bias=neg_th[:, j : j + 1])
-            turned[j] = psum.tile([P, PACK, P], F32, name=f"turned{j}", tag="turned", bufs=3)
+            turned[j] = psum.tile([P, PACK, P], F32, name=f"turned{j}", tag="turned", bufs=4)
             for u in range(PACK):
                 nc.tensor.transpose(turned[j][:, u, :], y_q[j][:, u, :], ident[:])
 
@@ -170,24 +182,10 @@ def tile_attend_plw_residsig_topk_kernel(tc, qT, k_words, k_scales, c_words, c_s
             nc.vector.quantize_mx(y_words[:].bitcast(FP8X4), y_scales[:, cols], y_bf[:].rearrange("p q u -> p (q u)"))
             nc.sync.dma_start(words_out[:, cols], y_words[:])
 
-        cast_q(2, nc.vector.tensor_copy)
-        quant_q(2)
-        for j in range(2, 4):
-            mm_k(j, 0, True)
-            mm_c(j, 0, False)
-        sigmoid_and_turn(0)
-        sigmoid_and_turn(1)
-        for j in range(2, 4):
-            cast_q(j + 1, nc.vector.tensor_copy)
-            quant_q(j + 1)
-            mm_k(j, 1, False)
-            mm_c(j, 1, True)
-        hand_out(0, nc.scalar.copy)
-        hand_out(1, nc.scalar.copy)
-        sigmoid_and_turn(2)
-        sigmoid_and_turn(3)
-        hand_out(2, nc.vector.tensor_copy)
-        hand_out(3, nc.scalar.copy)
+        for j in range(BLOCKS):
+            sigmoid_and_turn(j)
+        for j in range(BLOCKS):
+            hand_out(j, nc.vector.tensor_copy if j < 2 else nc.scalar.copy)
 
         for quad in range(4):
             queue = nc.sync if quad % 2 == 0 else nc.scalar

@@ -15,7 +15,7 @@ U8 = mybir.dt.uint8
 FP8X4 = mybir.dt.float8_e4m3fn_x4
 FP4X4 = mybir.dt.float4_e2m1fn_x4
 SIGMOID = mybir.ActivationFunctionType.Sigmoid
-MULT = mybir.AluOpType.mult
+COPY = mybir.ActivationFunctionType.Copy
 
 P = 128
 PACK = 4
@@ -27,8 +27,8 @@ C_PLANE = 4
 
 def weave(engine_copy, dst, src):
     engine_copy(
-        dst.rearrange("p (c i) t -> p c t i", i=PACK),
-        src.rearrange("p t (c i) -> p c t i", i=PACK),
+        dst.rearrange("p (c i) t -> p c t i", i=2),
+        src.rearrange("p t (c i) -> p c t i", i=2),
     )
 
 
@@ -38,38 +38,41 @@ def tile_attend_plw_residsig_topk_kernel(tc, qT, k_words, k_scales, c_words, c_s
         keep = ctx.enter_context(tc.tile_pool(name="keep", bufs=1))
         psum = ctx.enter_context(tc.psum_pool(name="psum", bufs=1))
 
-        offsets = keep.tile([P, N // 16], U16, name="offsets")
-        kw_pool = keep.tile([P, T], I32, name="kw_pool")
-        nc.sync.dma_start(offsets[:], offs)
         pieces = [(0, 0, 256), (1, 0, 256), (0, 256, 256), (1, 256, 128), (1, 384, 128)]
-        q_raw = [keep.tile([P, PACK, w], F32, name=f"q_raw{i}") for i, (o, q0, w) in enumerate(pieces)]
+        q_raw = {}
 
-        def load_q(i):
+        def load_q(i, dst):
             o, q0, w = pieces[i]
+            q_raw[i] = dst
             rows = qT[0, o * K_PASS : (o + 1) * K_PASS, q0 : q0 + w]
-            nc.sync.dma_start(q_raw[i][:], rows.rearrange("(p t) w -> p t w", t=PACK))
+            nc.sync.dma_start(dst, rows.rearrange("(p t) w -> p t w", t=PACK))
 
-        load_q(0)
-
-        ks_pool = keep.tile([P, PASSES * T], U8, name="ks_pool")
-        cs_pool = keep.tile([P, T], U8, name="cs_pool")
+        load_q(0, keep.tile([P, PACK, 256], F32, name="q_raw0")[:])
         th_rows = keep.tile([P, P], F32, name="th_rows")
-        nc.gpsimd.memset(ks_pool[:].bitcast(I32), 0)
-        nc.vector.memset(cs_pool[:].bitcast(I32), 0)
+        nc.gpsimd.memset(th_rows[:], 0.0)
+        nc.sync.dma_start(th_rows[0:BLOCKS, :], th[0, 0].rearrange("(j p) -> j p", p=P))
+        offsets = keep.tile([P, N // 16], U16, name="offsets")
+        nc.sync.dma_start(offsets[:], offs)
+
+        ks_pool = [keep.tile([P, T], U8, name=f"ks_pool{o}", align_bytes=64) for o in range(PASSES)]
+        cs_pool = keep.tile([P, T], U8, name="cs_pool", align_bytes=64)
+        ks = keep.tile([P, PASSES * N], U8, name="ks", align_bytes=64)
+        nc.gpsimd.memset(ks_pool[0][:].bitcast(I32), 0)
+        nc.vector.memset(ks_pool[1][:].bitcast(I32), 0)
+        nc.gpsimd.memset(cs_pool[:].bitcast(I32), 0)
+        nc.vector.memset(ks[:].bitcast(I32), 0)
         warm = keep.tile([P, 1], F32, name="warm")
         nc.vector.memset(warm[:], 0.0)
-        nc.vector.memset(th_rows[:], 0.0)
 
-        cw_pool = [keep.tile([P, T], I32, name=f"cw_pool{o}") for o in range(PASSES)]
+        cw_pool = {}
 
-        def load_c(o):
+        def load_c(o, tag):
+            cw_pool[o] = keep.tile([P, T], I32, name=f"cw_pool{o}", tag=tag, align_bytes=64)
             nc.sync.dma_start(cw_pool[o][:], c_words[o].rearrange("p t b -> p (t b)").bitcast(I32))
 
-        for quad in range(4):
-            nc.sync.dma_start(
-                ks_pool[32 * quad : 32 * quad + 4, :].bitcast(I32).rearrange("r (o t) -> r o t", o=PASSES),
-                k_scales[:, 4 * quad : 4 * quad + 4, :].bitcast(I32).rearrange("o r t -> r o t"),
-            )
+        for o in range(PASSES):
+            nc.sync.dma_start(ks_pool[o][0:P:8, :].bitcast(I32), k_scales[o].bitcast(I32))
+        kw_pool = keep.tile([P, T], I32, name="kw_pool", align_bytes=64)
         nc.sync.dma_start(kw_pool[:], k_words[0].rearrange("p t b -> p (t b)").bitcast(I32))
         for quad in range(4):
             nc.sync.dma_start(
@@ -81,33 +84,29 @@ def tile_attend_plw_residsig_topk_kernel(tc, qT, k_words, k_scales, c_words, c_s
         make_identity(nc, ident[:])
         nc.scalar.activation(warm[:], warm[:], SIGMOID)
 
-        load_q(2)
-        load_c(0)
-        nc.sync.dma_start(th_rows[0:BLOCKS, :], th[0, 0].rearrange("(j p) -> j p", p=P))
-        load_q(1)
-        load_c(1)
-        load_q(3)
-        load_q(4)
+        load_q(2, keep.tile([P, PACK, 256], F32, name="q_raw2", align_bytes=64)[:])
+        load_c(0, "cw_pool0")
 
         th_psum = psum.tile([P, PACK, P], F32, name="th_psum", tag="turned", bufs=4)
         nc.tensor.transpose(th_psum[:, 0, :], th_rows[:], ident[:])
         neg_th = keep.tile([P, BLOCKS], F32, name="neg_th")
-        nc.vector.tensor_scalar(neg_th[:], th_psum[:, 0, 0:BLOCKS], -1.0, None, MULT)
+        nc.scalar.activation(neg_th[:], th_psum[:, 0, 0:BLOCKS], COPY, scale=-1.0)
 
-        ks = [keep.tile([P, N], U8, name=f"ks{o}", align_bytes=64) for o in range(PASSES)]
-        cs = keep.tile([P, N], U8, name="cs", align_bytes=64)
         kw_pair = keep.tile([P, N], U32, name="kw_pair", align_bytes=64)
         kw = keep.tile([P, PASSES * N], U16, name="kw", align_bytes=64)
-        cw = [keep.tile([P, N], U32, name=f"cw{o}", align_bytes=64) for o in range(PASSES)]
-
-        q_bf = [keep.tile([P, w, PACK], BF16, name=f"q_bf{i}", align_bytes=64) for i, (o, q0, w) in enumerate(pieces)]
-        q_codes = [keep.tile([P, w], U32, name=f"q_codes{i}", align_bytes=64) for i, (o, q0, w) in enumerate(pieces)]
+        cw, q_bf, q_codes = {}, {}, {}
         q_scales = [keep.tile([P, w], U8, name=f"q_scales{i}", align_bytes=64) for i, (o, q0, w) in enumerate(pieces)]
 
-        def cast_q(i, engine_copy):
-            weave(engine_copy, q_bf[i][:], q_raw[i][:])
+        def gather_c(o, tag):
+            cw[o] = keep.tile([P, N], U32, name=f"cw{o}", tag=tag, align_bytes=64)
+            nc.vector.tensor_copy(cw[o][:], cw_pool[o][:].bitcast(U32).indirect(offsets[:]))
 
-        def quant_q(i):
+        def cast_q(i, engine_copy, tag):
+            q_bf[i] = keep.tile([P, pieces[i][2], PACK], BF16, name=f"q_bf{i}", tag=tag, align_bytes=64)
+            weave(engine_copy, q_bf[i][:], q_raw[i])
+
+        def quant_q(i, tag):
+            q_codes[i] = keep.tile([P, pieces[i][2]], U32, name=f"q_codes{i}", tag=tag, align_bytes=64)
             nc.vector.quantize_mx(q_codes[i][:].bitcast(FP8X4), q_scales[i][:], q_bf[i][:].rearrange("p c t -> p (c t)"))
 
         def q_operand(o, j):
@@ -120,42 +119,52 @@ def tile_attend_plw_residsig_topk_kernel(tc, qT, k_words, k_scales, c_words, c_s
 
         def mm_k(j, o, start):
             codes, scales = q_operand(o, j)
-            nc.tensor.matmul_mx(acc[j][:], codes, scales, kw[:, o * N : (o + 1) * N].bitcast(FP4X4), ks[o][:], start=start, stop=False)
+            nc.tensor.matmul_mx(acc[j][:], codes, scales, kw[:, o * N : (o + 1) * N].bitcast(FP4X4), ks[:, o * N : (o + 1) * N], start=start, stop=False)
 
         def mm_c(j, o, stop):
             codes, scales = q_operand(o, j)
             nc.tensor.matmul_mx(acc[j][:], codes, scales, cw[o][:].bitcast(FP8X4), cs[C_PLANE + 4 * o : P, :], start=False, stop=stop)
 
+        ks_rows = keep.tile([P, PASSES * N], U8, name="ks_rows", align_bytes=64)
         for o in range(PASSES):
-            nc.vector.tensor_copy(ks[o][:], ks_pool[:, o * T : (o + 1) * T].indirect(offsets[:]))
+            nc.vector.tensor_copy(ks_rows[:, o * N : (o + 1) * N], ks_pool[o][:].indirect(offsets[:]))
+        for r in range(4):
+            nc.sync.dma_start(ks[r:P:32, :].bitcast(I32), ks_rows[8 * r : P : 32, :].bitcast(I32))
+        load_q(1, keep.tile([P, PACK, 256], F32, name="q_raw1", tag="ks_pool1", align_bytes=64)[:])
         nc.vector.tensor_copy(kw_pair[:], kw_pool[:].bitcast(U32).indirect(offsets[:]))
+        load_c(1, "kw_pool")
         nc.vector.tensor_copy(
             kw[:].rearrange("p (o s) -> p o s", o=PASSES),
             kw_pair[:].bitcast(U16).rearrange("p (s o) -> p o s", o=PASSES),
         )
-        cast_q(0, nc.scalar.copy)
-        quant_q(0)
+        cast_q(0, nc.scalar.copy, "q_bf0")
+        quant_q(0, "ks_pool0")
         for j in range(2):
             mm_k(j, 0, True)
+        cs = keep.tile([P, N], U8, name="cs", tag="kw_pair", align_bytes=64)
         nc.vector.tensor_copy(cs[:], cs_pool[:].indirect(offsets[:]))
-        cast_q(2, nc.scalar.copy)
-        quant_q(2)
+        q_last = keep.tile([P, 2, PACK, P], F32, name="q_last", tag="cs_pool", align_bytes=64)
+        load_q(3, q_last[:, 0])
+        load_q(4, q_last[:, 1])
+        gather_c(0, "cw0")
+        cast_q(2, nc.scalar.copy, "q_bf2")
+        quant_q(2, "cw_pool0")
         for j in range(2, 4):
             mm_k(j, 0, True)
-        nc.vector.tensor_copy(cw[0][:], cw_pool[0][:].bitcast(U32).indirect(offsets[:]))
-        for j in range(2, 4):
             mm_c(j, 0, False)
-        cast_q(1, nc.scalar.copy)
-        quant_q(1)
+        cast_q(1, nc.scalar.copy, "q_raw2")
+        quant_q(1, "q_bf2")
         for j in range(2):
             mm_k(j, 1, False)
             mm_c(j, 0, False)
-        nc.vector.tensor_copy(cw[1][:], cw_pool[1][:].bitcast(U32).indirect(offsets[:]))
+        gather_c(1, "q_raw2")
         for j in range(2):
             mm_c(j, 1, True)
+        cast_q(3, nc.scalar.copy, "ks_pool1")
+        cast_q(4, nc.vector.tensor_copy, "kw_pool")
+        quant_q(3, "cs_pool")
+        quant_q(4, "q_codes4")
         for j in range(2, 4):
-            cast_q(j + 1, nc.scalar.copy if j == 2 else nc.vector.tensor_copy)
-            quant_q(j + 1)
             mm_k(j, 1, False)
             mm_c(j, 1, True)
 
@@ -164,10 +173,16 @@ def tile_attend_plw_residsig_topk_kernel(tc, qT, k_words, k_scales, c_words, c_s
 
         y_q = [keep.tile([P, PACK, P], F32, name=f"y_q{j}") for j in range(BLOCKS)]
         y = [keep.tile([P, PACK, P], F32, name=f"y{j}") for j in range(BLOCKS)]
+        y_words = [keep.tile([P, 2 * P], I32, name=f"y_words{h}", align_bytes=64) for h in range(BLOCKS // 2)]
         turned = {}
 
         def sigmoid_and_turn(j):
-            nc.scalar.activation(y_q[j][:], acc[j][:].rearrange("q (p u) -> q u p", u=PACK), SIGMOID, bias=neg_th[:, j : j + 1])
+            nc.scalar.activation(
+                y_q[j][:].rearrange("q (h e) p -> q h p e", e=2),
+                acc[j][:].rearrange("q (p h e) -> q h p e", h=2, e=2),
+                SIGMOID,
+                bias=neg_th[:, j : j + 1],
+            )
             turned[j] = psum.tile([P, PACK, P], F32, name=f"turned{j}", tag="turned", bufs=4)
             for u in range(PACK):
                 nc.tensor.transpose(turned[j][:, u, :], y_q[j][:, u, :], ident[:])
@@ -178,14 +193,17 @@ def tile_attend_plw_residsig_topk_kernel(tc, qT, k_words, k_scales, c_words, c_s
             nc.sync.dma_start(out_0[:, cols].rearrange("(p u) q -> p u q", u=PACK), y[j][:])
             y_bf = keep.tile([P, P, PACK], BF16, name=f"y_bf{j}", align_bytes=64)
             weave(nc.vector.tensor_copy, y_bf[:], y[j][:])
-            y_words = keep.tile([P, P], I32, name=f"y_words{j}", align_bytes=64)
-            nc.vector.quantize_mx(y_words[:].bitcast(FP8X4), y_scales[:, cols], y_bf[:].rearrange("p q u -> p (q u)"))
-            nc.sync.dma_start(words_out[:, cols], y_words[:])
+            half = y_words[j // 2]
+            nc.vector.quantize_mx(
+                half[:, (j % 2) * P : (j % 2 + 1) * P].bitcast(FP8X4), y_scales[:, cols], y_bf[:].rearrange("p q u -> p (q u)")
+            )
+            if j % 2 == 1:
+                nc.sync.dma_start(words_out[:, (j - 1) * P : (j + 1) * P], half[:])
 
         for j in range(BLOCKS):
             sigmoid_and_turn(j)
         for j in range(BLOCKS):
-            hand_out(j, nc.vector.tensor_copy if j < 2 else nc.scalar.copy)
+            hand_out(j, nc.vector.tensor_copy if j == 0 else nc.scalar.copy)
 
         for quad in range(4):
             queue = nc.sync if quad % 2 == 0 else nc.scalar

@@ -22,10 +22,17 @@ PACK = 4
 K_PASS = P * PACK
 PASSES = D // K_PASS
 BLOCKS = NQ // P
-C_PLANE = 4
+QUAD = 32
+QUAD_ROWS = 4
+SPREAD = P // (QUAD_ROWS * P // QUAD)
+C_FIRST = QUAD_ROWS
+ALIGN = 64
+
+EARLY_0, LATE_0, EARLY_1, BLOCK2_1, BLOCK3_1 = (0, 0, 2 * P), (0, 2 * P, 2 * P), (1, 0, 2 * P), (1, 2 * P, P), (1, 3 * P, P)
+EARLY, LATE = (0, 1), (2, 3)
 
 
-def weave(engine_copy, dst, src):
+def interleave(engine_copy, dst, src):
     engine_copy(
         dst.rearrange("p (c i) t -> p c t i", i=2),
         src.rearrange("p t (c i) -> p c t i", i=2),
@@ -35,176 +42,187 @@ def weave(engine_copy, dst, src):
 def tile_attend_plw_residsig_topk_kernel(tc, qT, k_words, k_scales, c_words, c_scales, th, offs, out_0, out_1, out_2):
     nc = tc.nc
     with ExitStack() as ctx:
-        keep = ctx.enter_context(tc.tile_pool(name="keep", bufs=1))
+        sbuf = ctx.enter_context(tc.tile_pool(name="sbuf", bufs=1))
         psum = ctx.enter_context(tc.psum_pool(name="psum", bufs=1))
 
-        pieces = [(0, 0, 256), (1, 0, 256), (0, 256, 256), (1, 256, 128), (1, 384, 128)]
-        q_raw = {}
+        q_raw, q_bf, q_codes, q_scales = {}, {}, {}, {}
+        cw_pool, cw = {}, {}
 
-        def load_q(i, dst):
-            o, q0, w = pieces[i]
-            q_raw[i] = dst
-            rows = qT[0, o * K_PASS : (o + 1) * K_PASS, q0 : q0 + w]
+        def load_q(piece, dst):
+            o, first, width = piece
+            q_raw[piece] = dst
+            rows = qT[0, o * K_PASS : (o + 1) * K_PASS, first : first + width]
             nc.sync.dma_start(dst, rows.rearrange("(p t) w -> p t w", t=PACK))
 
-        load_q(0, keep.tile([P, PACK, 256], F32, name="q_raw0")[:])
-        th_rows = keep.tile([P, P], F32, name="th_rows")
+        def load_c(o, buffer):
+            cw_pool[o] = sbuf.tile([P, T], I32, name=f"cw_pool{o}", tag=buffer, align_bytes=ALIGN)
+            nc.sync.dma_start(cw_pool[o][:], c_words[o].rearrange("p t b -> p (t b)").bitcast(I32))
+
+        load_q(EARLY_0, sbuf.tile([P, PACK, 2 * P], F32, name="q_early0")[:])
+        th_rows = sbuf.tile([P, P], F32, name="th_rows")
         nc.gpsimd.memset(th_rows[:], 0.0)
         nc.sync.dma_start(th_rows[0:BLOCKS, :], th[0, 0].rearrange("(j p) -> j p", p=P))
-        offsets = keep.tile([P, N // 16], U16, name="offsets")
+        offsets = sbuf.tile([P, N // 16], U16, name="offsets")
         nc.sync.dma_start(offsets[:], offs)
 
-        ks_pool = [keep.tile([P, T], U8, name=f"ks_pool{o}", align_bytes=64) for o in range(PASSES)]
-        cs_pool = keep.tile([P, T], U8, name="cs_pool", align_bytes=64)
-        ks = keep.tile([P, PASSES * N], U8, name="ks", align_bytes=64)
+        ks_pool = [sbuf.tile([P, T], U8, name=f"ks_pool{o}", align_bytes=ALIGN) for o in range(PASSES)]
+        cs_pool = sbuf.tile([P, T], U8, name="cs_pool", align_bytes=ALIGN)
+        ks = sbuf.tile([P, PASSES * N], U8, name="ks", align_bytes=ALIGN)
         nc.gpsimd.memset(ks_pool[0][:].bitcast(I32), 0)
         nc.vector.memset(ks_pool[1][:].bitcast(I32), 0)
         nc.gpsimd.memset(cs_pool[:].bitcast(I32), 0)
         nc.vector.memset(ks[:].bitcast(I32), 0)
-        warm = keep.tile([P, 1], F32, name="warm")
-        nc.vector.memset(warm[:], 0.0)
-
-        cw_pool = {}
-
-        def load_c(o, tag):
-            cw_pool[o] = keep.tile([P, T], I32, name=f"cw_pool{o}", tag=tag, align_bytes=64)
-            nc.sync.dma_start(cw_pool[o][:], c_words[o].rearrange("p t b -> p (t b)").bitcast(I32))
 
         for o in range(PASSES):
-            nc.sync.dma_start(ks_pool[o][0:P:8, :].bitcast(I32), k_scales[o].bitcast(I32))
-        kw_pool = keep.tile([P, T], I32, name="kw_pool", align_bytes=64)
+            nc.sync.dma_start(ks_pool[o][0:P:SPREAD, :].bitcast(I32), k_scales[o].bitcast(I32))
+        kw_pool = sbuf.tile([P, T], I32, name="kw_pool", align_bytes=ALIGN)
         nc.sync.dma_start(kw_pool[:], k_words[0].rearrange("p t b -> p (t b)").bitcast(I32))
-        for quad in range(4):
+        for quad in range(P // QUAD):
+            first = QUAD * quad + C_FIRST
             nc.sync.dma_start(
-                cs_pool[32 * quad + C_PLANE : 32 * quad + C_PLANE + 4 * PASSES, :].bitcast(I32),
-                c_scales[:, 4 * quad : 4 * quad + 4, :].bitcast(I32),
+                cs_pool[first : first + QUAD_ROWS * PASSES, :].bitcast(I32),
+                c_scales[:, QUAD_ROWS * quad : QUAD_ROWS * (quad + 1), :].bitcast(I32),
             )
 
-        ident = keep.tile([P, P], F32, name="ident")
+        ident = sbuf.tile([P, P], F32, name="ident")
         make_identity(nc, ident[:])
-        nc.scalar.activation(warm[:], warm[:], SIGMOID)
 
-        load_q(2, keep.tile([P, PACK, 256], F32, name="q_raw2", align_bytes=64)[:])
+        load_q(LATE_0, sbuf.tile([P, PACK, 2 * P], F32, name="q_late0", align_bytes=ALIGN)[:])
         load_c(0, "cw_pool0")
 
-        th_psum = psum.tile([P, PACK, P], F32, name="th_psum", tag="turned", bufs=4)
-        nc.tensor.transpose(th_psum[:, 0, :], th_rows[:], ident[:])
-        neg_th = keep.tile([P, BLOCKS], F32, name="neg_th")
-        nc.scalar.activation(neg_th[:], th_psum[:, 0, 0:BLOCKS], COPY, scale=-1.0)
+        def turn_bank(name):
+            return psum.tile([P, PACK, P], F32, name=name, tag="turned", bufs=BLOCKS)
 
-        kw_pair = keep.tile([P, N], U32, name="kw_pair", align_bytes=64)
-        kw = keep.tile([P, PASSES * N], U16, name="kw", align_bytes=64)
-        cw, q_bf, q_codes = {}, {}, {}
-        q_scales = [keep.tile([P, w], U8, name=f"q_scales{i}", align_bytes=64) for i, (o, q0, w) in enumerate(pieces)]
+        th_turned = turn_bank("th_turned")
+        nc.tensor.transpose(th_turned[:, 0, :], th_rows[:], ident[:])
+        neg_th = sbuf.tile([P, BLOCKS], F32, name="neg_th")
+        nc.scalar.activation(neg_th[:], th_turned[:, 0, 0:BLOCKS], COPY, scale=-1.0)
 
-        def gather_c(o, tag):
-            cw[o] = keep.tile([P, N], U32, name=f"cw{o}", tag=tag, align_bytes=64)
+        kw_pair = sbuf.tile([P, N], U32, name="kw_pair", align_bytes=ALIGN)
+        kw = sbuf.tile([P, PASSES * N], U16, name="kw", align_bytes=ALIGN)
+        sums = [psum.tile([P, N], F32, name=f"sum{j}") for j in range(BLOCKS)]
+
+        def gather_c(o, buffer):
+            cw[o] = sbuf.tile([P, N], U32, name=f"cw{o}", tag=buffer, align_bytes=ALIGN)
             nc.vector.tensor_copy(cw[o][:], cw_pool[o][:].bitcast(U32).indirect(offsets[:]))
 
-        def cast_q(i, engine_copy, tag):
-            q_bf[i] = keep.tile([P, pieces[i][2], PACK], BF16, name=f"q_bf{i}", tag=tag, align_bytes=64)
-            weave(engine_copy, q_bf[i][:], q_raw[i])
+        def bf_tile(name, width, buffer):
+            return sbuf.tile([P, width, PACK], BF16, name=name, tag=buffer, align_bytes=ALIGN)
 
-        def quant_q(i, tag):
-            q_codes[i] = keep.tile([P, pieces[i][2]], U32, name=f"q_codes{i}", tag=tag, align_bytes=64)
-            nc.vector.quantize_mx(q_codes[i][:].bitcast(FP8X4), q_scales[i][:], q_bf[i][:].rearrange("p c t -> p (c t)"))
+        def round_q(piece, engine_copy, dst):
+            q_bf[piece] = dst
+            interleave(engine_copy, dst, q_raw[piece])
 
-        def q_operand(o, j):
-            for i, (po, q0, w) in enumerate(pieces):
-                if po == o and q0 <= j * P < q0 + w:
-                    cols = slice(j * P - q0, (j + 1) * P - q0)
-                    return q_codes[i][:, cols].bitcast(FP8X4), q_scales[i][:, cols]
+        def quantise_q(piece, buffer):
+            o, first, width = piece
+            q_codes[piece] = sbuf.tile([P, width], U32, name=f"q_codes{o}_{first}", tag=buffer, align_bytes=ALIGN)
+            q_scales[piece] = sbuf.tile([P, width], U8, name=f"q_scales{o}_{first}", align_bytes=ALIGN)
+            nc.vector.quantize_mx(
+                q_codes[piece][:].bitcast(FP8X4), q_scales[piece][:], q_bf[piece].rearrange("p c t -> p (c t)")
+            )
 
-        acc = [psum.tile([P, N], F32, name=f"acc{j}") for j in range(BLOCKS)]
+        def product(j, piece, keys, key_scales, start, stop):
+            cols = slice(j * P - piece[1], (j + 1) * P - piece[1])
+            nc.tensor.matmul_mx(
+                sums[j][:], q_codes[piece][:, cols].bitcast(FP8X4), q_scales[piece][:, cols], keys, key_scales, start=start, stop=stop
+            )
 
-        def mm_k(j, o, start):
-            codes, scales = q_operand(o, j)
-            nc.tensor.matmul_mx(acc[j][:], codes, scales, kw[:, o * N : (o + 1) * N].bitcast(FP4X4), ks[:, o * N : (o + 1) * N], start=start, stop=False)
+        def coarse(j, piece):
+            o = piece[0]
+            cols = slice(o * N, (o + 1) * N)
+            product(j, piece, kw[:, cols].bitcast(FP4X4), ks[:, cols], o == 0, False)
 
-        def mm_c(j, o, stop):
-            codes, scales = q_operand(o, j)
-            nc.tensor.matmul_mx(acc[j][:], codes, scales, cw[o][:].bitcast(FP8X4), cs[C_PLANE + 4 * o : P, :], start=False, stop=stop)
+        def fine(j, piece):
+            o = piece[0]
+            product(j, piece, cw[o][:].bitcast(FP8X4), cs[C_FIRST + QUAD_ROWS * o : P, :], False, o == PASSES - 1)
 
-        ks_rows = keep.tile([P, PASSES * N], U8, name="ks_rows", align_bytes=64)
+        ks_rows = sbuf.tile([P, PASSES * N], U8, name="ks_rows", align_bytes=ALIGN)
         for o in range(PASSES):
             nc.vector.tensor_copy(ks_rows[:, o * N : (o + 1) * N], ks_pool[o][:].indirect(offsets[:]))
-        for r in range(4):
-            nc.sync.dma_start(ks[r:P:32, :].bitcast(I32), ks_rows[8 * r : P : 32, :].bitcast(I32))
-        load_q(1, keep.tile([P, PACK, 256], F32, name="q_raw1", tag="ks_pool1", align_bytes=64)[:])
+        for r in range(QUAD_ROWS):
+            nc.sync.dma_start(ks[r:P:QUAD, :].bitcast(I32), ks_rows[SPREAD * r : P : QUAD, :].bitcast(I32))
+        load_q(EARLY_1, sbuf.tile([P, PACK, 2 * P], F32, name="q_early1", tag="ks_pool1", align_bytes=ALIGN)[:])
+
         nc.vector.tensor_copy(kw_pair[:], kw_pool[:].bitcast(U32).indirect(offsets[:]))
         load_c(1, "kw_pool")
         nc.vector.tensor_copy(
             kw[:].rearrange("p (o s) -> p o s", o=PASSES),
             kw_pair[:].bitcast(U16).rearrange("p (s o) -> p o s", o=PASSES),
         )
-        cast_q(0, nc.scalar.copy, "q_bf0")
-        quant_q(0, "ks_pool0")
-        for j in range(2):
-            mm_k(j, 0, True)
-        cs = keep.tile([P, N], U8, name="cs", tag="kw_pair", align_bytes=64)
+        round_q(EARLY_0, nc.scalar.copy, bf_tile("q_bf_early0", 2 * P, "q_bf_early0")[:])
+        quantise_q(EARLY_0, "ks_pool0")
+        for j in EARLY:
+            coarse(j, EARLY_0)
+        round_q(LATE_0, nc.scalar.copy, bf_tile("q_bf_late0", 2 * P, "q_bf_late0")[:])
+        quantise_q(LATE_0, "kw_pair")
+        for j in LATE:
+            coarse(j, LATE_0)
+
+        cs = sbuf.tile([P, N], U8, name="cs", tag="q_bf_late0", align_bytes=ALIGN)
         nc.vector.tensor_copy(cs[:], cs_pool[:].indirect(offsets[:]))
-        q_last = keep.tile([P, 2, PACK, P], F32, name="q_last", tag="cs_pool", align_bytes=64)
-        load_q(3, q_last[:, 0])
-        load_q(4, q_last[:, 1])
+        q_late1 = sbuf.tile([P, len(LATE), PACK, P], F32, name="q_late1", tag="cs_pool", align_bytes=ALIGN)
+        load_q(BLOCK2_1, q_late1[:, 0])
+        load_q(BLOCK3_1, q_late1[:, 1])
         gather_c(0, "cw0")
-        cast_q(2, nc.scalar.copy, "q_bf2")
-        quant_q(2, "cw_pool0")
-        for j in range(2, 4):
-            mm_k(j, 0, True)
-            mm_c(j, 0, False)
-        cast_q(1, nc.scalar.copy, "q_raw2")
-        quant_q(1, "q_bf2")
-        for j in range(2):
-            mm_k(j, 1, False)
-            mm_c(j, 0, False)
-        gather_c(1, "q_raw2")
-        for j in range(2):
-            mm_c(j, 1, True)
-        cast_q(3, nc.scalar.copy, "ks_pool1")
-        cast_q(4, nc.vector.tensor_copy, "kw_pool")
-        quant_q(3, "cs_pool")
-        quant_q(4, "q_codes4")
-        for j in range(2, 4):
-            mm_k(j, 1, False)
-            mm_c(j, 1, True)
+        for j in LATE:
+            fine(j, LATE_0)
+        round_q(EARLY_1, nc.scalar.copy, bf_tile("q_bf_early1", 2 * P, "q_late0")[:])
+        quantise_q(EARLY_1, "cw_pool0")
+        for j in EARLY:
+            coarse(j, EARLY_1)
+            fine(j, EARLY_0)
+        gather_c(1, "q_late0")
+        for j in EARLY:
+            fine(j, EARLY_1)
+        q_bf_late1 = bf_tile("q_bf_late1", len(LATE) * P, "kw_pool")
+        for place, piece in enumerate((BLOCK2_1, BLOCK3_1)):
+            round_q(piece, nc.vector.tensor_copy, q_bf_late1[:, place * P : (place + 1) * P, :])
+            quantise_q(piece, f"q_codes_late1_{place}")
 
-        y_scales = keep.tile([P, NQ], U8, name="y_scales", align_bytes=64)
+        y_scales = sbuf.tile([P, NQ], U8, name="y_scales", align_bytes=ALIGN)
         words_out = out_1[0].rearrange("p q t -> p (q t)").bitcast(I32)
-
-        y_q = [keep.tile([P, PACK, P], F32, name=f"y_q{j}") for j in range(BLOCKS)]
-        y = [keep.tile([P, PACK, P], F32, name=f"y{j}") for j in range(BLOCKS)]
-        y_words = [keep.tile([P, 2 * P], I32, name=f"y_words{h}", align_bytes=64) for h in range(BLOCKS // 2)]
+        y_by_query = [sbuf.tile([P, PACK, P], F32, name=f"y_by_query{j}") for j in range(BLOCKS)]
+        y = [sbuf.tile([P, PACK, P], F32, name=f"y{j}") for j in range(BLOCKS)]
+        y_words = [sbuf.tile([P, 2 * P], I32, name=f"y_words{h}", align_bytes=ALIGN) for h in range(BLOCKS // 2)]
         turned = {}
 
-        def sigmoid_and_turn(j):
+        def weigh_and_turn(j):
             nc.scalar.activation(
-                y_q[j][:].rearrange("q (h e) p -> q h p e", e=2),
-                acc[j][:].rearrange("q (p h e) -> q h p e", h=2, e=2),
+                y_by_query[j][:].rearrange("q (h e) p -> q h p e", e=2),
+                sums[j][:].rearrange("q (p h e) -> q h p e", h=2, e=2),
                 SIGMOID,
                 bias=neg_th[:, j : j + 1],
             )
-            turned[j] = psum.tile([P, PACK, P], F32, name=f"turned{j}", tag="turned", bufs=4)
+            turned[j] = turn_bank(f"turned{j}")
             for u in range(PACK):
-                nc.tensor.transpose(turned[j][:, u, :], y_q[j][:, u, :], ident[:])
+                nc.tensor.transpose(turned[j][:, u, :], y_by_query[j][:, u, :], ident[:])
 
         def hand_out(j, engine_copy):
             cols = slice(j * P, (j + 1) * P)
             engine_copy(y[j][:], turned[j][:])
             nc.sync.dma_start(out_0[:, cols].rearrange("(p u) q -> p u q", u=PACK), y[j][:])
-            y_bf = keep.tile([P, P, PACK], BF16, name=f"y_bf{j}", align_bytes=64)
-            weave(nc.vector.tensor_copy, y_bf[:], y[j][:])
-            half = y_words[j // 2]
+            y_bf = sbuf.tile([P, P, PACK], BF16, name=f"y_bf{j}", align_bytes=ALIGN)
+            interleave(nc.vector.tensor_copy, y_bf[:], y[j][:])
+            pair, place = divmod(j, 2)
             nc.vector.quantize_mx(
-                half[:, (j % 2) * P : (j % 2 + 1) * P].bitcast(FP8X4), y_scales[:, cols], y_bf[:].rearrange("p q u -> p (q u)")
+                y_words[pair][:, place * P : (place + 1) * P].bitcast(FP8X4),
+                y_scales[:, cols],
+                y_bf[:].rearrange("p q u -> p (q u)"),
             )
-            if j % 2 == 1:
-                nc.sync.dma_start(words_out[:, (j - 1) * P : (j + 1) * P], half[:])
+            if place == 1:
+                nc.sync.dma_start(words_out[:, 2 * pair * P : 2 * (pair + 1) * P], y_words[pair][:])
 
+        for j, piece, ready in ((LATE[0], BLOCK2_1, EARLY), (LATE[1], BLOCK3_1, LATE)):
+            coarse(j, piece)
+            fine(j, piece)
+            for done in ready:
+                weigh_and_turn(done)
         for j in range(BLOCKS):
-            sigmoid_and_turn(j)
-        for j in range(BLOCKS):
-            hand_out(j, nc.vector.tensor_copy if j == 0 else nc.scalar.copy)
+            hand_out(j, nc.vector.tensor_copy if j % 2 == 0 else nc.scalar.copy)
 
-        for quad in range(4):
+        for quad in range(P // QUAD):
             queue = nc.sync if quad % 2 == 0 else nc.scalar
-            queue.dma_start(out_2[0, 4 * quad : 4 * quad + 4, :].bitcast(I32), y_scales[32 * quad : 32 * quad + 4, :].bitcast(I32))
+            queue.dma_start(
+                out_2[0, QUAD_ROWS * quad : QUAD_ROWS * (quad + 1), :].bitcast(I32),
+                y_scales[QUAD * quad : QUAD * quad + QUAD_ROWS, :].bitcast(I32),
+            )

@@ -28,8 +28,8 @@ SPREAD = P // (QUAD_ROWS * P // QUAD)
 C_FIRST = QUAD_ROWS
 ALIGN = 64
 
-EARLY_0, LATE_0, EARLY_1, BLOCK2_1, BLOCK3_1 = (0, 0, 2 * P), (0, 2 * P, 2 * P), (1, 0, 2 * P), (1, 2 * P, P), (1, 3 * P, P)
-EARLY, LATE = (0, 1), (2, 3)
+
+FIRST_0, SECOND_0, BACK_0, FRONT_1, BLOCK2_1, BLOCK3_1 = (0, 0, P), (0, P, P), (0, 2 * P, 2 * P), (1, 0, 2 * P), (1, 2 * P, P), (1, 3 * P, P)
 
 
 def interleave(engine_copy, dst, src):
@@ -43,83 +43,84 @@ def tile_attend_plw_residsig_topk_kernel(tc, qT, k_words, k_scales, c_words, c_s
     nc = tc.nc
     with ExitStack() as ctx:
         sbuf = ctx.enter_context(tc.tile_pool(name="sbuf", bufs=1))
+        shared = ctx.enter_context(tc.tile_pool(name="shared", bufs=1))
         psum = ctx.enter_context(tc.psum_pool(name="psum", bufs=1))
 
-        q_raw, q_bf, q_codes, q_scales = {}, {}, {}, {}
-        cw_pool, cw = {}, {}
+        def tile(shape, dtype, name, buffer=None):
+            return sbuf.tile(shape, dtype, name=name, tag=buffer or name, align_bytes=ALIGN)
+
+        def shared_tile(shape, dtype, name, offset):
+            return shared.tile(shape, dtype, name=name, offset=offset, align_bytes=ALIGN)
 
         def load_q(piece, dst):
             o, first, width = piece
-            q_raw[piece] = dst
             rows = qT[0, o * K_PASS : (o + 1) * K_PASS, first : first + width]
             nc.sync.dma_start(dst, rows.rearrange("(p t) w -> p t w", t=PACK))
 
-        def load_c(o, buffer):
-            cw_pool[o] = sbuf.tile([P, T], I32, name=f"cw_pool{o}", tag=buffer, align_bytes=ALIGN)
-            nc.sync.dma_start(cw_pool[o][:], c_words[o].rearrange("p t b -> p (t b)").bitcast(I32))
+        def load_words(pool, words):
+            nc.sync.dma_start(pool[:], words.rearrange("p t b -> p (t b)").bitcast(I32))
+            return pool
 
-        load_q(EARLY_0, sbuf.tile([P, PACK, 2 * P], F32, name="q_early0")[:])
-        th_rows = sbuf.tile([P, P], F32, name="th_rows")
-        nc.gpsimd.memset(th_rows[:], 0.0)
-        nc.sync.dma_start(th_rows[0:BLOCKS, :], th[0, 0].rearrange("(j p) -> j p", p=P))
         offsets = sbuf.tile([P, N // 16], U16, name="offsets")
         nc.sync.dma_start(offsets[:], offs)
-
-        ks_pool = [sbuf.tile([P, T], U8, name=f"ks_pool{o}", align_bytes=ALIGN) for o in range(PASSES)]
-        cs_pool = sbuf.tile([P, T], U8, name="cs_pool", align_bytes=ALIGN)
-        ks = sbuf.tile([P, PASSES * N], U8, name="ks", align_bytes=ALIGN)
+        ks_pool = [tile([P, T], U8, "ks_pool0"), shared_tile([P, T], U8, "ks_pool1", 1024)]
+        cs_pool = shared_tile([P, T], U8, "cs_pool", 17408)
+        ks = tile([P, PASSES * N], U8, "ks")
+        th_rows = tile([P, P], F32, "th_rows")
         nc.gpsimd.memset(ks_pool[0][:].bitcast(I32), 0)
         nc.vector.memset(ks_pool[1][:].bitcast(I32), 0)
         nc.gpsimd.memset(cs_pool[:].bitcast(I32), 0)
+        q_first0 = tile([P, PACK, P], F32, "q_first0")
+        q_second0 = tile([P, PACK, P], F32, "q_second0")
+        load_q(FIRST_0, q_first0[:])
+        nc.sync.dma_start(ks_pool[0][0:P:SPREAD, :].bitcast(I32), k_scales[0].bitcast(I32))
+        load_q(SECOND_0, q_second0[:])
+        nc.sync.dma_start(ks_pool[1][0:P:SPREAD, :].bitcast(I32), k_scales[1].bitcast(I32))
+        ident = tile([P, P], F32, "ident")
+        nc.vector.memset(ident[:], 0.0)
+        make_identity(nc, ident[:], nomemset=True)
+        nc.vector.memset(th_rows[:], 0.0)
         nc.vector.memset(ks[:].bitcast(I32), 0)
+        nc.gpsimd.dma_start(th_rows[0:BLOCKS, :], th[0, 0].rearrange("(j p) -> j p", p=P))
 
-        for o in range(PASSES):
-            nc.sync.dma_start(ks_pool[o][0:P:SPREAD, :].bitcast(I32), k_scales[o].bitcast(I32))
-        kw_pool = sbuf.tile([P, T], I32, name="kw_pool", align_bytes=ALIGN)
-        nc.sync.dma_start(kw_pool[:], k_words[0].rearrange("p t b -> p (t b)").bitcast(I32))
+        kw_pool = load_words(shared_tile([P, T], I32, "kw_pool", 20480), k_words[0])
         for quad in range(P // QUAD):
             first = QUAD * quad + C_FIRST
             nc.sync.dma_start(
                 cs_pool[first : first + QUAD_ROWS * PASSES, :].bitcast(I32),
                 c_scales[:, QUAD_ROWS * quad : QUAD_ROWS * (quad + 1), :].bitcast(I32),
             )
+        q_back0 = tile([P, PACK, 2 * P], F32, "q_back0")
+        load_q(BACK_0, q_back0[:])
+        cw_pool0 = load_words(tile([P, T], I32, "cw_pool0"), c_words[0])
 
-        ident = sbuf.tile([P, P], F32, name="ident")
-        make_identity(nc, ident[:])
+        def gather(dst, window):
+            nc.vector.tensor_copy(dst, window.indirect(offsets[:]))
 
-        load_q(LATE_0, sbuf.tile([P, PACK, 2 * P], F32, name="q_late0", align_bytes=ALIGN)[:])
-        load_c(0, "cw_pool0")
+        def gather_scales(rows, pools):
+            for o in range(PASSES):
+                gather(rows[:, o * N : (o + 1) * N], pools[o][:])
+            return rows
 
-        def turn_bank(name):
-            return psum.tile([P, PACK, P], F32, name=name, tag="turned", bufs=BLOCKS)
+        def move_scales(queue, dst, rows, first):
+            for r in range(QUAD_ROWS):
+                queue.dma_start(dst[first + r : P : QUAD, :].bitcast(I32), rows[first + SPREAD * r : P : QUAD, :].bitcast(I32))
 
-        th_turned = turn_bank("th_turned")
-        nc.tensor.transpose(th_turned[:, 0, :], th_rows[:], ident[:])
-        neg_th = sbuf.tile([P, BLOCKS], F32, name="neg_th")
-        nc.scalar.activation(neg_th[:], th_turned[:, 0, 0:BLOCKS], COPY, scale=-1.0)
+        q_bf, q_codes, q_scales = {}, {}, {}
 
-        kw_pair = sbuf.tile([P, N], U32, name="kw_pair", align_bytes=ALIGN)
-        kw = sbuf.tile([P, PASSES * N], U16, name="kw", align_bytes=ALIGN)
-        sums = [psum.tile([P, N], F32, name=f"sum{j}") for j in range(BLOCKS)]
-
-        def gather_c(o, buffer):
-            cw[o] = sbuf.tile([P, N], U32, name=f"cw{o}", tag=buffer, align_bytes=ALIGN)
-            nc.vector.tensor_copy(cw[o][:], cw_pool[o][:].bitcast(U32).indirect(offsets[:]))
-
-        def bf_tile(name, width, buffer):
-            return sbuf.tile([P, width, PACK], BF16, name=name, tag=buffer, align_bytes=ALIGN)
-
-        def round_q(piece, engine_copy, dst):
+        def round_q(piece, engine_copy, dst, raw):
             q_bf[piece] = dst
-            interleave(engine_copy, dst, q_raw[piece])
+            interleave(engine_copy, dst, raw)
 
-        def quantise_q(piece, buffer):
+        def quantise_q(piece, buffer=None, scales=None):
             o, first, width = piece
-            q_codes[piece] = sbuf.tile([P, width], U32, name=f"q_codes{o}_{first}", tag=buffer, align_bytes=ALIGN)
-            q_scales[piece] = sbuf.tile([P, width], U8, name=f"q_scales{o}_{first}", align_bytes=ALIGN)
+            q_codes[piece] = tile([P, width], U32, f"q_codes{o}_{first}", buffer)
+            q_scales[piece] = scales or tile([P, width], U8, f"q_scales{o}_{first}")
             nc.vector.quantize_mx(
                 q_codes[piece][:].bitcast(FP8X4), q_scales[piece][:], q_bf[piece].rearrange("p c t -> p (c t)")
             )
+
+        sums = [psum.tile([P, N], F32, name=f"sum{j}") for j in range(BLOCKS)]
 
         def product(j, piece, keys, key_scales, start, stop):
             cols = slice(j * P - piece[1], (j + 1) * P - piece[1])
@@ -136,89 +137,111 @@ def tile_attend_plw_residsig_topk_kernel(tc, qT, k_words, k_scales, c_words, c_s
             o = piece[0]
             product(j, piece, cw[o][:].bitcast(FP8X4), cs[C_FIRST + QUAD_ROWS * o : P, :], False, o == PASSES - 1)
 
-        ks_rows = sbuf.tile([P, PASSES * N], U8, name="ks_rows", align_bytes=ALIGN)
-        for o in range(PASSES):
-            nc.vector.tensor_copy(ks_rows[:, o * N : (o + 1) * N], ks_pool[o][:].indirect(offsets[:]))
-        for r in range(QUAD_ROWS):
-            nc.sync.dma_start(ks[r:P:QUAD, :].bitcast(I32), ks_rows[SPREAD * r : P : QUAD, :].bitcast(I32))
-        load_q(EARLY_1, sbuf.tile([P, PACK, 2 * P], F32, name="q_early1", tag="ks_pool1", align_bytes=ALIGN)[:])
+        def turn_bank(name):
+            return psum.tile([P, PACK, P], F32, name=name, tag="turned", bufs=BLOCKS)
 
-        nc.vector.tensor_copy(kw_pair[:], kw_pool[:].bitcast(U32).indirect(offsets[:]))
-        load_c(1, "kw_pool")
+        q_bf_front0 = tile([P, 2 * P * PACK], BF16, "q_bf_front0")
+        for place, raw in enumerate((q_first0, q_second0)):
+            interleave(nc.scalar.copy, q_bf_front0[:, place * P * PACK : (place + 1) * P * PACK].rearrange("p (c t) -> p c t", t=PACK), raw[:])
+        ks_rows = gather_scales(tile([P, PASSES * N], U8, "ks_rows"), ks_pool)
+        move_scales(nc.sync, ks, ks_rows, 0)
+        q_front1 = tile([P, PACK, 2 * P], F32, "q_front1", "ks_pool0")
+        load_q(FRONT_1, q_front1[:])
+        cw_pool1 = load_words(shared_tile([P, T], I32, "cw_pool1", 2048), c_words[1])
+
+
+        kw_pair = shared_tile([P, N], U32, "kw_pair", 0)
+        gather(kw_pair[:], kw_pool[:].bitcast(U32))
+        late = (BLOCK2_1, BLOCK3_1)
+        q_late = [shared_tile([P, PACK, P], F32, f"q_late{place}", 20480 + 2048 * place) for place in range(2)]
+        for place, piece in enumerate(late):
+            load_q(piece, q_late[place][:])
+        kw = tile([P, PASSES * N], U16, "kw")
         nc.vector.tensor_copy(
             kw[:].rearrange("p (o s) -> p o s", o=PASSES),
             kw_pair[:].bitcast(U16).rearrange("p (s o) -> p o s", o=PASSES),
         )
-        round_q(EARLY_0, nc.scalar.copy, bf_tile("q_bf_early0", 2 * P, "q_bf_early0")[:])
-        quantise_q(EARLY_0, "ks_pool0")
-        for j in EARLY:
-            coarse(j, EARLY_0)
-        round_q(LATE_0, nc.scalar.copy, bf_tile("q_bf_late0", 2 * P, "q_bf_late0")[:])
-        quantise_q(LATE_0, "kw_pair")
-        for j in LATE:
-            coarse(j, LATE_0)
+        front0 = (0, 0, 2 * P)
+        q_bf[front0] = q_bf_front0[:].rearrange("p (c t) -> p c t", t=PACK)
+        quantise_q(front0, None, shared_tile([P, 2 * P], U8, "q_scales_front0", 0))
+        round_q(BACK_0, nc.scalar.copy, tile([P, 2 * P, PACK], BF16, "q_bf_back0")[:], q_back0[:])
+        th_turned = turn_bank("th_turned")
+        nc.tensor.transpose(th_turned[:, 0, :], th_rows[:], ident[:])
+        neg_th = tile([P, BLOCKS], F32, "neg_th", "q_back0")
+        nc.scalar.activation(neg_th[:], th_turned[:, 0, 0:BLOCKS], COPY, scale=-1.0)
+        quantise_q(BACK_0)
+        pass0 = [front0, front0, BACK_0, BACK_0]
+        for j in range(BLOCKS):
+            coarse(j, pass0[j])
+        cs = tile([P, N], U8, "cs", "q_bf_back0")
+        gather(cs[:], cs_pool[:])
+        cw = [shared_tile([P, N], U32, "cw0", 17408)]
+        gather(cw[0][:], cw_pool0[:].bitcast(U32))
+        for j in range(BLOCKS):
+            fine(j, pass0[j])
+        round_q(FRONT_1, nc.scalar.copy, tile([P, 2 * P, PACK], BF16, "q_bf_front1")[:], q_front1[:])
+        quantise_q(FRONT_1, "cw_pool0")
+        for j in range(2):
+            coarse(j, FRONT_1)
+        cw.append(tile([P, N], U32, "cw1", "q_bf_front1"))
+        gather(cw[1][:], cw_pool1[:].bitcast(U32))
 
-        cs = sbuf.tile([P, N], U8, name="cs", tag="q_bf_late0", align_bytes=ALIGN)
-        nc.vector.tensor_copy(cs[:], cs_pool[:].indirect(offsets[:]))
-        q_late1 = sbuf.tile([P, len(LATE), PACK, P], F32, name="q_late1", tag="cs_pool", align_bytes=ALIGN)
-        load_q(BLOCK2_1, q_late1[:, 0])
-        load_q(BLOCK3_1, q_late1[:, 1])
-        gather_c(0, "cw0")
-        for j in LATE:
-            fine(j, LATE_0)
-        round_q(EARLY_1, nc.scalar.copy, bf_tile("q_bf_early1", 2 * P, "q_late0")[:])
-        quantise_q(EARLY_1, "cw_pool0")
-        for j in EARLY:
-            coarse(j, EARLY_1)
-            fine(j, EARLY_0)
-        gather_c(1, "q_late0")
-        for j in EARLY:
-            fine(j, EARLY_1)
-        q_bf_late1 = bf_tile("q_bf_late1", len(LATE) * P, "kw_pool")
-        for place, piece in enumerate((BLOCK2_1, BLOCK3_1)):
-            round_q(piece, nc.vector.tensor_copy, q_bf_late1[:, place * P : (place + 1) * P, :])
-            quantise_q(piece, f"q_codes_late1_{place}")
+        for place, piece in enumerate(late):
+            dst = shared_tile([P, P, PACK], BF16, f"q_bf_late{place}", 2048 + place * P * PACK * 2)
+            round_q(piece, nc.vector.tensor_copy, dst[:], q_late[place][:])
+        for piece in late:
+            quantise_q(piece)
+        pass1 = [FRONT_1, FRONT_1, BLOCK2_1, BLOCK3_1]
 
-        y_scales = sbuf.tile([P, NQ], U8, name="y_scales", align_bytes=ALIGN)
+        y_scales = tile([P, NQ], U8, "y_scales")
         words_out = out_1[0].rearrange("p q t -> p (q t)").bitcast(I32)
-        y_by_query = [sbuf.tile([P, PACK, P], F32, name=f"y_by_query{j}") for j in range(BLOCKS)]
-        y = [sbuf.tile([P, PACK, P], F32, name=f"y{j}") for j in range(BLOCKS)]
-        y_words = [sbuf.tile([P, 2 * P], I32, name=f"y_words{h}", align_bytes=ALIGN) for h in range(BLOCKS // 2)]
+        y_by_query = [tile([P, PACK, P], F32, f"y_by_query{j}") for j in range(BLOCKS)]
+        y = [tile([P, PACK, P], F32, f"y{j}") for j in range(BLOCKS)]
+        y_words = [tile([P, 2 * P], I32, f"y_words{h}") for h in range(BLOCKS // 2)]
         turned = {}
 
-        def weigh_and_turn(j):
+        def close(j):
+            if pass1[j] in late:
+                coarse(j, pass1[j])
+            fine(j, pass1[j])
             nc.scalar.activation(
                 y_by_query[j][:].rearrange("q (h e) p -> q h p e", e=2),
                 sums[j][:].rearrange("q (p h e) -> q h p e", h=2, e=2),
                 SIGMOID,
                 bias=neg_th[:, j : j + 1],
             )
+
+        def turn(j):
             turned[j] = turn_bank(f"turned{j}")
             for u in range(PACK):
                 nc.tensor.transpose(turned[j][:, u, :], y_by_query[j][:, u, :], ident[:])
 
-        def hand_out(j, engine_copy):
-            cols = slice(j * P, (j + 1) * P)
+        y_bf = [tile([P, P, PACK], BF16, f"y_bf{j}") for j in range(BLOCKS)]
+
+        def store(j, engine_copy):
             engine_copy(y[j][:], turned[j][:])
-            nc.sync.dma_start(out_0[:, cols].rearrange("(p u) q -> p u q", u=PACK), y[j][:])
-            y_bf = sbuf.tile([P, P, PACK], BF16, name=f"y_bf{j}", align_bytes=ALIGN)
-            interleave(nc.vector.tensor_copy, y_bf[:], y[j][:])
+            nc.sync.dma_start(out_0[:, j * P : (j + 1) * P].rearrange("(p u) q -> p u q", u=PACK), y[j][:])
+
+        def quantise_y(j):
             pair, place = divmod(j, 2)
             nc.vector.quantize_mx(
                 y_words[pair][:, place * P : (place + 1) * P].bitcast(FP8X4),
-                y_scales[:, cols],
-                y_bf[:].rearrange("p q u -> p (q u)"),
+                y_scales[:, j * P : (j + 1) * P],
+                y_bf[j][:].rearrange("p q u -> p (q u)"),
             )
             if place == 1:
                 nc.sync.dma_start(words_out[:, 2 * pair * P : 2 * (pair + 1) * P], y_words[pair][:])
 
-        for j, piece, ready in ((LATE[0], BLOCK2_1, EARLY), (LATE[1], BLOCK3_1, LATE)):
-            coarse(j, piece)
-            fine(j, piece)
-            for done in ready:
-                weigh_and_turn(done)
         for j in range(BLOCKS):
-            hand_out(j, nc.vector.tensor_copy if j % 2 == 0 else nc.scalar.copy)
+            close(j)
+        for j in range(BLOCKS):
+            turn(j)
+        for j in range(BLOCKS):
+            store(j, nc.vector.tensor_copy if j % 2 == 0 else nc.scalar.copy)
+        for j in (0, 2, 3, 1):
+            interleave(nc.scalar.copy if j == 1 else nc.vector.tensor_copy, y_bf[j][:], y[j][:])
+        for j in (0, 2, 3, 1):
+            quantise_y(j)
 
         for quad in range(P // QUAD):
             queue = nc.sync if quad % 2 == 0 else nc.scalar

@@ -29,7 +29,7 @@ C_FIRST = QUAD_ROWS
 ALIGN = 64
 
 
-FIRST_0, SECOND_0, BACK_0, FRONT_1, BLOCK2_1, BLOCK3_1 = (0, 0, P), (0, P, P), (0, 2 * P, 2 * P), (1, 0, 2 * P), (1, 2 * P, P), (1, 3 * P, P)
+FRONT_0, BACK_0, FRONT_1, BLOCK2_1, BLOCK3_1 = (0, 0, 2 * P), (0, 2 * P, 2 * P), (1, 0, 2 * P), (1, 2 * P, P), (1, 3 * P, P)
 
 
 def interleave(engine_copy, dst, src):
@@ -61,27 +61,26 @@ def tile_attend_plw_residsig_topk_kernel(tc, qT, k_words, k_scales, c_words, c_s
             nc.sync.dma_start(pool[:], words.rearrange("p t b -> p (t b)").bitcast(I32))
             return pool
 
+        q_pass0 = tile([P, PACK, NQ], F32, "q_pass0")
+        rows0 = qT[0, 0:K_PASS, :].rearrange("(p t) w -> p t w", t=PACK)
+        nc.sync.dma_start(q_pass0[:, 0:2, :], rows0[:, 0:2, :])
         offsets = sbuf.tile([P, N // 16], U16, name="offsets")
         nc.sync.dma_start(offsets[:], offs)
         ks_pool = [tile([P, T], U8, "ks_pool0"), shared_tile([P, T], U8, "ks_pool1", 1024)]
         cs_pool = shared_tile([P, T], U8, "cs_pool", 17408)
         ks = tile([P, PASSES * N], U8, "ks")
-        th_rows = tile([P, P], F32, "th_rows")
+        th_rows = shared_tile([P, P], F32, "th_rows", 13056)
+        nc.gpsimd.memset(th_rows[:], 0.0)
+        nc.sync.dma_start(th_rows[0:BLOCKS, :], th[0, 0].rearrange("(j p) -> j p", p=P))
         nc.gpsimd.memset(ks_pool[0][:].bitcast(I32), 0)
         nc.vector.memset(ks_pool[1][:].bitcast(I32), 0)
         nc.gpsimd.memset(cs_pool[:].bitcast(I32), 0)
-        q_first0 = tile([P, PACK, P], F32, "q_first0")
-        q_second0 = tile([P, PACK, P], F32, "q_second0")
-        load_q(FIRST_0, q_first0[:])
-        nc.sync.dma_start(ks_pool[0][0:P:SPREAD, :].bitcast(I32), k_scales[0].bitcast(I32))
-        load_q(SECOND_0, q_second0[:])
-        nc.sync.dma_start(ks_pool[1][0:P:SPREAD, :].bitcast(I32), k_scales[1].bitcast(I32))
+        for o in range(PASSES):
+            nc.sync.dma_start(ks_pool[o][0:P:SPREAD, :].bitcast(I32), k_scales[o].bitcast(I32))
         ident = tile([P, P], F32, "ident")
         nc.vector.memset(ident[:], 0.0)
         make_identity(nc, ident[:], nomemset=True)
-        nc.vector.memset(th_rows[:], 0.0)
         nc.vector.memset(ks[:].bitcast(I32), 0)
-        nc.gpsimd.dma_start(th_rows[0:BLOCKS, :], th[0, 0].rearrange("(j p) -> j p", p=P))
 
         kw_pool = load_words(shared_tile([P, T], I32, "kw_pool", 20480), k_words[0])
         for quad in range(P // QUAD):
@@ -90,9 +89,10 @@ def tile_attend_plw_residsig_topk_kernel(tc, qT, k_words, k_scales, c_words, c_s
                 cs_pool[first : first + QUAD_ROWS * PASSES, :].bitcast(I32),
                 c_scales[:, QUAD_ROWS * quad : QUAD_ROWS * (quad + 1), :].bitcast(I32),
             )
-        q_back0 = tile([P, PACK, 2 * P], F32, "q_back0")
-        load_q(BACK_0, q_back0[:])
+        nc.sync.dma_start(q_pass0[:, 2:4, :], rows0[:, 2:4, :])
         cw_pool0 = load_words(tile([P, T], I32, "cw_pool0"), c_words[0])
+        q_front1 = tile([P, PACK, 2 * P], F32, "q_front1")
+        load_q(FRONT_1, q_front1[:])
 
         def gather(dst, window):
             nc.vector.tensor_copy(dst, window.indirect(offsets[:]))
@@ -140,13 +140,13 @@ def tile_attend_plw_residsig_topk_kernel(tc, qT, k_words, k_scales, c_words, c_s
         def turn_bank(name):
             return psum.tile([P, PACK, P], F32, name=name, tag="turned", bufs=BLOCKS)
 
-        q_bf_front0 = tile([P, 2 * P * PACK], BF16, "q_bf_front0")
-        for place, raw in enumerate((q_first0, q_second0)):
-            interleave(nc.scalar.copy, q_bf_front0[:, place * P * PACK : (place + 1) * P * PACK].rearrange("p (c t) -> p c t", t=PACK), raw[:])
+        th_turned = turn_bank("th_turned")
+        nc.tensor.transpose(th_turned[:, 0, :], th_rows[:], ident[:])
+        neg_th = tile([P, BLOCKS], F32, "neg_th")
+        nc.scalar.activation(neg_th[:], th_turned[:, 0, 0:BLOCKS], COPY, scale=-1.0)
+        round_q(FRONT_0, nc.scalar.copy, shared_tile([P, 2 * P, PACK], BF16, "q_bf_front0", 11264)[:], q_pass0[:, :, 0 : 2 * P])
         ks_rows = gather_scales(tile([P, PASSES * N], U8, "ks_rows"), ks_pool)
         move_scales(nc.sync, ks, ks_rows, 0)
-        q_front1 = tile([P, PACK, 2 * P], F32, "q_front1", "ks_pool0")
-        load_q(FRONT_1, q_front1[:])
         cw_pool1 = load_words(shared_tile([P, T], I32, "cw_pool1", 2048), c_words[1])
 
 
@@ -161,21 +161,15 @@ def tile_attend_plw_residsig_topk_kernel(tc, qT, k_words, k_scales, c_words, c_s
             kw[:].rearrange("p (o s) -> p o s", o=PASSES),
             kw_pair[:].bitcast(U16).rearrange("p (s o) -> p o s", o=PASSES),
         )
-        front0 = (0, 0, 2 * P)
-        q_bf[front0] = q_bf_front0[:].rearrange("p (c t) -> p c t", t=PACK)
-        quantise_q(front0, None, shared_tile([P, 2 * P], U8, "q_scales_front0", 0))
-        round_q(BACK_0, nc.scalar.copy, tile([P, 2 * P, PACK], BF16, "q_bf_back0")[:], q_back0[:])
-        th_turned = turn_bank("th_turned")
-        nc.tensor.transpose(th_turned[:, 0, :], th_rows[:], ident[:])
-        neg_th = tile([P, BLOCKS], F32, "neg_th", "q_back0")
-        nc.scalar.activation(neg_th[:], th_turned[:, 0, 0:BLOCKS], COPY, scale=-1.0)
-        quantise_q(BACK_0)
-        pass0 = [front0, front0, BACK_0, BACK_0]
+        cs = shared_tile([P, N], U8, "cs", 0)
+        gather(cs[:], cs_pool[:])
+        quantise_q(FRONT_0, None, shared_tile([P, 2 * P], U8, "q_scales_front0", 17408))
+        round_q(BACK_0, nc.scalar.copy, shared_tile([P, 2 * P, PACK], BF16, "q_bf_back0", 13312)[:], q_pass0[:, :, 2 * P : NQ])
+        quantise_q(BACK_0, None, shared_tile([P, 2 * P], U8, "q_scales_back0", 17408 + 2 * P))
+        pass0 = [FRONT_0, FRONT_0, BACK_0, BACK_0]
         for j in range(BLOCKS):
             coarse(j, pass0[j])
-        cs = tile([P, N], U8, "cs", "q_bf_back0")
-        gather(cs[:], cs_pool[:])
-        cw = [shared_tile([P, N], U32, "cw0", 17408)]
+        cw = [shared_tile([P, N], U32, "cw0", 13312)]
         gather(cw[0][:], cw_pool0[:].bitcast(U32))
         for j in range(BLOCKS):
             fine(j, pass0[j])
@@ -189,7 +183,6 @@ def tile_attend_plw_residsig_topk_kernel(tc, qT, k_words, k_scales, c_words, c_s
         for place, piece in enumerate(late):
             dst = shared_tile([P, P, PACK], BF16, f"q_bf_late{place}", 2048 + place * P * PACK * 2)
             round_q(piece, nc.vector.tensor_copy, dst[:], q_late[place][:])
-        for piece in late:
             quantise_q(piece)
         pass1 = [FRONT_1, FRONT_1, BLOCK2_1, BLOCK3_1]
 
@@ -232,16 +225,20 @@ def tile_attend_plw_residsig_topk_kernel(tc, qT, k_words, k_scales, c_words, c_s
             if place == 1:
                 nc.sync.dma_start(words_out[:, 2 * pair * P : 2 * (pair + 1) * P], y_words[pair][:])
 
-        for j in range(BLOCKS):
+        for j in (0, 1, 2):
             close(j)
+        turn(0)
+        turn(1)
+        close(3)
+        turn(2)
+        turn(3)
         for j in range(BLOCKS):
-            turn(j)
-        for j in range(BLOCKS):
-            store(j, nc.vector.tensor_copy if j % 2 == 0 else nc.scalar.copy)
-        for j in (0, 2, 3, 1):
-            interleave(nc.scalar.copy if j == 1 else nc.vector.tensor_copy, y_bf[j][:], y[j][:])
-        for j in (0, 2, 3, 1):
-            quantise_y(j)
+            store(j, nc.vector.tensor_copy if j < 2 else nc.scalar.copy)
+        for group in ((0, 1), (2,), (3,)):
+            for j in group:
+                interleave(nc.vector.tensor_copy, y_bf[j][:], y[j][:])
+            for j in group:
+                quantise_y(j)
 
         for quad in range(P // QUAD):
             queue = nc.sync if quad % 2 == 0 else nc.scalar

@@ -66,7 +66,7 @@ def tile_attend_plw_residsig_topk_kernel(tc, qT, k_words, k_scales, c_words, c_s
         nc.sync.dma_start(q_pass0[:, 0:2, :], rows0[:, 0:2, :])
         offsets = sbuf.tile([P, N // 16], U16, name="offsets")
         nc.sync.dma_start(offsets[:], offs)
-        ks_pool = [tile([P, T], U8, "ks_pool0"), shared_tile([P, T], U8, "ks_pool1", 1024)]
+        ks_pool = [shared_tile([P, T], U8, "ks_pool0", 0), shared_tile([P, T], U8, "ks_pool1", 31744)]
         cs_pool = shared_tile([P, T], U8, "cs_pool", 17408)
         ks = tile([P, PASSES * N], U8, "ks")
         th_rows = shared_tile([P, P], F32, "th_rows", 13056)
@@ -91,8 +91,6 @@ def tile_attend_plw_residsig_topk_kernel(tc, qT, k_words, k_scales, c_words, c_s
             )
         nc.sync.dma_start(q_pass0[:, 2:4, :], rows0[:, 2:4, :])
         cw_pool0 = load_words(tile([P, T], I32, "cw_pool0"), c_words[0])
-        q_front1 = tile([P, PACK, 2 * P], F32, "q_front1")
-        load_q(FRONT_1, q_front1[:])
 
         def gather(dst, window):
             nc.vector.tensor_copy(dst, window.indirect(offsets[:]))
@@ -147,7 +145,9 @@ def tile_attend_plw_residsig_topk_kernel(tc, qT, k_words, k_scales, c_words, c_s
         round_q(FRONT_0, nc.scalar.copy, shared_tile([P, 2 * P, PACK], BF16, "q_bf_front0", 11264)[:], q_pass0[:, :, 0 : 2 * P])
         ks_rows = gather_scales(tile([P, PASSES * N], U8, "ks_rows"), ks_pool)
         move_scales(nc.sync, ks, ks_rows, 0)
-        cw_pool1 = load_words(shared_tile([P, T], I32, "cw_pool1", 2048), c_words[1])
+        q_front1 = shared_tile([P, PACK, 2 * P], F32, "q_front1", 28672)
+        load_q(FRONT_1, q_front1[:])
+        cw_pool1 = load_words(shared_tile([P, T], I32, "cw_pool1", 33280), c_words[1])
 
 
         kw_pair = shared_tile([P, N], U32, "kw_pair", 0)
@@ -161,9 +161,9 @@ def tile_attend_plw_residsig_topk_kernel(tc, qT, k_words, k_scales, c_words, c_s
             kw[:].rearrange("p (o s) -> p o s", o=PASSES),
             kw_pair[:].bitcast(U16).rearrange("p (s o) -> p o s", o=PASSES),
         )
-        cs = shared_tile([P, N], U8, "cs", 0)
+        quantise_q(FRONT_0, None, shared_tile([P, 2 * P], U8, "q_scales_front0", 0))
+        cs = shared_tile([P, N], U8, "cs", 11264)
         gather(cs[:], cs_pool[:])
-        quantise_q(FRONT_0, None, shared_tile([P, 2 * P], U8, "q_scales_front0", 17408))
         round_q(BACK_0, nc.scalar.copy, shared_tile([P, 2 * P, PACK], BF16, "q_bf_back0", 13312)[:], q_pass0[:, :, 2 * P : NQ])
         quantise_q(BACK_0, None, shared_tile([P, 2 * P], U8, "q_scales_back0", 17408 + 2 * P))
         pass0 = [FRONT_0, FRONT_0, BACK_0, BACK_0]
@@ -181,7 +181,7 @@ def tile_attend_plw_residsig_topk_kernel(tc, qT, k_words, k_scales, c_words, c_s
         gather(cw[1][:], cw_pool1[:].bitcast(U32))
 
         for place, piece in enumerate(late):
-            dst = shared_tile([P, P, PACK], BF16, f"q_bf_late{place}", 2048 + place * P * PACK * 2)
+            dst = shared_tile([P, P, PACK], BF16, f"q_bf_late{place}", 33280 + place * P * PACK * 2)
             round_q(piece, nc.vector.tensor_copy, dst[:], q_late[place][:])
             quantise_q(piece)
         pass1 = [FRONT_1, FRONT_1, BLOCK2_1, BLOCK3_1]

@@ -171,12 +171,13 @@ def tile_attend_plw_residsig_topk_kernel(tc, qT, k_words, k_scales, c_words, c_s
             coarse(j, pass0[j])
         cw = [shared_tile([P, N], U32, "cw0", 13312)]
         gather(cw[0][:], cw_pool0[:].bitcast(U32))
-        for j in range(BLOCKS):
-            fine(j, pass0[j])
+        for j in (2, 3):
+            fine(j, BACK_0)
         round_q(FRONT_1, nc.scalar.copy, tile([P, 2 * P, PACK], BF16, "q_bf_front1")[:], q_front1[:])
         quantise_q(FRONT_1, "cw_pool0")
-        for j in range(2):
+        for j in (0, 1):
             coarse(j, FRONT_1)
+            fine(j, FRONT_0)
         cw.append(tile([P, N], U32, "cw1", "q_bf_front1"))
         gather(cw[1][:], cw_pool1[:].bitcast(U32))
 

@@ -61,9 +61,8 @@ def tile_attend_plw_residsig_topk_kernel(tc, qT, k_words, k_scales, c_words, c_s
             nc.sync.dma_start(pool[:], words.rearrange("p t b -> p (t b)").bitcast(I32))
             return pool
 
-        q_pass0 = tile([P, PACK, NQ], F32, "q_pass0")
-        rows0 = qT[0, 0:K_PASS, :].rearrange("(p t) w -> p t w", t=PACK)
-        nc.sync.dma_start(q_pass0[:, 0:2, :], rows0[:, 0:2, :])
+        q_front1 = tile([P, PACK, 2 * P], F32, "q_front1")
+        load_q(FRONT_1, q_front1[:])
         offsets = sbuf.tile([P, N // 16], U16, name="offsets")
         nc.sync.dma_start(offsets[:], offs)
         ks_pool = [shared_tile([P, T], U8, "ks_pool0", 0), shared_tile([P, T], U8, "ks_pool1", 31744)]
@@ -89,7 +88,8 @@ def tile_attend_plw_residsig_topk_kernel(tc, qT, k_words, k_scales, c_words, c_s
                 cs_pool[first : first + QUAD_ROWS * PASSES, :].bitcast(I32),
                 c_scales[:, QUAD_ROWS * quad : QUAD_ROWS * (quad + 1), :].bitcast(I32),
             )
-        nc.sync.dma_start(q_pass0[:, 2:4, :], rows0[:, 2:4, :])
+        q_pass0 = tile([P, PACK, NQ], F32, "q_pass0")
+        load_q((0, 0, NQ), q_pass0[:])
         cw_pool0 = load_words(tile([P, T], I32, "cw_pool0"), c_words[0])
 
         def gather(dst, window):
@@ -126,10 +126,10 @@ def tile_attend_plw_residsig_topk_kernel(tc, qT, k_words, k_scales, c_words, c_s
                 sums[j][:], q_codes[piece][:, cols].bitcast(FP8X4), q_scales[piece][:, cols], keys, key_scales, start=start, stop=stop
             )
 
-        def coarse(j, piece):
+        def coarse(j, piece, start):
             o = piece[0]
             cols = slice(o * N, (o + 1) * N)
-            product(j, piece, kw[:, cols].bitcast(FP4X4), ks[:, cols], o == 0, False)
+            product(j, piece, kw[:, cols].bitcast(FP4X4), ks[:, cols], start, False)
 
         def fine(j, piece):
             o = piece[0]
@@ -142,11 +142,9 @@ def tile_attend_plw_residsig_topk_kernel(tc, qT, k_words, k_scales, c_words, c_s
         nc.tensor.transpose(th_turned[:, 0, :], th_rows[:], ident[:])
         neg_th = tile([P, BLOCKS], F32, "neg_th")
         nc.scalar.activation(neg_th[:], th_turned[:, 0, 0:BLOCKS], COPY, scale=-1.0)
-        round_q(FRONT_0, nc.scalar.copy, shared_tile([P, 2 * P, PACK], BF16, "q_bf_front0", 11264)[:], q_pass0[:, :, 0 : 2 * P])
+        round_q(FRONT_1, nc.scalar.copy, shared_tile([P, 2 * P, PACK], BF16, "q_bf_front1", 11264)[:], q_front1[:])
         ks_rows = gather_scales(tile([P, PASSES * N], U8, "ks_rows"), ks_pool)
         move_scales(nc.sync, ks, ks_rows, 0)
-        q_front1 = shared_tile([P, PACK, 2 * P], F32, "q_front1", 28672)
-        load_q(FRONT_1, q_front1[:])
         cw_pool1 = load_words(shared_tile([P, T], I32, "cw_pool1", 33280), c_words[1])
 
 
@@ -161,24 +159,25 @@ def tile_attend_plw_residsig_topk_kernel(tc, qT, k_words, k_scales, c_words, c_s
             kw[:].rearrange("p (o s) -> p o s", o=PASSES),
             kw_pair[:].bitcast(U16).rearrange("p (s o) -> p o s", o=PASSES),
         )
-        quantise_q(FRONT_0, None, shared_tile([P, 2 * P], U8, "q_scales_front0", 0))
+        quantise_q(FRONT_1, None, shared_tile([P, 2 * P], U8, "q_scales_front1", 0))
+        for j in (0, 1):
+            coarse(j, FRONT_1, True)
         cs = shared_tile([P, N], U8, "cs", 11264)
         gather(cs[:], cs_pool[:])
-        round_q(BACK_0, nc.scalar.copy, shared_tile([P, 2 * P, PACK], BF16, "q_bf_back0", 13312)[:], q_pass0[:, :, 2 * P : NQ])
-        quantise_q(BACK_0, None, shared_tile([P, 2 * P], U8, "q_scales_back0", 17408 + 2 * P))
-        pass0 = [FRONT_0, FRONT_0, BACK_0, BACK_0]
-        for j in range(BLOCKS):
-            coarse(j, pass0[j])
+        round_q(FRONT_0, nc.scalar.copy, shared_tile([P, 2 * P, PACK], BF16, "q_bf_front0", 13312)[:], q_pass0[:, :, 0 : 2 * P])
+        round_q(BACK_0, nc.scalar.copy, tile([P, 2 * P, PACK], BF16, "q_bf_back0")[:], q_pass0[:, :, 2 * P : NQ])
+        quantise_q(FRONT_0, None, shared_tile([P, 2 * P], U8, "q_scales_front0", 17408))
+        for j in (0, 1):
+            coarse(j, FRONT_0, False)
         cw = [shared_tile([P, N], U32, "cw0", 13312)]
         gather(cw[0][:], cw_pool0[:].bitcast(U32))
-        for j in (2, 3):
-            fine(j, BACK_0)
-        round_q(FRONT_1, nc.scalar.copy, tile([P, 2 * P, PACK], BF16, "q_bf_front1")[:], q_front1[:])
-        quantise_q(FRONT_1, "cw_pool0")
         for j in (0, 1):
-            coarse(j, FRONT_1)
             fine(j, FRONT_0)
-        cw.append(tile([P, N], U32, "cw1", "q_bf_front1"))
+        quantise_q(BACK_0, "cw_pool0")
+        for j in (2, 3):
+            coarse(j, BACK_0, True)
+            fine(j, BACK_0)
+        cw.append(tile([P, N], U32, "cw1", "q_bf_back0"))
         gather(cw[1][:], cw_pool1[:].bitcast(U32))
 
         for place, piece in enumerate(late):
@@ -196,7 +195,7 @@ def tile_attend_plw_residsig_topk_kernel(tc, qT, k_words, k_scales, c_words, c_s
 
         def close(j):
             if pass1[j] in late:
-                coarse(j, pass1[j])
+                coarse(j, pass1[j], False)
             fine(j, pass1[j])
             nc.scalar.activation(
                 y_by_query[j][:].rearrange("q (h e) p -> q h p e", e=2),

@@ -61,48 +61,47 @@ def tile_attend_plw_residsig_topk_kernel(tc, qT, k_words, k_scales, c_words, c_s
             nc.sync.dma_start(pool[:], words.rearrange("p t b -> p (t b)").bitcast(I32))
             return pool
 
-        q_front1 = tile([P, PACK, 2 * P], F32, "q_front1")
-        load_q(FRONT_1, q_front1[:])
+        TH_AT, KS_AT = 2048, 12288
+        ks_pool = shared_tile([P, T], U8, "ks_pool", KS_AT)
+        nc.sync.dma_start(ks_pool[0:QUAD, :].bitcast(I32), k_scales.rearrange("o f t -> (o f) t").bitcast(I32))
         offsets = sbuf.tile([P, N // 16], U16, name="offsets")
         nc.sync.dma_start(offsets[:], offs)
-        ks_pool = [shared_tile([P, T], U8, "ks_pool0", 0), shared_tile([P, T], U8, "ks_pool1", 31744)]
-        cs_pool = shared_tile([P, T], U8, "cs_pool", 17408)
-        ks = tile([P, PASSES * N], U8, "ks")
-        th_rows = shared_tile([P, P], F32, "th_rows", 13056)
+        q_front1 = tile([P, PACK, 2 * P], F32, "q_front1")
+        load_q(FRONT_1, q_front1[:])
+        th_rows = shared_tile([P, P], F32, "th_rows", TH_AT)
+        cs_pool = tile([P, T], U8, "cs_pool")
         nc.gpsimd.memset(th_rows[:], 0.0)
         nc.sync.dma_start(th_rows[0:BLOCKS, :], th[0, 0].rearrange("(j p) -> j p", p=P))
-        nc.gpsimd.memset(ks_pool[0][:].bitcast(I32), 0)
-        nc.vector.memset(ks_pool[1][:].bitcast(I32), 0)
         nc.gpsimd.memset(cs_pool[:].bitcast(I32), 0)
-        for o in range(PASSES):
-            nc.sync.dma_start(ks_pool[o][0:P:SPREAD, :].bitcast(I32), k_scales[o].bitcast(I32))
+        nc.gpsimd.memset(ks_pool[QUAD : 2 * QUAD, :].bitcast(I32), 0)
+        nc.vector.memset(ks_pool[2 * QUAD : P, :].bitcast(I32), 0)
         ident = tile([P, P], F32, "ident")
         nc.vector.memset(ident[:], 0.0)
         make_identity(nc, ident[:], nomemset=True)
-        nc.vector.memset(ks[:].bitcast(I32), 0)
+        ks = [tile([P, N], U8, f"ks{o}") for o in range(PASSES)]
+        for plane in ks:
+            nc.vector.memset(plane[:].bitcast(I32), 0)
 
-        kw_pool = load_words(shared_tile([P, T], I32, "kw_pool", 20480), k_words[0])
         for quad in range(P // QUAD):
             first = QUAD * quad + C_FIRST
             nc.sync.dma_start(
                 cs_pool[first : first + QUAD_ROWS * PASSES, :].bitcast(I32),
                 c_scales[:, QUAD_ROWS * quad : QUAD_ROWS * (quad + 1), :].bitcast(I32),
             )
+        kw_pool = load_words(tile([P, T], I32, "kw_pool"), k_words[0])
         q_pass0 = tile([P, PACK, NQ], F32, "q_pass0")
         load_q((0, 0, NQ), q_pass0[:])
-        cw_pool0 = load_words(tile([P, T], I32, "cw_pool0"), c_words[0])
 
         def gather(dst, window):
             nc.vector.tensor_copy(dst, window.indirect(offsets[:]))
 
-        def gather_scales(rows, pools):
-            for o in range(PASSES):
-                gather(rows[:, o * N : (o + 1) * N], pools[o][:])
-            return rows
-
-        def move_scales(queue, dst, rows, first):
-            for r in range(QUAD_ROWS):
-                queue.dma_start(dst[first + r : P : QUAD, :].bitcast(I32), rows[first + SPREAD * r : P : QUAD, :].bitcast(I32))
+        def move_scales(o, dst):
+            for quad in range(P // QUAD):
+                first = QUAD_ROWS * (o * P // QUAD + quad)
+                nc.sync.dma_start(
+                    dst[QUAD * quad : QUAD * quad + QUAD_ROWS, :].bitcast(I32), ks_rows[first : first + QUAD_ROWS, :].bitcast(I32)
+                )
+            return dst
 
         q_bf, q_codes, q_scales = {}, {}, {}
 
@@ -110,10 +109,10 @@ def tile_attend_plw_residsig_topk_kernel(tc, qT, k_words, k_scales, c_words, c_s
             q_bf[piece] = dst
             interleave(engine_copy, dst, raw)
 
-        def quantise_q(piece, buffer=None, scales=None):
+        def quantise_q(piece):
             o, first, width = piece
-            q_codes[piece] = tile([P, width], U32, f"q_codes{o}_{first}", buffer)
-            q_scales[piece] = scales or tile([P, width], U8, f"q_scales{o}_{first}")
+            q_codes[piece] = tile([P, width], U32, f"q_codes{o}_{first}")
+            q_scales[piece] = tile([P, width], U8, f"q_scales{o}_{first}")
             nc.vector.quantize_mx(
                 q_codes[piece][:].bitcast(FP8X4), q_scales[piece][:], q_bf[piece].rearrange("p c t -> p (c t)")
             )
@@ -126,10 +125,9 @@ def tile_attend_plw_residsig_topk_kernel(tc, qT, k_words, k_scales, c_words, c_s
                 sums[j][:], q_codes[piece][:, cols].bitcast(FP8X4), q_scales[piece][:, cols], keys, key_scales, start=start, stop=stop
             )
 
-        def coarse(j, piece, start):
+        def coarse(j, piece):
             o = piece[0]
-            cols = slice(o * N, (o + 1) * N)
-            product(j, piece, kw[:, cols].bitcast(FP4X4), ks[:, cols], start, False)
+            product(j, piece, kw[:, o * N : (o + 1) * N].bitcast(FP4X4), ks[o][:], o == 0, False)
 
         def fine(j, piece):
             o = piece[0]
@@ -142,47 +140,51 @@ def tile_attend_plw_residsig_topk_kernel(tc, qT, k_words, k_scales, c_words, c_s
         nc.tensor.transpose(th_turned[:, 0, :], th_rows[:], ident[:])
         neg_th = tile([P, BLOCKS], F32, "neg_th")
         nc.scalar.activation(neg_th[:], th_turned[:, 0, 0:BLOCKS], COPY, scale=-1.0)
-        round_q(FRONT_1, nc.scalar.copy, shared_tile([P, 2 * P, PACK], BF16, "q_bf_front1", 11264)[:], q_front1[:])
-        ks_rows = gather_scales(tile([P, PASSES * N], U8, "ks_rows"), ks_pool)
-        move_scales(nc.sync, ks, ks_rows, 0)
-        cw_pool1 = load_words(shared_tile([P, T], I32, "cw_pool1", 33280), c_words[1])
+        round_q(FRONT_1, nc.scalar.copy, shared_tile([P, 2 * P, PACK], BF16, "q_bf_front1", TH_AT + 256 - 2048)[:], q_front1[:])
+        ks_rows = tile([P, N], U8, "ks_rows")
+        gather(ks_rows[:], ks_pool[:])
+        move_scales(0, ks[0])
+        cw_pool0 = load_words(shared_tile([P, T], I32, "cw_pool0", KS_AT + 512 - 8192), c_words[0])
+        cw_pool1 = load_words(shared_tile([P, T], I32, "cw_pool1", KS_AT + 1536), c_words[1])
+        move_scales(1, ks[1])
+        cs = shared_tile([P, N], U8, "cs", KS_AT + 512)
+        gather(cs[:], cs_pool[:])
+        quantise_q(FRONT_1)
 
-
-        kw_pair = shared_tile([P, N], U32, "kw_pair", 0)
+        kw_pair = tile([P, N], U32, "kw_pair", "cs_pool")
         gather(kw_pair[:], kw_pool[:].bitcast(U32))
         late = (BLOCK2_1, BLOCK3_1)
-        q_late = [shared_tile([P, PACK, P], F32, f"q_late{place}", 20480 + 2048 * place) for place in range(2)]
+        q_late_both = tile([P, 2 * PACK * P], F32, "q_late", "kw_pool")
+        q_late = [q_late_both[:, place * PACK * P : (place + 1) * PACK * P].rearrange("p (t w) -> p t w", t=PACK) for place in range(2)]
         for place, piece in enumerate(late):
-            load_q(piece, q_late[place][:])
+            load_q(piece, q_late[place])
         kw = tile([P, PASSES * N], U16, "kw")
         nc.vector.tensor_copy(
             kw[:].rearrange("p (o s) -> p o s", o=PASSES),
             kw_pair[:].bitcast(U16).rearrange("p (s o) -> p o s", o=PASSES),
         )
-        quantise_q(FRONT_1, None, shared_tile([P, 2 * P], U8, "q_scales_front1", 0))
+        round_q(FRONT_0, nc.scalar.copy, tile([P, 2 * P, PACK], BF16, "q_bf_front0")[:], q_pass0[:, :, 0 : 2 * P])
+        round_q(BACK_0, nc.vector.tensor_copy, tile([P, 2 * P, PACK], BF16, "q_bf_back0", "cs_pool")[:], q_pass0[:, :, 2 * P : NQ])
+        quantise_q(BACK_0)
+        for j in (2, 3):
+            coarse(j, BACK_0)
+        quantise_q(FRONT_0)
         for j in (0, 1):
-            coarse(j, FRONT_1, True)
-        cs = shared_tile([P, N], U8, "cs", 11264)
-        gather(cs[:], cs_pool[:])
-        round_q(FRONT_0, nc.scalar.copy, shared_tile([P, 2 * P, PACK], BF16, "q_bf_front0", 13312)[:], q_pass0[:, :, 0 : 2 * P])
-        round_q(BACK_0, nc.scalar.copy, tile([P, 2 * P, PACK], BF16, "q_bf_back0")[:], q_pass0[:, :, 2 * P : NQ])
-        quantise_q(FRONT_0, None, shared_tile([P, 2 * P], U8, "q_scales_front0", 17408))
-        for j in (0, 1):
-            coarse(j, FRONT_0, False)
-        cw = [shared_tile([P, N], U32, "cw0", 13312)]
+            coarse(j, FRONT_0)
+        cw = [tile([P, N], U32, "cw0", "q_bf_front0")]
         gather(cw[0][:], cw_pool0[:].bitcast(U32))
+        for j in (2, 3):
+            fine(j, BACK_0)
         for j in (0, 1):
             fine(j, FRONT_0)
-        quantise_q(BACK_0, "cw_pool0")
-        for j in (2, 3):
-            coarse(j, BACK_0, True)
-            fine(j, BACK_0)
-        cw.append(tile([P, N], U32, "cw1", "q_bf_back0"))
+            coarse(j, FRONT_1)
+        cw.append(shared_tile([P, N], U32, "cw1", KS_AT + 512 - 8192))
         gather(cw[1][:], cw_pool1[:].bitcast(U32))
 
+        q_bf_late = shared_tile([P, 2 * P * PACK], BF16, "q_bf_late", KS_AT + 1536)
         for place, piece in enumerate(late):
-            dst = shared_tile([P, P, PACK], BF16, f"q_bf_late{place}", 33280 + place * P * PACK * 2)
-            round_q(piece, nc.vector.tensor_copy, dst[:], q_late[place][:])
+            dst = q_bf_late[:, place * P * PACK : (place + 1) * P * PACK].rearrange("p (c t) -> p c t", t=PACK)
+            round_q(piece, nc.vector.tensor_copy, dst, q_late[place])
             quantise_q(piece)
         pass1 = [FRONT_1, FRONT_1, BLOCK2_1, BLOCK3_1]
 
@@ -195,7 +197,7 @@ def tile_attend_plw_residsig_topk_kernel(tc, qT, k_words, k_scales, c_words, c_s
 
         def close(j):
             if pass1[j] in late:
-                coarse(j, pass1[j], False)
+                coarse(j, pass1[j])
             fine(j, pass1[j])
             nc.scalar.activation(
                 y_by_query[j][:].rearrange("q (h e) p -> q h p e", e=2),

@@ -69,10 +69,11 @@ def tile_attend_plw_residsig_topk_kernel(tc, qT, k_words, k_scales, c_words, c_s
         q_front1 = tile([P, PACK, 2 * P], F32, "q_front1")
         load_q(FRONT_1, q_front1[:])
         th_rows = shared_tile([P, P], F32, "th_rows", TH_AT)
-        cs_pool = tile([P, T], U8, "cs_pool")
+        cs_pool = [tile([P, T], U8, f"cs_pool{o}") for o in range(PASSES)]
         nc.gpsimd.memset(th_rows[:], 0.0)
         nc.sync.dma_start(th_rows[0:BLOCKS, :], th[0, 0].rearrange("(j p) -> j p", p=P))
-        nc.gpsimd.memset(cs_pool[:].bitcast(I32), 0)
+        nc.gpsimd.memset(cs_pool[0][:].bitcast(I32), 0)
+        nc.vector.memset(cs_pool[1][:].bitcast(I32), 0)
         nc.gpsimd.memset(ks_pool[QUAD : 2 * QUAD, :].bitcast(I32), 0)
         nc.vector.memset(ks_pool[2 * QUAD : P, :].bitcast(I32), 0)
         ident = tile([P, P], F32, "ident")
@@ -81,13 +82,11 @@ def tile_attend_plw_residsig_topk_kernel(tc, qT, k_words, k_scales, c_words, c_s
         ks = [tile([P, N], U8, f"ks{o}") for o in range(PASSES)]
         for plane in ks:
             nc.vector.memset(plane[:].bitcast(I32), 0)
+        cs = tile([P, PASSES * N], U8, "cs")
+        nc.gpsimd.memset(cs[:].bitcast(I32), 0)
 
-        for quad in range(P // QUAD):
-            first = QUAD * quad + C_FIRST
-            nc.sync.dma_start(
-                cs_pool[first : first + QUAD_ROWS * PASSES, :].bitcast(I32),
-                c_scales[:, QUAD_ROWS * quad : QUAD_ROWS * (quad + 1), :].bitcast(I32),
-            )
+        for o in range(PASSES):
+            nc.sync.dma_start(cs_pool[o][C_FIRST:P:SPREAD, :].bitcast(I32), c_scales[o].bitcast(I32))
         kw_pool = load_words(tile([P, T], I32, "kw_pool"), k_words[0])
         q_pass0 = tile([P, PACK, NQ], F32, "q_pass0")
         load_q((0, 0, NQ), q_pass0[:])
@@ -131,7 +130,7 @@ def tile_attend_plw_residsig_topk_kernel(tc, qT, k_words, k_scales, c_words, c_s
 
         def fine(j, piece):
             o = piece[0]
-            product(j, piece, cw[o][:].bitcast(FP8X4), cs[C_FIRST + QUAD_ROWS * o : P, :], False, o == PASSES - 1)
+            product(j, piece, cw[o][:].bitcast(FP8X4), cs[C_FIRST:P, o * N : (o + 1) * N], False, o == PASSES - 1)
 
         def turn_bank(name):
             return psum.tile([P, PACK, P], F32, name=name, tag="turned", bufs=BLOCKS)
@@ -145,13 +144,16 @@ def tile_attend_plw_residsig_topk_kernel(tc, qT, k_words, k_scales, c_words, c_s
         gather(ks_rows[:], ks_pool[:])
         move_scales(0, ks[0])
         cw_pool0 = load_words(shared_tile([P, T], I32, "cw_pool0", KS_AT + 512 - 8192), c_words[0])
-        cw_pool1 = load_words(shared_tile([P, T], I32, "cw_pool1", KS_AT + 1536), c_words[1])
+        cs_rows = shared_tile([P, PASSES * N], U8, "cs_rows", KS_AT + 512)
+        for o in range(PASSES):
+            gather(cs_rows[:, o * N : (o + 1) * N], cs_pool[o][:])
+        for r in range(QUAD_ROWS):
+            nc.sync.dma_start(cs[C_FIRST + r : P : QUAD, :].bitcast(I32), cs_rows[C_FIRST + SPREAD * r : P : QUAD, :].bitcast(I32))
+        cw_pool1 = load_words(tile([P, T], I32, "cw_pool1", "cs_pool1"), c_words[1])
         move_scales(1, ks[1])
-        cs = shared_tile([P, N], U8, "cs", KS_AT + 512)
-        gather(cs[:], cs_pool[:])
         quantise_q(FRONT_1)
 
-        kw_pair = tile([P, N], U32, "kw_pair", "cs_pool")
+        kw_pair = tile([P, N], U32, "kw_pair", "cs_pool0")
         gather(kw_pair[:], kw_pool[:].bitcast(U32))
         late = (BLOCK2_1, BLOCK3_1)
         q_late_both = tile([P, 2 * PACK * P], F32, "q_late", "kw_pool")
@@ -164,7 +166,7 @@ def tile_attend_plw_residsig_topk_kernel(tc, qT, k_words, k_scales, c_words, c_s
             kw_pair[:].bitcast(U16).rearrange("p (s o) -> p o s", o=PASSES),
         )
         round_q(FRONT_0, nc.scalar.copy, tile([P, 2 * P, PACK], BF16, "q_bf_front0")[:], q_pass0[:, :, 0 : 2 * P])
-        round_q(BACK_0, nc.vector.tensor_copy, tile([P, 2 * P, PACK], BF16, "q_bf_back0", "cs_pool")[:], q_pass0[:, :, 2 * P : NQ])
+        round_q(BACK_0, nc.vector.tensor_copy, tile([P, 2 * P, PACK], BF16, "q_bf_back0", "cs_pool0")[:], q_pass0[:, :, 2 * P : NQ])
         quantise_q(BACK_0)
         for j in (2, 3):
             coarse(j, BACK_0)
@@ -181,7 +183,7 @@ def tile_attend_plw_residsig_topk_kernel(tc, qT, k_words, k_scales, c_words, c_s
         cw.append(shared_tile([P, N], U32, "cw1", KS_AT + 512 - 8192))
         gather(cw[1][:], cw_pool1[:].bitcast(U32))
 
-        q_bf_late = shared_tile([P, 2 * P * PACK], BF16, "q_bf_late", KS_AT + 1536)
+        q_bf_late = tile([P, 2 * P * PACK], BF16, "q_bf_late", "cs_pool1")
         for place, piece in enumerate(late):
             dst = q_bf_late[:, place * P * PACK : (place + 1) * P * PACK].rearrange("p (c t) -> p c t", t=PACK)
             round_q(piece, nc.vector.tensor_copy, dst, q_late[place])

@@ -95,11 +95,9 @@ def tile_attend_plw_residsig_topk_kernel(tc, qT, k_words, k_scales, c_words, c_s
             nc.vector.tensor_copy(dst, window.indirect(offsets[:]))
 
         def move_scales(o, dst):
-            for quad in range(P // QUAD):
-                first = QUAD_ROWS * (o * P // QUAD + quad)
-                nc.sync.dma_start(
-                    dst[QUAD * quad : QUAD * quad + QUAD_ROWS, :].bitcast(I32), ks_rows[first : first + QUAD_ROWS, :].bitcast(I32)
-                )
+            rows = P // SPREAD
+            for r in range(QUAD_ROWS):
+                nc.sync.dma_start(dst[r:P:QUAD, :].bitcast(I32), ks_rows[o * rows + r : (o + 1) * rows : QUAD_ROWS, :].bitcast(I32))
             return dst
 
         q_bf, q_codes, q_scales = {}, {}, {}
@@ -184,69 +182,85 @@ def tile_attend_plw_residsig_topk_kernel(tc, qT, k_words, k_scales, c_words, c_s
         gather(cw[1][:], cw_pool1[:].bitcast(U32))
 
         q_bf_late = tile([P, 2 * P * PACK], BF16, "q_bf_late", "cs_pool1")
-        for place, piece in enumerate(late):
+
+        def prepare_late(place):
             dst = q_bf_late[:, place * P * PACK : (place + 1) * P * PACK].rearrange("p (c t) -> p c t", t=PACK)
-            round_q(piece, nc.vector.tensor_copy, dst, q_late[place])
-            quantise_q(piece)
+            round_q(late[place], nc.vector.tensor_copy, dst, q_late[place])
+            quantise_q(late[place])
+
+        prepare_late(0)
         pass1 = [FRONT_1, FRONT_1, BLOCK2_1, BLOCK3_1]
 
         y_scales = tile([P, NQ], U8, "y_scales")
-        words_out = out_1[0].rearrange("p q t -> p (q t)").bitcast(I32)
+        y_words = tile([P, NQ], I32, "y_words")
         y_by_query = [tile([P, PACK, P], F32, f"y_by_query{j}") for j in range(BLOCKS)]
         y = [tile([P, PACK, P], F32, f"y{j}") for j in range(BLOCKS)]
-        y_words = [tile([P, 2 * P], I32, f"y_words{h}") for h in range(BLOCKS // 2)]
-        turned = {}
+        y_bf = [tile([P, P, PACK], BF16, f"y_bf{j}") for j in range(BLOCKS)]
+        WHOLE, LOW, HIGH = slice(0, 2), slice(0, 1), slice(1, 2)
+
+        def places(halves):
+            return slice(2 * halves.start, 2 * halves.stop)
 
         def close(j):
             if pass1[j] in late:
                 coarse(j, pass1[j])
             fine(j, pass1[j])
+
+        def weigh(j, halves):
             nc.scalar.activation(
-                y_by_query[j][:].rearrange("q (h e) p -> q h p e", e=2),
-                sums[j][:].rearrange("q (p h e) -> q h p e", h=2, e=2),
+                y_by_query[j][:].rearrange("q (h e) p -> q h p e", e=2)[:, halves],
+                sums[j][:].rearrange("q (p h e) -> q h p e", h=2, e=2)[:, halves],
                 SIGMOID,
                 bias=neg_th[:, j : j + 1],
             )
 
-        def turn(j):
-            turned[j] = turn_bank(f"turned{j}")
-            for u in range(PACK):
-                nc.tensor.transpose(turned[j][:, u, :], y_by_query[j][:, u, :], ident[:])
+        def turn(j, halves):
+            bank = turn_bank(f"turned{j}_{halves.start}")
+            for u in range(PACK)[places(halves)]:
+                nc.tensor.transpose(bank[:, u, :], y_by_query[j][:, u, :], ident[:])
+            return bank
 
-        y_bf = [tile([P, P, PACK], BF16, f"y_bf{j}") for j in range(BLOCKS)]
+        def empty(j, halves, bank, engine_copy):
+            engine_copy(y[j][:, places(halves), :], bank[:, places(halves), :])
 
-        def store(j, engine_copy):
-            engine_copy(y[j][:], turned[j][:])
-            nc.sync.dma_start(out_0[:, j * P : (j + 1) * P].rearrange("(p u) q -> p u q", u=PACK), y[j][:])
+        def store(j, halves):
+            rows = out_0[:, j * P : (j + 1) * P].rearrange("(p u) q -> p u q", u=PACK)
+            nc.sync.dma_start(rows[:, places(halves), :], y[j][:, places(halves), :])
+
+        def weave(j, engine_copy):
+            interleave(engine_copy, y_bf[j][:], y[j][:])
 
         def quantise_y(j):
-            pair, place = divmod(j, 2)
-            nc.vector.quantize_mx(
-                y_words[pair][:, place * P : (place + 1) * P].bitcast(FP8X4),
-                y_scales[:, j * P : (j + 1) * P],
-                y_bf[j][:].rearrange("p q u -> p (q u)"),
-            )
-            if place == 1:
-                nc.sync.dma_start(words_out[:, 2 * pair * P : 2 * (pair + 1) * P], y_words[pair][:])
+            cols = slice(j * P, (j + 1) * P)
+            nc.vector.quantize_mx(y_words[:, cols].bitcast(FP8X4), y_scales[:, cols], y_bf[j][:].rearrange("p q u -> p (q u)"))
 
+        prepare_late(1)
         for j in (0, 1, 2):
             close(j)
-        turn(0)
-        turn(1)
+            weigh(j, WHOLE)
+        for half in (LOW, HIGH):
+            empty(0, half, turn(0, half), nc.vector.tensor_copy)
+            store(0, half)
+        empty(1, WHOLE, turn(1, WHOLE), nc.scalar.copy)
+        store(1, WHOLE)
         close(3)
-        turn(2)
-        turn(3)
-        for j in range(BLOCKS):
-            store(j, nc.vector.tensor_copy if j < 2 else nc.scalar.copy)
-        for group in ((0, 1), (2,), (3,)):
-            for j in group:
-                interleave(nc.vector.tensor_copy, y_bf[j][:], y[j][:])
-            for j in group:
-                quantise_y(j)
+        weave(0, nc.vector.tensor_copy)
+        weave(1, nc.vector.tensor_copy)
+        empty(2, WHOLE, turn(2, WHOLE), nc.vector.tensor_copy)
+        store(2, WHOLE)
+        weigh(3, LOW)
+        weigh(3, HIGH)
+        quantise_y(0)
+        empty(3, LOW, turn(3, LOW), nc.scalar.copy)
+        empty(3, HIGH, turn(3, HIGH), nc.vector.tensor_copy)
+        store(3, WHOLE)
+        weave(2, nc.scalar.copy)
+        quantise_y(1)
+        weave(3, nc.vector.tensor_copy)
+        quantise_y(2)
+        quantise_y(3)
+        nc.sync.dma_start(out_1[0].rearrange("p q t -> p (q t)").bitcast(I32), y_words[:])
 
-        for quad in range(P // QUAD):
-            queue = nc.sync if quad % 2 == 0 else nc.scalar
-            queue.dma_start(
-                out_2[0, QUAD_ROWS * quad : QUAD_ROWS * (quad + 1), :].bitcast(I32),
-                y_scales[QUAD * quad : QUAD * quad + QUAD_ROWS, :].bitcast(I32),
-            )
+        for r in range(QUAD_ROWS):
+            queue = nc.sync if r % 2 == 0 else nc.scalar
+            queue.dma_start(out_2[0, r : P // SPREAD : QUAD_ROWS, :].bitcast(I32), y_scales[r:P:QUAD, :].bitcast(I32))

@@ -194,7 +194,8 @@ def tile_attend_plw_residsig_topk_kernel(tc, qT, k_words, k_scales, c_words, c_s
         y_scales = tile([P, NQ], U8, "y_scales")
         y_words = tile([P, NQ], I32, "y_words")
         y_by_query = [tile([P, PACK, P], F32, f"y_by_query{j}") for j in range(BLOCKS)]
-        y = [tile([P, PACK, P], F32, f"y{j}") for j in range(BLOCKS)]
+        y_front = tile([P, PACK, 2 * P], F32, "y_front")
+        y = [y_front[:, :, 0:P], y_front[:, :, P : 2 * P]] + [tile([P, PACK, P], F32, f"y{j}")[:] for j in (2, 3)]
         y_bf = [tile([P, P, PACK], BF16, f"y_bf{j}") for j in range(BLOCKS)]
         WHOLE, LOW, HIGH = slice(0, 2), slice(0, 1), slice(1, 2)
 
@@ -223,37 +224,41 @@ def tile_attend_plw_residsig_topk_kernel(tc, qT, k_words, k_scales, c_words, c_s
         def empty(j, halves, bank, engine_copy):
             engine_copy(y[j][:, places(halves), :], bank[:, places(halves), :])
 
-        def store(j, halves):
-            rows = out_0[:, j * P : (j + 1) * P].rearrange("(p u) q -> p u q", u=PACK)
-            nc.sync.dma_start(rows[:, places(halves), :], y[j][:, places(halves), :])
+        def store(first, src, halves):
+            rows = out_0[:, first * P : first * P + src.shape[2]].rearrange("(p u) q -> p u q", u=PACK)
+            nc.sync.dma_start(rows[:, places(halves), :], src[:, places(halves), :])
 
         def weave(j, engine_copy):
-            interleave(engine_copy, y_bf[j][:], y[j][:])
+            interleave(engine_copy, y_bf[j][:], y[j])
 
         def quantise_y(j):
             cols = slice(j * P, (j + 1) * P)
             nc.vector.quantize_mx(y_words[:, cols].bitcast(FP8X4), y_scales[:, cols], y_bf[j][:].rearrange("p q u -> p (q u)"))
 
         prepare_late(1)
-        for j in (0, 1, 2):
-            close(j)
-            weigh(j, WHOLE)
+        close(0)
+        close(1)
+        for half in (LOW, HIGH):
+            weigh(0, half)
+            weigh(1, half)
+        close(2)
+        weigh(2, WHOLE)
         for half in (LOW, HIGH):
             empty(0, half, turn(0, half), nc.vector.tensor_copy)
-            store(0, half)
-        empty(1, WHOLE, turn(1, WHOLE), nc.scalar.copy)
-        store(1, WHOLE)
+            empty(1, half, turn(1, half), nc.vector.tensor_copy if half is LOW else nc.scalar.copy)
+            store(0, y_front[:], half)
         close(3)
         weave(0, nc.vector.tensor_copy)
         weave(1, nc.vector.tensor_copy)
-        empty(2, WHOLE, turn(2, WHOLE), nc.vector.tensor_copy)
-        store(2, WHOLE)
+        for half in (LOW, HIGH):
+            empty(2, half, turn(2, half), nc.vector.tensor_copy)
+            store(2, y[2], half)
         weigh(3, LOW)
         weigh(3, HIGH)
         quantise_y(0)
         empty(3, LOW, turn(3, LOW), nc.scalar.copy)
         empty(3, HIGH, turn(3, HIGH), nc.vector.tensor_copy)
-        store(3, WHOLE)
+        store(3, y[3], WHOLE)
         weave(2, nc.scalar.copy)
         quantise_y(1)
         weave(3, nc.vector.tensor_copy)
@@ -262,5 +267,4 @@ def tile_attend_plw_residsig_topk_kernel(tc, qT, k_words, k_scales, c_words, c_s
         nc.sync.dma_start(out_1[0].rearrange("p q t -> p (q t)").bitcast(I32), y_words[:])
 
         for r in range(QUAD_ROWS):
-            queue = nc.sync if r % 2 == 0 else nc.scalar
-            queue.dma_start(out_2[0, r : P // SPREAD : QUAD_ROWS, :].bitcast(I32), y_scales[r:P:QUAD, :].bitcast(I32))
+            nc.scalar.dma_start(out_2[0, r : P // SPREAD : QUAD_ROWS, :].bitcast(I32), y_scales[r:P:QUAD, :].bitcast(I32))

@@ -196,7 +196,7 @@ def tile_attend_plw_residsig_topk_kernel(tc, qT, k_words, k_scales, c_words, c_s
         y_by_query = [tile([P, PACK, P], F32, f"y_by_query{j}") for j in range(BLOCKS)]
         y_front = tile([P, PACK, 2 * P], F32, "y_front")
         y = [y_front[:, :, 0:P], y_front[:, :, P : 2 * P]] + [tile([P, PACK, P], F32, f"y{j}")[:] for j in (2, 3)]
-        y_bf = [tile([P, P, PACK], BF16, f"y_bf{j}") for j in range(BLOCKS)]
+        y_bf = {}
         WHOLE, LOW, HIGH = slice(0, 2), slice(0, 1), slice(1, 2)
 
         def places(halves):
@@ -228,11 +228,12 @@ def tile_attend_plw_residsig_topk_kernel(tc, qT, k_words, k_scales, c_words, c_s
             rows = out_0[:, first * P : first * P + src.shape[2]].rearrange("(p u) q -> p u q", u=PACK)
             nc.sync.dma_start(rows[:, places(halves), :], src[:, places(halves), :])
 
-        def weave(j, engine_copy):
-            interleave(engine_copy, y_bf[j][:], y[j])
+        def weave(j, src, engine_copy):
+            y_bf[j] = tile([P, src.shape[2], PACK], BF16, f"y_bf{j}")
+            interleave(engine_copy, y_bf[j][:], src)
 
         def quantise_y(j):
-            cols = slice(j * P, (j + 1) * P)
+            cols = slice(j * P, j * P + y_bf[j].shape[1])
             nc.vector.quantize_mx(y_words[:, cols].bitcast(FP8X4), y_scales[:, cols], y_bf[j][:].rearrange("p q u -> p (q u)"))
 
         prepare_late(1)
@@ -248,23 +249,23 @@ def tile_attend_plw_residsig_topk_kernel(tc, qT, k_words, k_scales, c_words, c_s
             empty(1, half, turn(1, half), nc.vector.tensor_copy if half is LOW else nc.scalar.copy)
             store(0, y_front[:], half)
         close(3)
-        weave(0, nc.vector.tensor_copy)
-        weave(1, nc.vector.tensor_copy)
-        for half in (LOW, HIGH):
-            empty(2, half, turn(2, half), nc.vector.tensor_copy)
-            store(2, y[2], half)
+        weave(0, y_front[:], nc.vector.tensor_copy)
+        empty(2, WHOLE, turn(2, WHOLE), nc.vector.tensor_copy)
+        store(2, y[2], WHOLE)
         weigh(3, LOW)
         weigh(3, HIGH)
-        quantise_y(0)
         empty(3, LOW, turn(3, LOW), nc.scalar.copy)
         empty(3, HIGH, turn(3, HIGH), nc.vector.tensor_copy)
         store(3, y[3], WHOLE)
-        weave(2, nc.scalar.copy)
-        quantise_y(1)
-        weave(3, nc.vector.tensor_copy)
+        weave(2, y[2], nc.scalar.copy)
+        quantise_y(0)
+        weave(3, y[3], nc.vector.tensor_copy)
+        words_out = out_1[0].rearrange("p q t -> p (q t)").bitcast(I32)
         quantise_y(2)
+        nc.sync.dma_start(words_out[:, 0 : 3 * P], y_words[:, 0 : 3 * P])
         quantise_y(3)
-        nc.sync.dma_start(out_1[0].rearrange("p q t -> p (q t)").bitcast(I32), y_words[:])
+        nc.sync.dma_start(words_out[:, 3 * P : NQ], y_words[:, 3 * P : NQ])
 
         for r in range(QUAD_ROWS):
-            nc.scalar.dma_start(out_2[0, r : P // SPREAD : QUAD_ROWS, :].bitcast(I32), y_scales[r:P:QUAD, :].bitcast(I32))
+            queue = nc.scalar if r % 2 == 0 else nc.sync
+            queue.dma_start(out_2[0, r : P // SPREAD : QUAD_ROWS, :].bitcast(I32), y_scales[r:P:QUAD, :].bitcast(I32))

@@ -252,17 +252,20 @@ def tile_attend_plw_residsig_topk_kernel(tc, qT, k_words, k_scales, c_words, c_s
         weave(0, y_front[:], nc.vector.tensor_copy)
         empty(2, WHOLE, turn(2, WHOLE), nc.vector.tensor_copy)
         store(2, y[2], WHOLE)
-        weigh(3, LOW)
-        weigh(3, HIGH)
-        empty(3, LOW, turn(3, LOW), nc.scalar.copy)
-        empty(3, HIGH, turn(3, HIGH), nc.vector.tensor_copy)
-        store(3, y[3], WHOLE)
-        weave(2, y[2], nc.scalar.copy)
         quantise_y(0)
-        weave(3, y[3], nc.vector.tensor_copy)
+        weave(2, y[2], nc.vector.tensor_copy)
         words_out = out_1[0].rearrange("p q t -> p (q t)").bitcast(I32)
         quantise_y(2)
         nc.sync.dma_start(words_out[:, 0 : 3 * P], y_words[:, 0 : 3 * P])
+        weigh(3, LOW)
+        weigh(3, HIGH)
+        for_planes = turn_bank("turned3_planes")
+        for half in (LOW, HIGH):
+            for u in range(PACK)[places(half)]:
+                nc.tensor.transpose(for_planes[:, u, :], y_by_query[3][:, u, :], ident[:])
+            empty(3, half, turn(3, half), nc.scalar.copy)
+        store(3, y[3], WHOLE)
+        weave(3, for_planes[:], nc.vector.tensor_copy)
         quantise_y(3)
         nc.sync.dma_start(words_out[:, 3 * P : NQ], y_words[:, 3 * P : NQ])
 

@@ -15,7 +15,7 @@ U8 = mybir.dt.uint8
 FP8X4 = mybir.dt.float8_e4m3fn_x4
 FP4X4 = mybir.dt.float4_e2m1fn_x4
 SIGMOID = mybir.ActivationFunctionType.Sigmoid
-COPY = mybir.ActivationFunctionType.Copy
+SUBTRACT = mybir.AluOpType.subtract
 
 P = 128
 PACK = 4
@@ -24,12 +24,10 @@ PASSES = D // K_PASS
 BLOCKS = NQ // P
 QUAD = 32
 QUAD_ROWS = 4
-SPREAD = P // (QUAD_ROWS * P // QUAD)
-C_FIRST = QUAD_ROWS
+ROWS = 16
+LINE = 16
 ALIGN = 64
-
-
-FRONT_0, BACK_0, FRONT_1, BLOCK2_1, BLOCK3_1 = (0, 0, 2 * P), (0, 2 * P, 2 * P), (1, 0, 2 * P), (1, 2 * P, P), (1, 3 * P, P)
+FRONT = 2 * P
 
 
 def interleave(engine_copy, dst, src):
@@ -43,17 +41,12 @@ def tile_attend_plw_residsig_topk_kernel(tc, qT, k_words, k_scales, c_words, c_s
     nc = tc.nc
     with ExitStack() as ctx:
         sbuf = ctx.enter_context(tc.tile_pool(name="sbuf", bufs=1))
-        shared = ctx.enter_context(tc.tile_pool(name="shared", bufs=1))
         psum = ctx.enter_context(tc.psum_pool(name="psum", bufs=1))
 
         def tile(shape, dtype, name, buffer=None):
             return sbuf.tile(shape, dtype, name=name, tag=buffer or name, align_bytes=ALIGN)
 
-        def shared_tile(shape, dtype, name, offset):
-            return shared.tile(shape, dtype, name=name, offset=offset, align_bytes=ALIGN)
-
-        def load_q(piece, dst):
-            o, first, width = piece
+        def load_q(o, first, width, dst):
             rows = qT[0, o * K_PASS : (o + 1) * K_PASS, first : first + width]
             nc.sync.dma_start(dst, rows.rearrange("(p t) w -> p t w", t=PACK))
 
@@ -61,214 +54,184 @@ def tile_attend_plw_residsig_topk_kernel(tc, qT, k_words, k_scales, c_words, c_s
             nc.sync.dma_start(pool[:], words.rearrange("p t b -> p (t b)").bitcast(I32))
             return pool
 
-        TH_AT, KS_AT = 2048, 12288
-        ks_pool = shared_tile([P, T], U8, "ks_pool", KS_AT)
-        nc.sync.dma_start(ks_pool[0:QUAD, :].bitcast(I32), k_scales.rearrange("o f t -> (o f) t").bitcast(I32))
+        KS_AT, CS_AT = 0, 2 * QUAD
+        ks_pool = tile([P, T], U8, "ks_pool")
+        nc.sync.dma_start(ks_pool[KS_AT : KS_AT + QUAD, :].bitcast(I32), k_scales.rearrange("o f t -> f o t").bitcast(I32))
         offsets = sbuf.tile([P, N // 16], U16, name="offsets")
         nc.sync.dma_start(offsets[:], offs)
-        q_front1 = tile([P, PACK, 2 * P], F32, "q_front1")
-        load_q(FRONT_1, q_front1[:])
-        th_rows = shared_tile([P, P], F32, "th_rows", TH_AT)
-        cs_pool = [tile([P, T], U8, f"cs_pool{o}") for o in range(PASSES)]
+        cs_pool = tile([P, T], U8, "cs_pool")
+        nc.sync.dma_start(cs_pool[CS_AT : CS_AT + QUAD, :].bitcast(I32), c_scales.rearrange("o f t -> f o t").bitcast(I32))
+        q_front1 = tile([P, PACK, FRONT], F32, "q_front1")
+        load_q(1, 0, FRONT, q_front1[:])
+        th_rows = tile([P, P], F32, "th_rows")
         nc.gpsimd.memset(th_rows[:], 0.0)
         nc.sync.dma_start(th_rows[0:BLOCKS, :], th[0, 0].rearrange("(j p) -> j p", p=P))
-        nc.gpsimd.memset(cs_pool[0][:].bitcast(I32), 0)
-        nc.vector.memset(cs_pool[1][:].bitcast(I32), 0)
         nc.gpsimd.memset(ks_pool[QUAD : 2 * QUAD, :].bitcast(I32), 0)
         nc.vector.memset(ks_pool[2 * QUAD : P, :].bitcast(I32), 0)
+        nc.vector.memset(cs_pool[0 : 2 * QUAD, :].bitcast(I32), 0)
+        nc.gpsimd.memset(cs_pool[3 * QUAD : P, :].bitcast(I32), 0)
         ident = tile([P, P], F32, "ident")
         nc.vector.memset(ident[:], 0.0)
         make_identity(nc, ident[:], nomemset=True)
-        ks = [tile([P, N], U8, f"ks{o}") for o in range(PASSES)]
-        for plane in ks:
-            nc.vector.memset(plane[:].bitcast(I32), 0)
+        ks = tile([P, PASSES * N], U8, "ks")
         cs = tile([P, PASSES * N], U8, "cs")
-        nc.gpsimd.memset(cs[:].bitcast(I32), 0)
+        for planes in (ks, cs):
+            nc.gpsimd.memset(planes[:].bitcast(I32), 0)
 
-        for o in range(PASSES):
-            nc.sync.dma_start(cs_pool[o][C_FIRST:P:SPREAD, :].bitcast(I32), c_scales[o].bitcast(I32))
         kw_pool = load_words(tile([P, T], I32, "kw_pool"), k_words[0])
         q_pass0 = tile([P, PACK, NQ], F32, "q_pass0")
-        load_q((0, 0, NQ), q_pass0[:])
+        load_q(0, 0, NQ, q_pass0[:])
 
         def gather(dst, window):
             nc.vector.tensor_copy(dst, window.indirect(offsets[:]))
 
-        def move_scales(o, dst):
-            rows = P // SPREAD
-            for r in range(QUAD_ROWS):
-                nc.sync.dma_start(dst[r:P:QUAD, :].bitcast(I32), ks_rows[o * rows + r : (o + 1) * rows : QUAD_ROWS, :].bitcast(I32))
+        def gather_dealt(dst, pool):
+            gather(dst[:].rearrange("p (u s) -> p s u", u=PACK), pool[:].bitcast(U32))
+
+        def gather_scales(pool, name):
+            rows = tile([P, N], U8, name + "_rows")
+            gather(rows[:], pool[:])
+            dealt = tile([P, N], U8, name + "_dealt")
+            nc.vector.tensor_copy(
+                dealt[:].rearrange("p (u g i) -> p g u i", u=PACK, i=LINE),
+                rows[:].rearrange("p (g i u) -> p g u i", u=PACK, i=LINE),
+            )
+            return dealt
+
+        def move_scales(dst, src, first):
+            rows = PASSES * QUAD_ROWS
+            for quad in range(P // QUAD):
+                nc.sync.dma_start(
+                    dst[quad * QUAD : quad * QUAD + QUAD_ROWS, :].bitcast(I32),
+                    src[first + quad * rows : first + (quad + 1) * rows, :].bitcast(I32),
+                )
+
+        def rounded(name, engine_copy, raw, buffer=None):
+            dst = tile([P, raw.shape[2], PACK], BF16, name, buffer)
+            interleave(engine_copy, dst[:], raw)
             return dst
 
-        q_bf, q_codes, q_scales = {}, {}, {}
+        def quantised(name, q_bf, buffer=None):
+            width = q_bf.shape[1]
+            codes = tile([P, width], U32, name + "_codes", buffer)
+            scales = tile([P, width], U8, name + "_scales")
+            nc.vector.quantize_mx(codes[:].bitcast(FP8X4), scales[:], q_bf[:].rearrange("p c t -> p (c t)"))
+            return codes, scales
 
-        def round_q(piece, engine_copy, dst, raw):
-            q_bf[piece] = dst
-            interleave(engine_copy, dst, raw)
+        front = [psum.tile([P, FRONT], F32, name=f"front{u}") for u in range(PACK)]
+        back = [psum.tile([P, PACK, P], F32, name=f"back{j}") for j in range(2)]
 
-        def quantise_q(piece):
-            o, first, width = piece
-            q_codes[piece] = tile([P, width], U32, f"q_codes{o}_{first}")
-            q_scales[piece] = tile([P, width], U8, f"q_scales{o}_{first}")
-            nc.vector.quantize_mx(
-                q_codes[piece][:].bitcast(FP8X4), q_scales[piece][:], q_bf[piece].rearrange("p c t -> p (c t)")
-            )
+        def product(out, keys, key_scales, q, cols, start=False, stop=False):
+            nc.tensor.matmul_mx(out, keys, key_scales, q[0][:, cols].bitcast(FP8X4), q[1][:, cols], start=start, stop=stop)
 
-        sums = [psum.tile([P, N], F32, name=f"sum{j}") for j in range(BLOCKS)]
+        def coarse(out, o, u, q, cols, start=False):
+            product(out, kw[:, o, u * P : (u + 1) * P].bitcast(FP4X4), ks[:, o * N + u * P : o * N + (u + 1) * P], q, cols, start=start)
 
-        def product(j, piece, keys, key_scales, start, stop):
-            cols = slice(j * P - piece[1], (j + 1) * P - piece[1])
-            nc.tensor.matmul_mx(
-                sums[j][:], q_codes[piece][:, cols].bitcast(FP8X4), q_scales[piece][:, cols], keys, key_scales, start=start, stop=stop
-            )
+        def fine(out, o, u, q, cols, stop=False):
+            product(out, cw[o][:, u * P : (u + 1) * P].bitcast(FP8X4), cs[:, o * N + u * P : o * N + (u + 1) * P], q, cols, stop=stop)
 
-        def coarse(j, piece):
-            o = piece[0]
-            product(j, piece, kw[:, o * N : (o + 1) * N].bitcast(FP4X4), ks[o][:], o == 0, False)
+        def block(j):
+            return slice(j * P, (j + 1) * P)
 
-        def fine(j, piece):
-            o = piece[0]
-            product(j, piece, cw[o][:].bitcast(FP8X4), cs[C_FIRST:P, o * N : (o + 1) * N], False, o == PASSES - 1)
+        th_turned = psum.tile([P, P], F32, name="th_turned")
+        nc.tensor.transpose(th_turned[:], th_rows[:], ident[:])
+        th_cols = tile([P, BLOCKS], F32, "th_cols")
+        nc.scalar.copy(th_cols[:], th_turned[:, 0:BLOCKS])
+        th_spread = psum.tile([P, NQ], F32, name="th_spread")
+        for j in range(BLOCKS):
+            nc.tensor.transpose(th_spread[:, block(j)], th_cols[:, j : j + 1].to_broadcast([P, P]), ident[:])
+        bf_front1 = rounded("bf_front1", nc.scalar.copy, q_front1[:])
+        th_all = tile([P, NQ], F32, "th_all")
+        nc.scalar.copy(th_all[:], th_spread[:])
 
-        def turn_bank(name):
-            return psum.tile([P, PACK, P], F32, name=name, tag="turned", bufs=BLOCKS)
+        ks_dealt = gather_scales(ks_pool, "ks")
+        move_scales(ks, ks_dealt, KS_AT)
+        cw_pool0 = load_words(tile([P, T], I32, "cw_pool0", "ks_pool"), c_words[0])
+        cs_dealt = gather_scales(cs_pool, "cs")
+        move_scales(cs, cs_dealt, CS_AT)
+        cw_pool1 = load_words(tile([P, T], I32, "cw_pool1", "cs_pool"), c_words[1])
+        q1_front = quantised("q1_front", bf_front1)
 
-        th_turned = turn_bank("th_turned")
-        nc.tensor.transpose(th_turned[:, 0, :], th_rows[:], ident[:])
-        neg_th = tile([P, BLOCKS], F32, "neg_th")
-        nc.scalar.activation(neg_th[:], th_turned[:, 0, 0:BLOCKS], COPY, scale=-1.0)
-        round_q(FRONT_1, nc.scalar.copy, shared_tile([P, 2 * P, PACK], BF16, "q_bf_front1", TH_AT + 256 - 2048)[:], q_front1[:])
-        ks_rows = tile([P, N], U8, "ks_rows")
-        gather(ks_rows[:], ks_pool[:])
-        move_scales(0, ks[0])
-        cw_pool0 = load_words(shared_tile([P, T], I32, "cw_pool0", KS_AT + 512 - 8192), c_words[0])
-        cs_rows = shared_tile([P, PASSES * N], U8, "cs_rows", KS_AT + 512)
-        for o in range(PASSES):
-            gather(cs_rows[:, o * N : (o + 1) * N], cs_pool[o][:])
-        for r in range(QUAD_ROWS):
-            nc.sync.dma_start(cs[C_FIRST + r : P : QUAD, :].bitcast(I32), cs_rows[C_FIRST + SPREAD * r : P : QUAD, :].bitcast(I32))
-        cw_pool1 = load_words(tile([P, T], I32, "cw_pool1", "cs_pool1"), c_words[1])
-        move_scales(1, ks[1])
-        quantise_q(FRONT_1)
-
-        kw_pair = tile([P, N], U32, "kw_pair", "cs_pool0")
-        gather(kw_pair[:], kw_pool[:].bitcast(U32))
-        late = (BLOCK2_1, BLOCK3_1)
+        kw_pair = tile([P, N], U32, "kw_pair", "cs_rows")
+        gather_dealt(kw_pair, kw_pool)
         q_late_both = tile([P, 2 * PACK * P], F32, "q_late", "kw_pool")
-        q_late = [q_late_both[:, place * PACK * P : (place + 1) * PACK * P].rearrange("p (t w) -> p t w", t=PACK) for place in range(2)]
-        for place, piece in enumerate(late):
-            load_q(piece, q_late[place])
-        kw = tile([P, PASSES * N], U16, "kw")
-        nc.vector.tensor_copy(
-            kw[:].rearrange("p (o s) -> p o s", o=PASSES),
-            kw_pair[:].bitcast(U16).rearrange("p (s o) -> p o s", o=PASSES),
-        )
-        round_q(FRONT_0, nc.scalar.copy, tile([P, 2 * P, PACK], BF16, "q_bf_front0")[:], q_pass0[:, :, 0 : 2 * P])
-        round_q(BACK_0, nc.vector.tensor_copy, tile([P, 2 * P, PACK], BF16, "q_bf_back0", "cs_pool0")[:], q_pass0[:, :, 2 * P : NQ])
-        quantise_q(BACK_0)
-        for j in (2, 3):
-            coarse(j, BACK_0)
-        quantise_q(FRONT_0)
-        for j in (0, 1):
-            coarse(j, FRONT_0)
-        cw = [tile([P, N], U32, "cw0", "q_bf_front0")]
-        gather(cw[0][:], cw_pool0[:].bitcast(U32))
-        for j in (2, 3):
-            fine(j, BACK_0)
-        for j in (0, 1):
-            fine(j, FRONT_0)
-            coarse(j, FRONT_1)
-        cw.append(shared_tile([P, N], U32, "cw1", KS_AT + 512 - 8192))
-        gather(cw[1][:], cw_pool1[:].bitcast(U32))
-
-        q_bf_late = tile([P, 2 * P * PACK], BF16, "q_bf_late", "cs_pool1")
-
-        def prepare_late(place):
-            dst = q_bf_late[:, place * P * PACK : (place + 1) * P * PACK].rearrange("p (c t) -> p c t", t=PACK)
-            round_q(late[place], nc.vector.tensor_copy, dst, q_late[place])
-            quantise_q(late[place])
-
-        prepare_late(0)
-        pass1 = [FRONT_1, FRONT_1, BLOCK2_1, BLOCK3_1]
+        q_late = [q_late_both[:, j * PACK * P : (j + 1) * PACK * P].rearrange("p (t w) -> p t w", t=PACK) for j in range(2)]
+        for j in range(2):
+            load_q(1, FRONT + j * P, P, q_late[j])
+        kw = tile([P, PASSES, N], U16, "kw")
+        nc.vector.tensor_copy(kw[:], kw_pair[:].bitcast(U16).rearrange("p (s o) -> p o s", o=PASSES))
+        bf_front0 = rounded("bf_front0", nc.scalar.copy, q_pass0[:, :, 0:FRONT])
+        bf_back0 = rounded("bf_back0", nc.scalar.copy, q_pass0[:, :, FRONT:NQ])
+        q0_front = quantised("q0_front", bf_front0)
+        for u in range(PACK):
+            for j in range(2):
+                coarse(front[u][:, block(j)], 0, u, q0_front, block(j), start=j == 0)
+        cw = [tile([P, N], U32, "cw0", "bf_front0")]
+        gather_dealt(cw[0], cw_pool0)
+        q0_back = quantised("q0_back", bf_back0, "ks_pool")
+        for u in range(PACK):
+            for j in range(2):
+                coarse(front[u][:, block(j)], 1, u, q1_front, block(j))
+        for u in range(PACK):
+            fine(front[u][:], 0, u, q0_front, slice(0, FRONT))
+        for j in range(2):
+            for u in range(PACK):
+                coarse(back[j][:, u, :], 0, u, q0_back, block(j), start=u == 0)
+                fine(back[j][:, u, :], 0, u, q0_back, block(j))
+        cw.append(tile([P, N], U32, "cw1", "bf_back0"))
+        gather_dealt(cw[1], cw_pool1)
+        for u in range(PACK):
+            fine(front[u][:], 1, u, q1_front, slice(0, FRONT), stop=True)
 
         y_scales = tile([P, NQ], U8, "y_scales")
         y_words = tile([P, NQ], I32, "y_words")
-        y_by_query = [tile([P, PACK, P], F32, f"y_by_query{j}") for j in range(BLOCKS)]
-        y_front = tile([P, PACK, 2 * P], F32, "y_front")
-        y = [y_front[:, :, 0:P], y_front[:, :, P : 2 * P]] + [tile([P, PACK, P], F32, f"y{j}")[:] for j in (2, 3)]
-        y_bf = {}
-        WHOLE, LOW, HIGH = slice(0, 2), slice(0, 1), slice(1, 2)
-
-        def places(halves):
-            return slice(2 * halves.start, 2 * halves.stop)
-
-        def close(j):
-            if pass1[j] in late:
-                coarse(j, pass1[j])
-            fine(j, pass1[j])
-
-        def weigh(j, halves):
-            nc.scalar.activation(
-                y_by_query[j][:].rearrange("q (h e) p -> q h p e", e=2)[:, halves],
-                sums[j][:].rearrange("q (p h e) -> q h p e", h=2, e=2)[:, halves],
-                SIGMOID,
-                bias=neg_th[:, j : j + 1],
-            )
-
-        def turn(j, halves):
-            bank = turn_bank(f"turned{j}_{halves.start}")
-            for u in range(PACK)[places(halves)]:
-                nc.tensor.transpose(bank[:, u, :], y_by_query[j][:, u, :], ident[:])
-            return bank
-
-        def empty(j, halves, bank, engine_copy):
-            engine_copy(y[j][:, places(halves), :], bank[:, places(halves), :])
-
-        def store(first, src, halves):
-            rows = out_0[:, first * P : first * P + src.shape[2]].rearrange("(p u) q -> p u q", u=PACK)
-            nc.sync.dma_start(rows[:, places(halves), :], src[:, places(halves), :])
-
-        def weave(j, src, engine_copy):
-            y_bf[j] = tile([P, src.shape[2], PACK], BF16, f"y_bf{j}")
-            interleave(engine_copy, y_bf[j][:], src)
-
-        def quantise_y(j):
-            cols = slice(j * P, j * P + y_bf[j].shape[1])
-            nc.vector.quantize_mx(y_words[:, cols].bitcast(FP8X4), y_scales[:, cols], y_bf[j][:].rearrange("p q u -> p (q u)"))
-
-        prepare_late(1)
-        close(0)
-        close(1)
-        for half in (LOW, HIGH):
-            weigh(0, half)
-            weigh(1, half)
-        close(2)
-        weigh(2, WHOLE)
-        for half in (LOW, HIGH):
-            empty(0, half, turn(0, half), nc.vector.tensor_copy)
-            empty(1, half, turn(1, half), nc.vector.tensor_copy if half is LOW else nc.scalar.copy)
-            store(0, y_front[:], half)
-        close(3)
-        weave(0, y_front[:], nc.vector.tensor_copy)
-        empty(2, WHOLE, turn(2, WHOLE), nc.vector.tensor_copy)
-        store(2, y[2], WHOLE)
-        quantise_y(0)
-        weave(2, y[2], nc.vector.tensor_copy)
+        z_front = tile([P, PACK, FRONT], F32, "z_front")
+        y_front = tile([P, PACK, FRONT], F32, "y_front")
+        rows_out = out_0.rearrange("(p u) q -> p u q", u=PACK)
         words_out = out_1[0].rearrange("p q t -> p (q t)").bitcast(I32)
-        quantise_y(2)
-        nc.sync.dma_start(words_out[:, 0 : 3 * P], y_words[:, 0 : 3 * P])
-        weigh(3, LOW)
-        weigh(3, HIGH)
-        for_planes = turn_bank("turned3_planes")
-        for half in (LOW, HIGH):
-            for u in range(PACK)[places(half)]:
-                nc.tensor.transpose(for_planes[:, u, :], y_by_query[3][:, u, :], ident[:])
-            empty(3, half, turn(3, half), nc.scalar.copy)
-        store(3, y[3], WHOLE)
-        weave(3, for_planes[:], nc.vector.tensor_copy)
-        quantise_y(3)
-        nc.sync.dma_start(words_out[:, 3 * P : NQ], y_words[:, 3 * P : NQ])
 
+        def weigh_front(u):
+            nc.vector.tensor_tensor(z_front[:, u, :], front[u][:], th_all[:, 0:FRONT], SUBTRACT)
+            nc.scalar.activation(y_front[:, u, :], z_front[:, u, :], SIGMOID)
+
+        def close_back(j, q):
+            for u in range(PACK):
+                coarse(back[j][:, u, :], 1, u, q, block(0))
+                fine(back[j][:, u, :], 1, u, q, block(0), stop=u == PACK - 1)
+
+        def weigh_back(j):
+            z = tile([P, PACK, P], F32, f"z_back{j}")
+            th_block = th_all[:, block(2 + j)].unsqueeze(1).to_broadcast([P, PACK, P])
+            nc.vector.tensor_tensor(z[:], back[j][:], th_block, SUBTRACT)
+            y = tile([P, PACK, P], F32, f"y_back{j}")
+            nc.scalar.activation(y[:], z[:], SIGMOID)
+            nc.sync.dma_start(rows_out[:, :, block(2 + j)], y[:])
+            return y
+
+        def quantise_y(first, y_bf):
+            cols = slice(first, first + y_bf.shape[1])
+            nc.vector.quantize_mx(y_words[:, cols].bitcast(FP8X4), y_scales[:, cols], y_bf[:].rearrange("p q u -> p (q u)"))
+
+        bf_late = [rounded("bf_late0", nc.vector.tensor_copy, q_late[0], "cs_pool")]
+        weigh_front(0)
+        close_back(0, quantised("q1_late0", bf_late[0]))
+        bf_late.append(rounded("bf_late1", nc.vector.tensor_copy, q_late[1]))
+        weigh_front(1)
+        nc.sync.dma_start(rows_out[:, 0:2, 0:FRONT], y_front[:, 0:2, :])
+        close_back(1, quantised("q1_late1", bf_late[1]))
+        weigh_front(2)
+        weigh_front(3)
+        nc.sync.dma_start(rows_out[:, 2:4, 0:FRONT], y_front[:, 2:4, :])
+        y2 = weigh_back(0)
+        y3 = weigh_back(1)
+        y_bf_front = rounded("y_bf_front", nc.vector.tensor_copy, y_front[:])
+        y_bf2 = rounded("y_bf2", nc.vector.tensor_copy, y2[:])
+        quantise_y(0, y_bf_front)
+        y_bf3 = rounded("y_bf3", nc.vector.tensor_copy, y3[:])
+        quantise_y(FRONT, y_bf2)
+        nc.sync.dma_start(words_out[:, 0 : 3 * P], y_words[:, 0 : 3 * P])
+        quantise_y(3 * P, y_bf3)
+        nc.sync.dma_start(words_out[:, 3 * P : NQ], y_words[:, 3 * P : NQ])
         for r in range(QUAD_ROWS):
             queue = nc.scalar if r % 2 == 0 else nc.sync
-            queue.dma_start(out_2[0, r : P // SPREAD : QUAD_ROWS, :].bitcast(I32), y_scales[r:P:QUAD, :].bitcast(I32))
+            queue.dma_start(out_2[0, r:ROWS:QUAD_ROWS, :].bitcast(I32), y_scales[r:P:QUAD, :].bitcast(I32))

@@ -146,13 +146,13 @@ def tile_attend_plw_residsig_topk_kernel(tc, qT, k_words, k_scales, c_words, c_s
 
         ks_dealt = gather_scales(ks_pool, "ks")
         move_scales(ks, ks_dealt, KS_AT)
-        cw_pool0 = load_words(tile([P, T], I32, "cw_pool0", "ks_pool"), c_words[0])
+        cw_pool0 = load_words(tile([P, T], I32, "cw_pool0", "ks_rows"), c_words[0])
         cs_dealt = gather_scales(cs_pool, "cs")
         move_scales(cs, cs_dealt, CS_AT)
-        cw_pool1 = load_words(tile([P, T], I32, "cw_pool1", "cs_pool"), c_words[1])
+        cw_pool1 = load_words(tile([P, T], I32, "cw_pool1", "cs_rows"), c_words[1])
         q1_front = quantised("q1_front", bf_front1)
 
-        kw_pair = tile([P, N], U32, "kw_pair", "cs_rows")
+        kw_pair = tile([P, N], U32, "kw_pair", "cs_pool")
         gather_dealt(kw_pair, kw_pool)
         q_late_both = tile([P, 2 * PACK * P], F32, "q_late", "kw_pool")
         q_late = [q_late_both[:, j * PACK * P : (j + 1) * PACK * P].rearrange("p (t w) -> p t w", t=PACK) for j in range(2)]
@@ -160,24 +160,26 @@ def tile_attend_plw_residsig_topk_kernel(tc, qT, k_words, k_scales, c_words, c_s
             load_q(1, FRONT + j * P, P, q_late[j])
         kw = tile([P, PASSES, N], U16, "kw")
         nc.vector.tensor_copy(kw[:], kw_pair[:].bitcast(U16).rearrange("p (s o) -> p o s", o=PASSES))
+        for u in range(PACK):
+            for j in range(2):
+                coarse(front[u][:, block(j)], 1, u, q1_front, block(j), start=j == 0)
         bf_front0 = rounded("bf_front0", nc.scalar.copy, q_pass0[:, :, 0:FRONT])
-        bf_back0 = rounded("bf_back0", nc.scalar.copy, q_pass0[:, :, FRONT:NQ])
-        q0_front = quantised("q0_front", bf_front0)
-        for u in range(PACK):
-            for j in range(2):
-                coarse(front[u][:, block(j)], 0, u, q0_front, block(j), start=j == 0)
-        cw = [tile([P, N], U32, "cw0", "bf_front0")]
-        gather_dealt(cw[0], cw_pool0)
-        q0_back = quantised("q0_back", bf_back0, "ks_pool")
-        for u in range(PACK):
-            for j in range(2):
-                coarse(front[u][:, block(j)], 1, u, q1_front, block(j))
-        for u in range(PACK):
-            fine(front[u][:], 0, u, q0_front, slice(0, FRONT))
+        bf_back0 = rounded("bf_back0", nc.vector.tensor_copy, q_pass0[:, :, FRONT:NQ])
+        q0_back = quantised("q0_back", bf_back0)
         for j in range(2):
             for u in range(PACK):
                 coarse(back[j][:, u, :], 0, u, q0_back, block(j), start=u == 0)
+        q0_front = quantised("q0_front", bf_front0)
+        for u in range(PACK):
+            for j in range(2):
+                coarse(front[u][:, block(j)], 0, u, q0_front, block(j))
+        cw = [tile([P, N], U32, "cw0", "bf_front0")]
+        gather_dealt(cw[0], cw_pool0)
+        for j in range(2):
+            for u in range(PACK):
                 fine(back[j][:, u, :], 0, u, q0_back, block(j))
+        for u in range(PACK):
+            fine(front[u][:], 0, u, q0_front, slice(0, FRONT))
         cw.append(tile([P, N], U32, "cw1", "bf_back0"))
         gather_dealt(cw[1], cw_pool1)
         for u in range(PACK):
@@ -212,7 +214,7 @@ def tile_attend_plw_residsig_topk_kernel(tc, qT, k_words, k_scales, c_words, c_s
             cols = slice(first, first + y_bf.shape[1])
             nc.vector.quantize_mx(y_words[:, cols].bitcast(FP8X4), y_scales[:, cols], y_bf[:].rearrange("p q u -> p (q u)"))
 
-        bf_late = [rounded("bf_late0", nc.vector.tensor_copy, q_late[0], "cs_pool")]
+        bf_late = [rounded("bf_late0", nc.vector.tensor_copy, q_late[0], "cs_rows")]
         weigh_front(0)
         close_back(0, quantised("q1_late0", bf_late[0]))
         bf_late.append(rounded("bf_late1", nc.vector.tensor_copy, q_late[1]))

@@ -54,6 +54,9 @@ def tile_attend_plw_residsig_topk_kernel(tc, qT, k_words, k_scales, c_words, c_s
             nc.sync.dma_start(pool[:], words.rearrange("p t b -> p (t b)").bitcast(I32))
             return pool
 
+        warm = tile([P, 16], F32, "warm")
+        nc.vector.memset(warm[:, 0:1], 0.0)
+        nc.scalar.activation(warm[:, 8:9], warm[:, 0:1], SIGMOID)
         KS_AT, CS_AT = 0, 2 * QUAD
         ks_pool = tile([P, T], U8, "ks_pool")
         nc.sync.dma_start(ks_pool[KS_AT : KS_AT + QUAD, :].bitcast(I32), k_scales.rearrange("o f t -> f o t").bitcast(I32))
@@ -187,14 +190,15 @@ def tile_attend_plw_residsig_topk_kernel(tc, qT, k_words, k_scales, c_words, c_s
 
         y_scales = tile([P, NQ], U8, "y_scales")
         y_words = tile([P, NQ], I32, "y_words")
-        z_front = tile([P, PACK, FRONT], F32, "z_front")
-        y_front = tile([P, PACK, FRONT], F32, "y_front")
         rows_out = out_0.rearrange("(p u) q -> p u q", u=PACK)
         words_out = out_1[0].rearrange("p q t -> p (q t)").bitcast(I32)
 
         def weigh_front(u):
             nc.vector.tensor_tensor(z_front[:, u, :], front[u][:], th_all[:, 0:FRONT], SUBTRACT)
             nc.scalar.activation(y_front[:, u, :], z_front[:, u, :], SIGMOID)
+
+        def sigmoid(dst, src):
+            nc.scalar.activation(dst, src, SIGMOID)
 
         def close_back(j, q):
             for u in range(PACK):
@@ -208,28 +212,30 @@ def tile_attend_plw_residsig_topk_kernel(tc, qT, k_words, k_scales, c_words, c_s
             y = tile([P, PACK, P], F32, f"y_back{j}")
             nc.scalar.activation(y[:], z[:], SIGMOID)
             nc.sync.dma_start(rows_out[:, :, block(2 + j)], y[:])
-            return y
+            return y, z
 
         def quantise_y(first, y_bf):
             cols = slice(first, first + y_bf.shape[1])
             nc.vector.quantize_mx(y_words[:, cols].bitcast(FP8X4), y_scales[:, cols], y_bf[:].rearrange("p q u -> p (q u)"))
 
-        bf_late = [rounded("bf_late0", nc.vector.tensor_copy, q_late[0], "cs_rows")]
+        bf_late = [rounded(f"bf_late{j}", nc.scalar.copy, q_late[j]) for j in range(2)]
+        close_back(0, quantised("q1_late0", bf_late[0], "cs_rows"))
+        q_last = quantised("q1_late1", bf_late[1])
+        close_back(1, q_last)
+        z_front = tile([P, PACK, FRONT], F32, "z_front", "bf_late1")
+        y_front = tile([P, PACK, FRONT], F32, "y_front", "kw_pool")
         weigh_front(0)
-        close_back(0, quantised("q1_late0", bf_late[0]))
-        bf_late.append(rounded("bf_late1", nc.vector.tensor_copy, q_late[1]))
         weigh_front(1)
         nc.sync.dma_start(rows_out[:, 0:2, 0:FRONT], y_front[:, 0:2, :])
-        close_back(1, quantised("q1_late1", bf_late[1]))
         weigh_front(2)
         weigh_front(3)
         nc.sync.dma_start(rows_out[:, 2:4, 0:FRONT], y_front[:, 2:4, :])
-        y2 = weigh_back(0)
-        y3 = weigh_back(1)
+        y2, z2 = weigh_back(0)
+        y3, z3 = weigh_back(1)
+        y_bf3 = rounded("y_bf3", sigmoid, z3[:])
         y_bf_front = rounded("y_bf_front", nc.vector.tensor_copy, y_front[:])
         y_bf2 = rounded("y_bf2", nc.vector.tensor_copy, y2[:])
         quantise_y(0, y_bf_front)
-        y_bf3 = rounded("y_bf3", nc.vector.tensor_copy, y3[:])
         quantise_y(FRONT, y_bf2)
         nc.sync.dma_start(words_out[:, 0 : 3 * P], y_words[:, 0 : 3 * P])
         quantise_y(3 * P, y_bf3)

@@ -121,8 +121,6 @@ def tile_attend_plw_residsig_topk_kernel(tc, qT, k_words, k_scales, c_words, c_s
             nc.vector.quantize_mx(codes[:].bitcast(FP8X4), scales[:], q_bf[:].rearrange("p c t -> p (c t)"))
             return codes, scales
 
-        front = [psum.tile([P, FRONT], F32, name=f"front{u}") for u in range(PACK)]
-        back = [psum.tile([P, PACK, P], F32, name=f"back{j}") for j in range(2)]
 
         def product(out, keys, key_scales, q, cols, start=False, stop=False):
             nc.tensor.matmul_mx(out, keys, key_scales, q[0][:, cols].bitcast(FP8X4), q[1][:, cols], start=start, stop=stop)
@@ -136,16 +134,23 @@ def tile_attend_plw_residsig_topk_kernel(tc, qT, k_words, k_scales, c_words, c_s
         def block(j):
             return slice(j * P, (j + 1) * P)
 
-        th_turned = psum.tile([P, P], F32, name="th_turned")
+        th_turned = psum.tile([P, P], F32, name="th_turned", tag="back0")
         nc.tensor.transpose(th_turned[:], th_rows[:], ident[:])
         th_cols = tile([P, BLOCKS], F32, "th_cols")
         nc.scalar.copy(th_cols[:], th_turned[:, 0:BLOCKS])
-        th_spread = psum.tile([P, NQ], F32, name="th_spread")
+        th_spread = psum.tile([P, NQ], F32, name="th_spread", tag="back1")
         for j in range(BLOCKS):
             nc.tensor.transpose(th_spread[:, block(j)], th_cols[:, j : j + 1].to_broadcast([P, P]), ident[:])
         bf_front1 = rounded("bf_front1", nc.scalar.copy, q_front1[:])
         th_all = tile([P, NQ], F32, "th_all")
         nc.scalar.copy(th_all[:], th_spread[:])
+
+        front = [psum.tile([P, FRONT], F32, name=f"front{u}") for u in range(PACK)]
+        back = [psum.tile([P, FRONT], F32, name=f"back{u}") for u in range(PACK)]
+
+        def coarse_passes(bank, o, u, q, start=False):
+            for j in range(2):
+                coarse(bank[:, block(j)], o, u, q, block(j), start=start and j == 0)
 
         ks_dealt = gather_scales(ks_pool, "ks")
         move_scales(ks, ks_dealt, KS_AT)
@@ -163,83 +168,70 @@ def tile_attend_plw_residsig_topk_kernel(tc, qT, k_words, k_scales, c_words, c_s
             load_q(1, FRONT + j * P, P, q_late[j])
         kw = tile([P, PASSES, N], U16, "kw")
         nc.vector.tensor_copy(kw[:], kw_pair[:].bitcast(U16).rearrange("p (s o) -> p o s", o=PASSES))
+        whole = slice(0, FRONT)
         for u in range(PACK):
-            for j in range(2):
-                coarse(front[u][:, block(j)], 1, u, q1_front, block(j), start=j == 0)
+            coarse_passes(front[u], 1, u, q1_front, start=True)
         bf_front0 = rounded("bf_front0", nc.scalar.copy, q_pass0[:, :, 0:FRONT])
         bf_back0 = rounded("bf_back0", nc.vector.tensor_copy, q_pass0[:, :, FRONT:NQ])
         q0_back = quantised("q0_back", bf_back0)
-        for j in range(2):
-            for u in range(PACK):
-                coarse(back[j][:, u, :], 0, u, q0_back, block(j), start=u == 0)
+        for u in range(PACK):
+            coarse_passes(back[u], 0, u, q0_back, start=True)
         q0_front = quantised("q0_front", bf_front0)
         for u in range(PACK):
-            for j in range(2):
-                coarse(front[u][:, block(j)], 0, u, q0_front, block(j))
+            coarse_passes(front[u], 0, u, q0_front)
         cw = [tile([P, N], U32, "cw0", "bf_front0")]
         gather_dealt(cw[0], cw_pool0)
-        for j in range(2):
-            for u in range(PACK):
-                fine(back[j][:, u, :], 0, u, q0_back, block(j))
         for u in range(PACK):
-            fine(front[u][:], 0, u, q0_front, slice(0, FRONT))
+            fine(back[u][:], 0, u, q0_back, whole)
+        for u in range(PACK):
+            fine(front[u][:], 0, u, q0_front, whole)
         cw.append(tile([P, N], U32, "cw1", "bf_back0"))
         gather_dealt(cw[1], cw_pool1)
         for u in range(PACK):
-            fine(front[u][:], 1, u, q1_front, slice(0, FRONT), stop=True)
+            fine(front[u][:], 1, u, q1_front, whole, stop=True)
 
         y_scales = tile([P, NQ], U8, "y_scales")
         y_words = tile([P, NQ], I32, "y_words")
         rows_out = out_0.rearrange("(p u) q -> p u q", u=PACK)
         words_out = out_1[0].rearrange("p q t -> p (q t)").bitcast(I32)
-
-        def weigh_front(u):
-            nc.vector.tensor_tensor(z_front[:, u, :], front[u][:], th_all[:, 0:FRONT], SUBTRACT)
-            nc.scalar.activation(y_front[:, u, :], z_front[:, u, :], SIGMOID)
+        y_back = tile([P, PACK, FRONT], F32, "y_back")
+        z_back = tile([P, PACK, FRONT], F32, "z_back")
 
         def sigmoid(dst, src):
             nc.scalar.activation(dst, src, SIGMOID)
 
-        def close_back(j, q):
-            for u in range(PACK):
-                coarse(back[j][:, u, :], 1, u, q, block(0))
-                fine(back[j][:, u, :], 1, u, q, block(0), stop=u == PACK - 1)
+        def weigh(bank, cols, z, y, u, stored):
+            nc.vector.tensor_tensor(z[:, u, :], bank[:], th_all[:, cols], SUBTRACT)
+            sigmoid(y[:, u, :], z[:, u, :])
+            if (u + 1) % stored == 0:
+                nc.sync.dma_start(rows_out[:, u + 1 - stored : u + 1, cols], y[:, u + 1 - stored : u + 1, :])
 
-        def weigh_back(j):
-            z = tile([P, PACK, P], F32, f"z_back{j}")
-            th_block = th_all[:, block(2 + j)].unsqueeze(1).to_broadcast([P, PACK, P])
-            nc.vector.tensor_tensor(z[:], back[j][:], th_block, SUBTRACT)
-            y = tile([P, PACK, P], F32, f"y_back{j}")
-            nc.scalar.activation(y[:], z[:], SIGMOID)
-            nc.sync.dma_start(rows_out[:, :, block(2 + j)], y[:])
-            return y, z
-
-        def quantise_y(first, y_bf):
-            cols = slice(first, first + y_bf.shape[1])
+        def quantise_y(cols, y_bf):
             nc.vector.quantize_mx(y_words[:, cols].bitcast(FP8X4), y_scales[:, cols], y_bf[:].rearrange("p q u -> p (q u)"))
+            nc.sync.dma_start(words_out[:, cols], y_words[:, cols])
 
         bf_late = [rounded(f"bf_late{j}", nc.scalar.copy, q_late[j]) for j in range(2)]
-        close_back(0, quantised("q1_late0", bf_late[0], "cs_rows"))
-        q_last = quantised("q1_late1", bf_late[1])
-        close_back(1, q_last)
+        q1_back = tile([P, FRONT], U32, "q1_back_codes", "cs_rows"), tile([P, FRONT], U8, "q1_back_scales")
+        for j in range(2):
+            nc.vector.quantize_mx(
+                q1_back[0][:, block(j)].bitcast(FP8X4), q1_back[1][:, block(j)], bf_late[j][:].rearrange("p c t -> p (c t)")
+            )
+            for u in range(PACK):
+                coarse(back[u][:, block(j)], 1, u, q1_back, block(j))
+        for u in range(PACK):
+            fine(back[u][:], 1, u, q1_back, whole, stop=True)
         z_front = tile([P, PACK, FRONT], F32, "z_front", "bf_late1")
         y_front = tile([P, PACK, FRONT], F32, "y_front", "kw_pool")
-        weigh_front(0)
-        weigh_front(1)
-        nc.sync.dma_start(rows_out[:, 0:2, 0:FRONT], y_front[:, 0:2, :])
-        weigh_front(2)
-        weigh_front(3)
-        nc.sync.dma_start(rows_out[:, 2:4, 0:FRONT], y_front[:, 2:4, :])
-        y2, z2 = weigh_back(0)
-        y3, z3 = weigh_back(1)
-        y_bf3 = rounded("y_bf3", sigmoid, z3[:])
+        for u in range(PACK):
+            weigh(front[u], whole, z_front, y_front, u, 1)
+        for u in range(PACK):
+            weigh(back[u], slice(FRONT, NQ), z_back, y_back, u, 2)
         y_bf_front = rounded("y_bf_front", nc.vector.tensor_copy, y_front[:])
-        y_bf2 = rounded("y_bf2", nc.vector.tensor_copy, y2[:])
-        quantise_y(0, y_bf_front)
-        quantise_y(FRONT, y_bf2)
-        nc.sync.dma_start(words_out[:, 0 : 3 * P], y_words[:, 0 : 3 * P])
-        quantise_y(3 * P, y_bf3)
-        nc.sync.dma_start(words_out[:, 3 * P : NQ], y_words[:, 3 * P : NQ])
+        y_bf_back = tile([P, FRONT, PACK], BF16, "y_bf_back")
+        interleave(sigmoid, y_bf_back[:, block(1), :], z_back[:, :, block(1)])
+        interleave(nc.vector.tensor_copy, y_bf_back[:, block(0), :], y_back[:, :, block(0)])
+        quantise_y(whole, y_bf_front)
+        quantise_y(slice(FRONT, NQ), y_bf_back)
         for r in range(QUAD_ROWS):
             queue = nc.scalar if r % 2 == 0 else nc.sync
             queue.dma_start(out_2[0, r:ROWS:QUAD_ROWS, :].bitcast(I32), y_scales[r:P:QUAD, :].bitcast(I32))

@@ -220,8 +220,8 @@ def tile_attend_plw_residsig_topk_kernel(tc, qT, k_words, k_scales, c_words, c_s
                 coarse(back[u][:, block(j)], 1, u, q1_back, block(j))
         for u in range(PACK):
             fine(back[u][:], 1, u, q1_back, whole, stop=True)
-        z_front = tile([P, PACK, FRONT], F32, "z_front", "bf_late1")
-        y_front = tile([P, PACK, FRONT], F32, "y_front", "kw_pool")
+        z_front = tile([P, PACK, FRONT], F32, "z_front", "kw_pool")
+        y_front = tile([P, PACK, FRONT], F32, "y_front")
         for u in range(PACK):
             weigh(front[u], whole, z_front, y_front, u, 1)
         for u in range(PACK):

@@ -101,10 +101,10 @@ def tile_attend_plw_residsig_topk_kernel(tc, qT, k_words, k_scales, c_words, c_s
             )
             return dealt
 
-        def move_scales(dst, src, first):
+        def move_scales(dst, src, first, queues):
             rows = PASSES * QUAD_ROWS
-            for quad in range(P // QUAD):
-                nc.sync.dma_start(
+            for quad, queue in enumerate(queues):
+                queue.dma_start(
                     dst[quad * QUAD : quad * QUAD + QUAD_ROWS, :].bitcast(I32),
                     src[first + quad * rows : first + (quad + 1) * rows, :].bitcast(I32),
                 )
@@ -153,10 +153,10 @@ def tile_attend_plw_residsig_topk_kernel(tc, qT, k_words, k_scales, c_words, c_s
                 coarse(bank[:, block(j)], o, u, q, block(j), start=start and j == 0)
 
         ks_dealt = gather_scales(ks_pool, "ks")
-        move_scales(ks, ks_dealt, KS_AT)
+        move_scales(ks, ks_dealt, KS_AT, [nc.sync] * 4)
         cw_pool0 = load_words(tile([P, T], I32, "cw_pool0", "ks_rows"), c_words[0])
         cs_dealt = gather_scales(cs_pool, "cs")
-        move_scales(cs, cs_dealt, CS_AT)
+        move_scales(cs, cs_dealt, CS_AT, [nc.sync, nc.sync, nc.scalar, nc.scalar])
         cw_pool1 = load_words(tile([P, T], I32, "cw_pool1", "cs_rows"), c_words[1])
         q1_front = quantised("q1_front", bf_front1)
 

@@ -25,7 +25,7 @@ BLOCKS = NQ // P
 QUAD = 32
 QUAD_ROWS = 4
 ROWS = 16
-LINE = 16
+FINE_AT = 4
 ALIGN = 64
 FRONT = 2 * P
 
@@ -92,20 +92,15 @@ def tile_attend_plw_residsig_topk_kernel(tc, qT, k_words, k_scales, c_words, c_s
             gather(dst[:].rearrange("p (u s) -> p s u", u=PACK), pool[:].bitcast(U32))
 
         def gather_scales(pool, name):
-            rows = tile([P, N], U8, name + "_rows")
-            gather(rows[:], pool[:])
             dealt = tile([P, N], U8, name + "_dealt")
-            nc.vector.tensor_copy(
-                dealt[:].rearrange("p (u g i) -> p g u i", u=PACK, i=LINE),
-                rows[:].rearrange("p (g i u) -> p g u i", u=PACK, i=LINE),
-            )
+            gather(dealt[:].rearrange("p (u s) -> p s u", u=PACK), pool[:])
             return dealt
 
-        def move_scales(dst, src, first, queues):
+        def move_scales(dst, at, src, first, queues):
             rows = PASSES * QUAD_ROWS
-            for quad, queue in enumerate(queues):
+            for quad, queue in zip((0, 2, 1, 3), queues):
                 queue.dma_start(
-                    dst[quad * QUAD : quad * QUAD + QUAD_ROWS, :].bitcast(I32),
+                    dst[quad * QUAD + at : quad * QUAD + at + QUAD_ROWS, :].bitcast(I32),
                     src[first + quad * rows : first + (quad + 1) * rows, :].bitcast(I32),
                 )
 
@@ -129,7 +124,7 @@ def tile_attend_plw_residsig_topk_kernel(tc, qT, k_words, k_scales, c_words, c_s
             product(out, kw[:, o, u * P : (u + 1) * P].bitcast(FP4X4), ks[:, o * N + u * P : o * N + (u + 1) * P], q, cols, start=start)
 
         def fine(out, o, u, q, cols, stop=False):
-            product(out, cw[o][:, u * P : (u + 1) * P].bitcast(FP8X4), cs[:, o * N + u * P : o * N + (u + 1) * P], q, cols, stop=stop)
+            product(out, cw[o][:, u * P : (u + 1) * P].bitcast(FP8X4), cs[FINE_AT:P, o * N + u * P : o * N + (u + 1) * P], q, cols, stop=stop)
 
         def block(j):
             return slice(j * P, (j + 1) * P)
@@ -153,14 +148,14 @@ def tile_attend_plw_residsig_topk_kernel(tc, qT, k_words, k_scales, c_words, c_s
                 coarse(bank[:, block(j)], o, u, q, block(j), start=start and j == 0)
 
         ks_dealt = gather_scales(ks_pool, "ks")
-        move_scales(ks, ks_dealt, KS_AT, [nc.sync] * 4)
-        cw_pool0 = load_words(tile([P, T], I32, "cw_pool0", "ks_rows"), c_words[0])
+        move_scales(ks, 0, ks_dealt, KS_AT, [nc.sync] * 4)
+        cw_pool0 = load_words(tile([P, T], I32, "cw_pool0", "ks_pool"), c_words[0])
         cs_dealt = gather_scales(cs_pool, "cs")
-        move_scales(cs, cs_dealt, CS_AT, [nc.sync, nc.sync, nc.scalar, nc.scalar])
-        cw_pool1 = load_words(tile([P, T], I32, "cw_pool1", "cs_rows"), c_words[1])
+        move_scales(cs, FINE_AT, cs_dealt, CS_AT, [nc.sync, nc.sync, nc.scalar, nc.scalar])
+        cw_pool1 = load_words(tile([P, T], I32, "cw_pool1", "cs_pool"), c_words[1])
         q1_front = quantised("q1_front", bf_front1)
 
-        kw_pair = tile([P, N], U32, "kw_pair", "cs_pool")
+        kw_pair = tile([P, N], U32, "kw_pair")
         gather_dealt(kw_pair, kw_pool)
         q_late_both = tile([P, 2 * PACK * P], F32, "q_late", "kw_pool")
         q_late = [q_late_both[:, j * PACK * P : (j + 1) * PACK * P].rearrange("p (t w) -> p t w", t=PACK) for j in range(2)]
@@ -211,7 +206,7 @@ def tile_attend_plw_residsig_topk_kernel(tc, qT, k_words, k_scales, c_words, c_s
             nc.sync.dma_start(words_out[:, cols], y_words[:, cols])
 
         bf_late = [rounded(f"bf_late{j}", nc.scalar.copy, q_late[j]) for j in range(2)]
-        q1_back = tile([P, FRONT], U32, "q1_back_codes", "cs_rows"), tile([P, FRONT], U8, "q1_back_scales")
+        q1_back = tile([P, FRONT], U32, "q1_back_codes", "cs_pool"), tile([P, FRONT], U8, "q1_back_scales")
         for j in range(2):
             nc.vector.quantize_mx(
                 q1_back[0][:, block(j)].bitcast(FP8X4), q1_back[1][:, block(j)], bf_late[j][:].rearrange("p c t -> p (c t)")

@@ -28,6 +28,8 @@ ROWS = 16
 FINE_AT = 4
 ALIGN = 64
 FRONT = 2 * P
+SHARE = 96
+TH_AT = 16
 
 
 def interleave(engine_copy, dst, src):
@@ -68,7 +70,7 @@ def tile_attend_plw_residsig_topk_kernel(tc, qT, k_words, k_scales, c_words, c_s
         load_q(1, 0, FRONT, q_front1[:])
         th_rows = tile([P, P], F32, "th_rows")
         nc.gpsimd.memset(th_rows[:], 0.0)
-        nc.sync.dma_start(th_rows[0:BLOCKS, :], th[0, 0].rearrange("(j p) -> j p", p=P))
+        nc.sync.dma_start(th_rows[TH_AT : TH_AT + BLOCKS, :], th[0, 0].rearrange("(j p) -> j p", p=P))
         nc.gpsimd.memset(ks_pool[QUAD : 2 * QUAD, :].bitcast(I32), 0)
         nc.vector.memset(ks_pool[2 * QUAD : P, :].bitcast(I32), 0)
         nc.vector.memset(cs_pool[0 : 2 * QUAD, :].bitcast(I32), 0)
@@ -132,7 +134,7 @@ def tile_attend_plw_residsig_topk_kernel(tc, qT, k_words, k_scales, c_words, c_s
         th_turned = psum.tile([P, P], F32, name="th_turned", tag="back0")
         nc.tensor.transpose(th_turned[:], th_rows[:], ident[:])
         th_cols = tile([P, BLOCKS], F32, "th_cols")
-        nc.scalar.copy(th_cols[:], th_turned[:, 0:BLOCKS])
+        nc.scalar.copy(th_cols[:], th_turned[:, TH_AT : TH_AT + BLOCKS])
         th_spread = psum.tile([P, NQ], F32, name="th_spread", tag="back1")
         for j in range(BLOCKS):
             nc.tensor.transpose(th_spread[:, block(j)], th_cols[:, j : j + 1].to_broadcast([P, P]), ident[:])
@@ -211,9 +213,8 @@ def tile_attend_plw_residsig_topk_kernel(tc, qT, k_words, k_scales, c_words, c_s
             nc.vector.quantize_mx(
                 q1_back[0][:, block(j)].bitcast(FP8X4), q1_back[1][:, block(j)], bf_late[j][:].rearrange("p c t -> p (c t)")
             )
-            for u in range(PACK):
-                coarse(back[u][:, block(j)], 1, u, q1_back, block(j))
         for u in range(PACK):
+            coarse_passes(back[u], 1, u, q1_back)
             fine(back[u][:], 1, u, q1_back, whole, stop=True)
         z_front = tile([P, PACK, FRONT], F32, "z_front", "kw_pool")
         y_front = tile([P, PACK, FRONT], F32, "y_front")
@@ -223,8 +224,8 @@ def tile_attend_plw_residsig_topk_kernel(tc, qT, k_words, k_scales, c_words, c_s
             weigh(back[u], slice(FRONT, NQ), z_back, y_back, u, 2)
         y_bf_front = rounded("y_bf_front", nc.vector.tensor_copy, y_front[:])
         y_bf_back = tile([P, FRONT, PACK], BF16, "y_bf_back")
-        interleave(sigmoid, y_bf_back[:, block(1), :], z_back[:, :, block(1)])
-        interleave(nc.vector.tensor_copy, y_bf_back[:, block(0), :], y_back[:, :, block(0)])
+        interleave(sigmoid, y_bf_back[:, SHARE:FRONT, :], z_back[:, :, SHARE:FRONT])
+        interleave(nc.vector.tensor_copy, y_bf_back[:, 0:SHARE, :], y_back[:, :, 0:SHARE])
         quantise_y(whole, y_bf_front)
         quantise_y(slice(FRONT, NQ), y_bf_back)
         for r in range(QUAD_ROWS):

@@ -27,9 +27,11 @@ QUAD_ROWS = 4
 ROWS = 16
 FINE_AT = 4
 ALIGN = 64
-FRONT = 2 * P
+HALF = 2 * P
 SHARE = 96
 TH_AT = 16
+COARSE_ROWS_AT, FINE_ROWS_AT = 0, 2 * QUAD
+EARLY_BACK = 2
 
 
 def interleave(engine_copy, dst, src):
@@ -56,18 +58,59 @@ def tile_attend_plw_residsig_topk_kernel(tc, qT, k_words, k_scales, c_words, c_s
             nc.sync.dma_start(pool[:], words.rearrange("p t b -> p (t b)").bitcast(I32))
             return pool
 
+        def load_scale_rows(pool, first, scales):
+            nc.sync.dma_start(pool[first : first + QUAD, :].bitcast(I32), scales.rearrange("o f t -> f o t").bitcast(I32))
+
+        def gather_dealt(dst, window):
+            nc.vector.tensor_copy(dst[:].rearrange("p (u s) -> p s u", u=PACK), window.indirect(offsets[:]))
+
+        def move_scales(dst, at, src, first):
+            rows = PASSES * QUAD_ROWS
+            for quad in (0, 2, 1, 3):
+                nc.sync.dma_start(
+                    dst[quad * QUAD + at : quad * QUAD + at + QUAD_ROWS, :].bitcast(I32),
+                    src[first + quad * rows : first + (quad + 1) * rows, :].bitcast(I32),
+                )
+
+        def rounded(name, engine_copy, raw):
+            dst = tile([P, raw.shape[2], PACK], BF16, name)
+            interleave(engine_copy, dst[:], raw)
+            return dst
+
+        def quantise(codes, scales, values):
+            nc.vector.quantize_mx(codes.bitcast(FP8X4), scales, values[:].rearrange("p c t -> p (c t)"))
+
+        def quantised(name, q_bf, buffer=None):
+            codes = tile([P, HALF], U32, name + "_codes", buffer)
+            scales = tile([P, HALF], U8, name + "_scales")
+            quantise(codes[:], scales[:], q_bf)
+            return codes, scales
+
+        def block(j):
+            return slice(j * P, (j + 1) * P)
+
+        def coarse(bank, o, u, q, start=False):
+            nc.tensor.matmul_mx(
+                bank[:], kw[:, o, block(u)].bitcast(FP4X4), ks[:, o, block(u)], q[0][:].bitcast(FP8X4), q[1][:], start=start, stop=False
+            )
+
+        def fine(bank, o, u, q, stop=False):
+            nc.tensor.matmul_mx(
+                bank[:], cw[o][:, block(u)].bitcast(FP8X4), cs[FINE_AT:P, o, block(u)], q[0][:].bitcast(FP8X4), q[1][:], start=False, stop=stop
+            )
+
         warm = tile([P, 16], F32, "warm")
         nc.vector.memset(warm[:, 0:1], 0.0)
         nc.scalar.activation(warm[:, 8:9], warm[:, 0:1], SIGMOID)
-        KS_AT, CS_AT = 0, 2 * QUAD
+
         ks_pool = tile([P, T], U8, "ks_pool")
-        nc.sync.dma_start(ks_pool[KS_AT : KS_AT + QUAD, :].bitcast(I32), k_scales.rearrange("o f t -> f o t").bitcast(I32))
+        load_scale_rows(ks_pool, COARSE_ROWS_AT, k_scales)
         offsets = sbuf.tile([P, N // 16], U16, name="offsets")
         nc.sync.dma_start(offsets[:], offs)
         cs_pool = tile([P, T], U8, "cs_pool")
-        nc.sync.dma_start(cs_pool[CS_AT : CS_AT + QUAD, :].bitcast(I32), c_scales.rearrange("o f t -> f o t").bitcast(I32))
-        q_front1 = tile([P, PACK, FRONT], F32, "q_front1")
-        load_q(1, 0, FRONT, q_front1[:])
+        load_scale_rows(cs_pool, FINE_ROWS_AT, c_scales)
+        q_front1 = tile([P, PACK, HALF], F32, "q_front1")
+        load_q(1, 0, HALF, q_front1[:])
         th_rows = tile([P, P], F32, "th_rows")
         nc.gpsimd.memset(th_rows[:], 0.0)
         nc.sync.dma_start(th_rows[TH_AT : TH_AT + BLOCKS, :], th[0, 0].rearrange("(j p) -> j p", p=P))
@@ -78,58 +121,13 @@ def tile_attend_plw_residsig_topk_kernel(tc, qT, k_words, k_scales, c_words, c_s
         ident = tile([P, P], F32, "ident")
         nc.vector.memset(ident[:], 0.0)
         make_identity(nc, ident[:], nomemset=True)
-        ks = tile([P, PASSES * N], U8, "ks")
-        cs = tile([P, PASSES * N], U8, "cs")
+        ks = tile([P, PASSES, N], U8, "ks")
+        cs = tile([P, PASSES, N], U8, "cs")
         for planes in (ks, cs):
-            nc.gpsimd.memset(planes[:].bitcast(I32), 0)
-
+            nc.gpsimd.memset(planes[:].rearrange("p o s -> p (o s)").bitcast(I32), 0)
         kw_pool = load_words(tile([P, T], I32, "kw_pool"), k_words[0])
         q_pass0 = tile([P, PACK, NQ], F32, "q_pass0")
         load_q(0, 0, NQ, q_pass0[:])
-
-        def gather(dst, window):
-            nc.vector.tensor_copy(dst, window.indirect(offsets[:]))
-
-        def gather_dealt(dst, pool):
-            gather(dst[:].rearrange("p (u s) -> p s u", u=PACK), pool[:].bitcast(U32))
-
-        def gather_scales(pool, name):
-            dealt = tile([P, N], U8, name + "_dealt")
-            gather(dealt[:].rearrange("p (u s) -> p s u", u=PACK), pool[:])
-            return dealt
-
-        def move_scales(dst, at, src, first, queues):
-            rows = PASSES * QUAD_ROWS
-            for quad, queue in zip((0, 2, 1, 3), queues):
-                queue.dma_start(
-                    dst[quad * QUAD + at : quad * QUAD + at + QUAD_ROWS, :].bitcast(I32),
-                    src[first + quad * rows : first + (quad + 1) * rows, :].bitcast(I32),
-                )
-
-        def rounded(name, engine_copy, raw, buffer=None):
-            dst = tile([P, raw.shape[2], PACK], BF16, name, buffer)
-            interleave(engine_copy, dst[:], raw)
-            return dst
-
-        def quantised(name, q_bf, buffer=None):
-            width = q_bf.shape[1]
-            codes = tile([P, width], U32, name + "_codes", buffer)
-            scales = tile([P, width], U8, name + "_scales")
-            nc.vector.quantize_mx(codes[:].bitcast(FP8X4), scales[:], q_bf[:].rearrange("p c t -> p (c t)"))
-            return codes, scales
-
-
-        def product(out, keys, key_scales, q, cols, start=False, stop=False):
-            nc.tensor.matmul_mx(out, keys, key_scales, q[0][:, cols].bitcast(FP8X4), q[1][:, cols], start=start, stop=stop)
-
-        def coarse(out, o, u, q, cols, start=False):
-            product(out, kw[:, o, u * P : (u + 1) * P].bitcast(FP4X4), ks[:, o * N + u * P : o * N + (u + 1) * P], q, cols, start=start)
-
-        def fine(out, o, u, q, cols, stop=False):
-            product(out, cw[o][:, u * P : (u + 1) * P].bitcast(FP8X4), cs[FINE_AT:P, o * N + u * P : o * N + (u + 1) * P], q, cols, stop=stop)
-
-        def block(j):
-            return slice(j * P, (j + 1) * P)
 
         th_turned = psum.tile([P, P], F32, name="th_turned", tag="back0")
         nc.tensor.transpose(th_turned[:], th_rows[:], ident[:])
@@ -142,57 +140,54 @@ def tile_attend_plw_residsig_topk_kernel(tc, qT, k_words, k_scales, c_words, c_s
         th_all = tile([P, NQ], F32, "th_all")
         nc.scalar.copy(th_all[:], th_spread[:])
 
-        front = [psum.tile([P, FRONT], F32, name=f"front{u}") for u in range(PACK)]
-        back = [psum.tile([P, FRONT], F32, name=f"back{u}") for u in range(PACK)]
+        front = [psum.tile([P, HALF], F32, name=f"front{u}") for u in range(PACK)]
+        back = [psum.tile([P, HALF], F32, name=f"back{u}") for u in range(PACK)]
 
-        def coarse_passes(bank, o, u, q, start=False):
-            for j in range(2):
-                coarse(bank[:, block(j)], o, u, q, block(j), start=start and j == 0)
-
-        ks_dealt = gather_scales(ks_pool, "ks")
-        move_scales(ks, 0, ks_dealt, KS_AT, [nc.sync] * 4)
+        ks_dealt = tile([P, N], U8, "ks_dealt")
+        gather_dealt(ks_dealt, ks_pool[:])
+        move_scales(ks[:].rearrange("p o s -> p (o s)"), 0, ks_dealt, COARSE_ROWS_AT)
         cw_pool0 = load_words(tile([P, T], I32, "cw_pool0", "ks_pool"), c_words[0])
-        cs_dealt = gather_scales(cs_pool, "cs")
-        move_scales(cs, FINE_AT, cs_dealt, CS_AT, [nc.sync, nc.sync, nc.scalar, nc.scalar])
+        cs_dealt = tile([P, N], U8, "cs_dealt")
+        gather_dealt(cs_dealt, cs_pool[:])
         cw_pool1 = load_words(tile([P, T], I32, "cw_pool1", "cs_pool"), c_words[1])
-        q1_front = quantised("q1_front", bf_front1)
+        move_scales(cs[:].rearrange("p o s -> p (o s)"), FINE_AT, cs_dealt, FINE_ROWS_AT)
 
         kw_pair = tile([P, N], U32, "kw_pair")
-        gather_dealt(kw_pair, kw_pool)
+        gather_dealt(kw_pair, kw_pool[:].bitcast(U32))
         q_late_both = tile([P, 2 * PACK * P], F32, "q_late", "kw_pool")
         q_late = [q_late_both[:, j * PACK * P : (j + 1) * PACK * P].rearrange("p (t w) -> p t w", t=PACK) for j in range(2)]
         for j in range(2):
-            load_q(1, FRONT + j * P, P, q_late[j])
+            load_q(1, HALF + j * P, P, q_late[j])
         kw = tile([P, PASSES, N], U16, "kw")
         nc.vector.tensor_copy(kw[:], kw_pair[:].bitcast(U16).rearrange("p (s o) -> p o s", o=PASSES))
-        whole = slice(0, FRONT)
-        for u in range(PACK):
-            coarse_passes(front[u], 1, u, q1_front, start=True)
-        bf_front0 = rounded("bf_front0", nc.scalar.copy, q_pass0[:, :, 0:FRONT])
-        bf_back0 = rounded("bf_back0", nc.vector.tensor_copy, q_pass0[:, :, FRONT:NQ])
+        bf_front0 = rounded("bf_front0", nc.scalar.copy, q_pass0[:, :, 0:HALF])
+        bf_back0 = rounded("bf_back0", nc.vector.tensor_copy, q_pass0[:, :, HALF:NQ])
         q0_back = quantised("q0_back", bf_back0)
         for u in range(PACK):
-            coarse_passes(back[u], 0, u, q0_back, start=True)
+            coarse(back[u], 0, u, q0_back, start=True)
         q0_front = quantised("q0_front", bf_front0)
         for u in range(PACK):
-            coarse_passes(front[u], 0, u, q0_front)
+            coarse(front[u], 0, u, q0_front, start=True)
         cw = [tile([P, N], U32, "cw0", "bf_front0")]
-        gather_dealt(cw[0], cw_pool0)
+        gather_dealt(cw[0], cw_pool0[:].bitcast(U32))
+        q1_front = quantised("q1_front", bf_front1, "ks_pool")
         for u in range(PACK):
-            fine(back[u][:], 0, u, q0_back, whole)
+            coarse(front[u], 1, u, q1_front)
+        cw.append(tile([P, N], U32, "cw1", "bf_front1"))
+        gather_dealt(cw[1], cw_pool1[:].bitcast(U32))
         for u in range(PACK):
-            fine(front[u][:], 0, u, q0_front, whole)
-        cw.append(tile([P, N], U32, "cw1", "bf_back0"))
-        gather_dealt(cw[1], cw_pool1)
+            fine(front[u], 0, u, q0_front)
+        for u in range(EARLY_BACK):
+            fine(back[u], 0, u, q0_back)
         for u in range(PACK):
-            fine(front[u][:], 1, u, q1_front, whole, stop=True)
+            fine(front[u], 1, u, q1_front, stop=True)
 
         y_scales = tile([P, NQ], U8, "y_scales")
         y_words = tile([P, NQ], I32, "y_words")
         rows_out = out_0.rearrange("(p u) q -> p u q", u=PACK)
         words_out = out_1[0].rearrange("p q t -> p (q t)").bitcast(I32)
-        y_back = tile([P, PACK, FRONT], F32, "y_back")
-        z_back = tile([P, PACK, FRONT], F32, "z_back")
+        y_back = tile([P, PACK, HALF], F32, "y_back")
+        z_back = tile([P, PACK, HALF], F32, "z_back")
 
         def sigmoid(dst, src):
             nc.scalar.activation(dst, src, SIGMOID)
@@ -204,30 +199,30 @@ def tile_attend_plw_residsig_topk_kernel(tc, qT, k_words, k_scales, c_words, c_s
                 nc.sync.dma_start(rows_out[:, u + 1 - stored : u + 1, cols], y[:, u + 1 - stored : u + 1, :])
 
         def quantise_y(cols, y_bf):
-            nc.vector.quantize_mx(y_words[:, cols].bitcast(FP8X4), y_scales[:, cols], y_bf[:].rearrange("p q u -> p (q u)"))
+            quantise(y_words[:, cols], y_scales[:, cols], y_bf)
             nc.sync.dma_start(words_out[:, cols], y_words[:, cols])
 
         bf_late = [rounded(f"bf_late{j}", nc.scalar.copy, q_late[j]) for j in range(2)]
-        q1_back = tile([P, FRONT], U32, "q1_back_codes", "cs_pool"), tile([P, FRONT], U8, "q1_back_scales")
+        q1_back = tile([P, HALF], U32, "q1_back_codes", "cs_pool"), tile([P, HALF], U8, "q1_back_scales")
         for j in range(2):
-            nc.vector.quantize_mx(
-                q1_back[0][:, block(j)].bitcast(FP8X4), q1_back[1][:, block(j)], bf_late[j][:].rearrange("p c t -> p (c t)")
-            )
+            quantise(q1_back[0][:, block(j)], q1_back[1][:, block(j)], bf_late[j])
         for u in range(PACK):
-            coarse_passes(back[u], 1, u, q1_back)
-            fine(back[u][:], 1, u, q1_back, whole, stop=True)
-        z_front = tile([P, PACK, FRONT], F32, "z_front", "kw_pool")
-        y_front = tile([P, PACK, FRONT], F32, "y_front")
+            if u >= EARLY_BACK:
+                fine(back[u], 0, u, q0_back)
+            coarse(back[u], 1, u, q1_back)
+            fine(back[u], 1, u, q1_back, stop=True)
+        z_front = tile([P, PACK, HALF], F32, "z_front", "kw_pool")
+        y_front = tile([P, PACK, HALF], F32, "y_front")
         for u in range(PACK):
-            weigh(front[u], whole, z_front, y_front, u, 1)
+            weigh(front[u], slice(0, HALF), z_front, y_front, u, 1)
         for u in range(PACK):
-            weigh(back[u], slice(FRONT, NQ), z_back, y_back, u, 2)
+            weigh(back[u], slice(HALF, NQ), z_back, y_back, u, 2)
         y_bf_front = rounded("y_bf_front", nc.vector.tensor_copy, y_front[:])
-        y_bf_back = tile([P, FRONT, PACK], BF16, "y_bf_back")
-        interleave(sigmoid, y_bf_back[:, SHARE:FRONT, :], z_back[:, :, SHARE:FRONT])
+        y_bf_back = tile([P, HALF, PACK], BF16, "y_bf_back")
+        interleave(sigmoid, y_bf_back[:, SHARE:HALF, :], z_back[:, :, SHARE:HALF])
         interleave(nc.vector.tensor_copy, y_bf_back[:, 0:SHARE, :], y_back[:, :, 0:SHARE])
-        quantise_y(whole, y_bf_front)
-        quantise_y(slice(FRONT, NQ), y_bf_back)
+        quantise_y(slice(0, HALF), y_bf_front)
+        quantise_y(slice(HALF, NQ), y_bf_back)
         for r in range(QUAD_ROWS):
             queue = nc.scalar if r % 2 == 0 else nc.sync
             queue.dma_start(out_2[0, r:ROWS:QUAD_ROWS, :].bitcast(I32), y_scales[r:P:QUAD, :].bitcast(I32))

@@ -28,10 +28,9 @@ ROWS = 16
 FINE_AT = 4
 ALIGN = 64
 HALF = 2 * P
-SHARE = 96
+SHARE = 160
 TH_AT = 16
 COARSE_ROWS_AT, FINE_ROWS_AT = 0, 2 * QUAD
-EARLY_BACK = 2
 
 
 def interleave(engine_copy, dst, src):
@@ -64,11 +63,11 @@ def tile_attend_plw_residsig_topk_kernel(tc, qT, k_words, k_scales, c_words, c_s
         def gather_dealt(dst, window):
             nc.vector.tensor_copy(dst[:].rearrange("p (u s) -> p s u", u=PACK), window.indirect(offsets[:]))
 
-        def move_scales(dst, at, src, first):
+        def move_scales(planes, at, src, first, queues):
             rows = PASSES * QUAD_ROWS
-            for quad in (0, 2, 1, 3):
-                nc.sync.dma_start(
-                    dst[quad * QUAD + at : quad * QUAD + at + QUAD_ROWS, :].bitcast(I32),
+            for quad, queue in zip((0, 2, 1, 3), queues):
+                queue.dma_start(
+                    planes[quad * QUAD + at : quad * QUAD + at + QUAD_ROWS].rearrange("p o s -> p (o s)").bitcast(I32),
                     src[first + quad * rows : first + (quad + 1) * rows, :].bitcast(I32),
                 )
 
@@ -91,12 +90,12 @@ def tile_attend_plw_residsig_topk_kernel(tc, qT, k_words, k_scales, c_words, c_s
 
         def coarse(bank, o, u, q, start=False):
             nc.tensor.matmul_mx(
-                bank[:], kw[:, o, block(u)].bitcast(FP4X4), ks[:, o, block(u)], q[0][:].bitcast(FP8X4), q[1][:], start=start, stop=False
+                bank, kw[:, o, block(u)].bitcast(FP4X4), ks[:, o, block(u)], q[0][:].bitcast(FP8X4), q[1][:], start=start, stop=False
             )
 
         def fine(bank, o, u, q, stop=False):
             nc.tensor.matmul_mx(
-                bank[:], cw[o][:, block(u)].bitcast(FP8X4), cs[FINE_AT:P, o, block(u)], q[0][:].bitcast(FP8X4), q[1][:], start=False, stop=stop
+                bank, cw[o][:, block(u)].bitcast(FP8X4), cs[FINE_AT:P, o, block(u)], q[0][:].bitcast(FP8X4), q[1][:], start=False, stop=stop
             )
 
         warm = tile([P, 16], F32, "warm")
@@ -140,17 +139,19 @@ def tile_attend_plw_residsig_topk_kernel(tc, qT, k_words, k_scales, c_words, c_s
         th_all = tile([P, NQ], F32, "th_all")
         nc.scalar.copy(th_all[:], th_spread[:])
 
-        front = [psum.tile([P, HALF], F32, name=f"front{u}") for u in range(PACK)]
-        back = [psum.tile([P, HALF], F32, name=f"back{u}") for u in range(PACK)]
+        front = [psum.tile([P, HALF], F32, name=f"front{u}")[:] for u in range(PACK)]
+        back_pairs = [psum.tile([P, 2, HALF], F32, name=f"back{pair}") for pair in range(2)]
+        back = [back_pairs[u // 2][:, u % 2, :] for u in range(PACK)]
 
         ks_dealt = tile([P, N], U8, "ks_dealt")
         gather_dealt(ks_dealt, ks_pool[:])
-        move_scales(ks[:].rearrange("p o s -> p (o s)"), 0, ks_dealt, COARSE_ROWS_AT)
+        move_scales(ks, 0, ks_dealt, COARSE_ROWS_AT, [nc.sync] * 4)
         cw_pool0 = load_words(tile([P, T], I32, "cw_pool0", "ks_pool"), c_words[0])
         cs_dealt = tile([P, N], U8, "cs_dealt")
         gather_dealt(cs_dealt, cs_pool[:])
+        move_scales(cs, FINE_AT, cs_dealt, FINE_ROWS_AT, [nc.sync, nc.sync, nc.scalar, nc.scalar])
         cw_pool1 = load_words(tile([P, T], I32, "cw_pool1", "cs_pool"), c_words[1])
-        move_scales(cs[:].rearrange("p o s -> p (o s)"), FINE_AT, cs_dealt, FINE_ROWS_AT)
+        q1_front = quantised("q1_front", bf_front1)
 
         kw_pair = tile([P, N], U32, "kw_pair")
         gather_dealt(kw_pair, kw_pool[:].bitcast(U32))
@@ -160,25 +161,24 @@ def tile_attend_plw_residsig_topk_kernel(tc, qT, k_words, k_scales, c_words, c_s
             load_q(1, HALF + j * P, P, q_late[j])
         kw = tile([P, PASSES, N], U16, "kw")
         nc.vector.tensor_copy(kw[:], kw_pair[:].bitcast(U16).rearrange("p (s o) -> p o s", o=PASSES))
+        for u in range(PACK):
+            coarse(front[u], 1, u, q1_front, start=True)
         bf_front0 = rounded("bf_front0", nc.scalar.copy, q_pass0[:, :, 0:HALF])
         bf_back0 = rounded("bf_back0", nc.vector.tensor_copy, q_pass0[:, :, HALF:NQ])
         q0_back = quantised("q0_back", bf_back0)
         for u in range(PACK):
-            coarse(back[u], 0, u, q0_back, start=True)
+            coarse(back[u], 0, u, q0_back, start=u % 2 == 0)
         q0_front = quantised("q0_front", bf_front0)
         for u in range(PACK):
-            coarse(front[u], 0, u, q0_front, start=True)
+            coarse(front[u], 0, u, q0_front)
         cw = [tile([P, N], U32, "cw0", "bf_front0")]
         gather_dealt(cw[0], cw_pool0[:].bitcast(U32))
-        q1_front = quantised("q1_front", bf_front1, "ks_pool")
         for u in range(PACK):
-            coarse(front[u], 1, u, q1_front)
-        cw.append(tile([P, N], U32, "cw1", "bf_front1"))
-        gather_dealt(cw[1], cw_pool1[:].bitcast(U32))
+            fine(back[u], 0, u, q0_back)
         for u in range(PACK):
             fine(front[u], 0, u, q0_front)
-        for u in range(EARLY_BACK):
-            fine(back[u], 0, u, q0_back)
+        cw.append(tile([P, N], U32, "cw1", "bf_back0"))
+        gather_dealt(cw[1], cw_pool1[:].bitcast(U32))
         for u in range(PACK):
             fine(front[u], 1, u, q1_front, stop=True)
 
@@ -192,12 +192,6 @@ def tile_attend_plw_residsig_topk_kernel(tc, qT, k_words, k_scales, c_words, c_s
         def sigmoid(dst, src):
             nc.scalar.activation(dst, src, SIGMOID)
 
-        def weigh(bank, cols, z, y, u, stored):
-            nc.vector.tensor_tensor(z[:, u, :], bank[:], th_all[:, cols], SUBTRACT)
-            sigmoid(y[:, u, :], z[:, u, :])
-            if (u + 1) % stored == 0:
-                nc.sync.dma_start(rows_out[:, u + 1 - stored : u + 1, cols], y[:, u + 1 - stored : u + 1, :])
-
         def quantise_y(cols, y_bf):
             quantise(y_words[:, cols], y_scales[:, cols], y_bf)
             nc.sync.dma_start(words_out[:, cols], y_words[:, cols])
@@ -207,20 +201,26 @@ def tile_attend_plw_residsig_topk_kernel(tc, qT, k_words, k_scales, c_words, c_s
         for j in range(2):
             quantise(q1_back[0][:, block(j)], q1_back[1][:, block(j)], bf_late[j])
         for u in range(PACK):
-            if u >= EARLY_BACK:
-                fine(back[u], 0, u, q0_back)
             coarse(back[u], 1, u, q1_back)
-            fine(back[u], 1, u, q1_back, stop=True)
+            fine(back[u], 1, u, q1_back, stop=u % 2 == 1)
         z_front = tile([P, PACK, HALF], F32, "z_front", "kw_pool")
         y_front = tile([P, PACK, HALF], F32, "y_front")
         for u in range(PACK):
-            weigh(front[u], slice(0, HALF), z_front, y_front, u, 1)
-        for u in range(PACK):
-            weigh(back[u], slice(HALF, NQ), z_back, y_back, u, 2)
-        y_bf_front = rounded("y_bf_front", nc.vector.tensor_copy, y_front[:])
+            nc.vector.tensor_tensor(z_front[:, u, :], front[u], th_all[:, 0:HALF], SUBTRACT)
+            sigmoid(y_front[:, u, :], z_front[:, u, :])
+            nc.sync.dma_start(rows_out[:, u : u + 1, 0:HALF], y_front[:, u : u + 1, :])
         y_bf_back = tile([P, HALF, PACK], BF16, "y_bf_back")
+        for pair in range(2):
+            places = slice(2 * pair, 2 * pair + 2)
+            for j in range(2):
+                th_block = th_all[:, HALF + j * P : HALF + (j + 1) * P].unsqueeze(1).to_broadcast([P, 2, P])
+                nc.vector.tensor_tensor(z_back[:, places, block(j)], back_pairs[pair][:, :, block(j)], th_block, SUBTRACT)
+                sigmoid(y_back[:, places, block(j)], z_back[:, places, block(j)])
+            nc.sync.dma_start(rows_out[:, places, HALF:NQ], y_back[:, places, :])
+        y_bf_front = rounded("y_bf_front", nc.vector.tensor_copy, y_front[:])
         interleave(sigmoid, y_bf_back[:, SHARE:HALF, :], z_back[:, :, SHARE:HALF])
-        interleave(nc.vector.tensor_copy, y_bf_back[:, 0:SHARE, :], y_back[:, :, 0:SHARE])
+        for cols in (block(0), slice(P, SHARE)):
+            interleave(nc.vector.tensor_copy, y_bf_back[:, cols, :], y_back[:, :, cols])
         quantise_y(slice(0, HALF), y_bf_front)
         quantise_y(slice(HALF, NQ), y_bf_back)
         for r in range(QUAD_ROWS):

@@ -63,16 +63,16 @@ def tile_attend_plw_residsig_topk_kernel(tc, qT, k_words, k_scales, c_words, c_s
         def gather_dealt(dst, window):
             nc.vector.tensor_copy(dst[:].rearrange("p (u s) -> p s u", u=PACK), window.indirect(offsets[:]))
 
-        def move_scales(planes, at, src, first, queues):
+        def move_scales(planes, at, src, first):
             rows = PASSES * QUAD_ROWS
-            for quad, queue in zip((0, 2, 1, 3), queues):
-                queue.dma_start(
+            for quad in (0, 2, 1, 3):
+                nc.sync.dma_start(
                     planes[quad * QUAD + at : quad * QUAD + at + QUAD_ROWS].rearrange("p o s -> p (o s)").bitcast(I32),
                     src[first + quad * rows : first + (quad + 1) * rows, :].bitcast(I32),
                 )
 
-        def rounded(name, engine_copy, raw):
-            dst = tile([P, raw.shape[2], PACK], BF16, name)
+        def rounded(name, engine_copy, raw, buffer=None):
+            dst = tile([P, raw.shape[2], PACK], BF16, name, buffer)
             interleave(engine_copy, dst[:], raw)
             return dst
 
@@ -145,42 +145,43 @@ def tile_attend_plw_residsig_topk_kernel(tc, qT, k_words, k_scales, c_words, c_s
 
         ks_dealt = tile([P, N], U8, "ks_dealt")
         gather_dealt(ks_dealt, ks_pool[:])
-        move_scales(ks, 0, ks_dealt, COARSE_ROWS_AT, [nc.sync] * 4)
+        move_scales(ks, 0, ks_dealt, COARSE_ROWS_AT)
         cw_pool0 = load_words(tile([P, T], I32, "cw_pool0", "ks_pool"), c_words[0])
         cs_dealt = tile([P, N], U8, "cs_dealt")
         gather_dealt(cs_dealt, cs_pool[:])
-        move_scales(cs, FINE_AT, cs_dealt, FINE_ROWS_AT, [nc.sync, nc.sync, nc.scalar, nc.scalar])
         cw_pool1 = load_words(tile([P, T], I32, "cw_pool1", "cs_pool"), c_words[1])
-        q1_front = quantised("q1_front", bf_front1)
+        move_scales(cs, FINE_AT, cs_dealt, FINE_ROWS_AT)
 
         kw_pair = tile([P, N], U32, "kw_pair")
         gather_dealt(kw_pair, kw_pool[:].bitcast(U32))
-        q_late_both = tile([P, 2 * PACK * P], F32, "q_late", "kw_pool")
-        q_late = [q_late_both[:, j * PACK * P : (j + 1) * PACK * P].rearrange("p (t w) -> p t w", t=PACK) for j in range(2)]
-        for j in range(2):
-            load_q(1, HALF + j * P, P, q_late[j])
         kw = tile([P, PASSES, N], U16, "kw")
         nc.vector.tensor_copy(kw[:], kw_pair[:].bitcast(U16).rearrange("p (s o) -> p o s", o=PASSES))
-        for u in range(PACK):
-            coarse(front[u], 1, u, q1_front, start=True)
-        bf_front0 = rounded("bf_front0", nc.scalar.copy, q_pass0[:, :, 0:HALF])
+        q_late = [tile([P, PACK, P], F32, f"q_late{j}", buffer) for j, buffer in enumerate(("kw_pool", "kw_pair"))]
+        for j in range(2):
+            load_q(1, HALF + j * P, P, q_late[j][:])
+        bf_front0 = rounded("bf_front0", nc.scalar.copy, q_pass0[:, :, 0:HALF], "ks_dealt")
         bf_back0 = rounded("bf_back0", nc.vector.tensor_copy, q_pass0[:, :, HALF:NQ])
         q0_back = quantised("q0_back", bf_back0)
         for u in range(PACK):
             coarse(back[u], 0, u, q0_back, start=u % 2 == 0)
         q0_front = quantised("q0_front", bf_front0)
         for u in range(PACK):
-            coarse(front[u], 0, u, q0_front)
-        cw = [tile([P, N], U32, "cw0", "bf_front0")]
+            coarse(front[u], 0, u, q0_front, start=True)
+        cw = [tile([P, N], U32, "cw0", "ks_dealt")]
         gather_dealt(cw[0], cw_pool0[:].bitcast(U32))
+        q1_front = quantised("q1_front", bf_front1, "ks_pool")
         for u in range(PACK):
-            fine(back[u], 0, u, q0_back)
-        for u in range(PACK):
-            fine(front[u], 0, u, q0_front)
-        cw.append(tile([P, N], U32, "cw1", "bf_back0"))
+            coarse(front[u], 1, u, q1_front)
+        cw.append(tile([P, N], U32, "cw1", "bf_front1"))
         gather_dealt(cw[1], cw_pool1[:].bitcast(U32))
         for u in range(PACK):
+            fine(front[u], 0, u, q0_front)
+        for u in range(2):
+            fine(back[u], 0, u, q0_back)
+        for u in range(PACK):
             fine(front[u], 1, u, q1_front, stop=True)
+        for u in range(2, PACK):
+            fine(back[u], 0, u, q0_back)
 
         y_scales = tile([P, NQ], U8, "y_scales")
         y_words = tile([P, NQ], I32, "y_words")
@@ -196,14 +197,14 @@ def tile_attend_plw_residsig_topk_kernel(tc, qT, k_words, k_scales, c_words, c_s
             quantise(y_words[:, cols], y_scales[:, cols], y_bf)
             nc.sync.dma_start(words_out[:, cols], y_words[:, cols])
 
-        bf_late = [rounded(f"bf_late{j}", nc.scalar.copy, q_late[j]) for j in range(2)]
+        bf_late = [rounded(f"bf_late{j}", copy, q_late[j][:]) for j, copy in enumerate((nc.scalar.copy, nc.vector.tensor_copy))]
         q1_back = tile([P, HALF], U32, "q1_back_codes", "cs_pool"), tile([P, HALF], U8, "q1_back_scales")
         for j in range(2):
             quantise(q1_back[0][:, block(j)], q1_back[1][:, block(j)], bf_late[j])
         for u in range(PACK):
             coarse(back[u], 1, u, q1_back)
             fine(back[u], 1, u, q1_back, stop=u % 2 == 1)
-        z_front = tile([P, PACK, HALF], F32, "z_front", "kw_pool")
+        z_front = tile([P, PACK, HALF], F32, "z_front", "kw_pair")
         y_front = tile([P, PACK, HALF], F32, "y_front")
         for u in range(PACK):
             nc.vector.tensor_tensor(z_front[:, u, :], front[u], th_all[:, 0:HALF], SUBTRACT)

from contextlib import ExitStack

import concourse.mybir as mybir
from concourse.masks import make_identity

N, T, D, NQ = 512, 2048, 1024, 512
FLOPS = 2 * 2 * N * D * NQ

F32 = mybir.dt.float32
BF16 = mybir.dt.bfloat16
I32 = mybir.dt.int32
U32 = mybir.dt.uint32
U16 = mybir.dt.uint16
U8 = mybir.dt.uint8
FP8X4 = mybir.dt.float8_e4m3fn_x4
FP4X4 = mybir.dt.float4_e2m1fn_x4
SIGMOID = mybir.ActivationFunctionType.Sigmoid
SUBTRACT = mybir.AluOpType.subtract

P = 128
PACK = 4
K_PASS = P * PACK
PASSES = D // K_PASS
BLOCKS = NQ // P
QUAD = 32
QUAD_ROWS = 4
ROWS = 16
FINE_AT = 4
ALIGN = 64
HALF = 2 * P
SHARE = 160
TH_AT = 16
COARSE_ROWS_AT, FINE_ROWS_AT = 0, 2 * QUAD


def interleave(engine_copy, dst, src):
    engine_copy(
        dst.rearrange("p (c i) t -> p c t i", i=2),
        src.rearrange("p t (c i) -> p c t i", i=2),
    )


def tile_attend_plw_residsig_topk_kernel(tc, qT, k_words, k_scales, c_words, c_scales, th, offs, out_0, out_1, out_2):
    nc = tc.nc
    with ExitStack() as ctx:
        sbuf = ctx.enter_context(tc.tile_pool(name="sbuf", bufs=1))
        psum = ctx.enter_context(tc.psum_pool(name="psum", bufs=1))

        def tile(shape, dtype, name, buffer=None):
            return sbuf.tile(shape, dtype, name=name, tag=buffer or name, align_bytes=ALIGN)

        def load_q(o, first, width, dst):
            rows = qT[0, o * K_PASS : (o + 1) * K_PASS, first : first + width]
            nc.sync.dma_start(dst, rows.rearrange("(p t) w -> p t w", t=PACK))

        def load_words(pool, words):
            nc.sync.dma_start(pool[:], words.rearrange("p t b -> p (t b)").bitcast(I32))
            return pool

        def load_scale_rows(pool, first, scales):
            nc.sync.dma_start(pool[first : first + QUAD, :].bitcast(I32), scales.rearrange("o f t -> f o t").bitcast(I32))

        def gather_dealt(dst, window):
            nc.vector.tensor_copy(dst[:].rearrange("p (u s) -> p s u", u=PACK), window.indirect(offsets[:]))

        def move_scales(planes, at, src, first):
            rows = PASSES * QUAD_ROWS
            for quad in (0, 2, 1, 3):
                nc.sync.dma_start(
                    planes[quad * QUAD + at : quad * QUAD + at + QUAD_ROWS].rearrange("p o s -> p (o s)").bitcast(I32),
                    src[first + quad * rows : first + (quad + 1) * rows, :].bitcast(I32),
                )

        def rounded(name, engine_copy, raw, buffer=None):
            dst = tile([P, raw.shape[2], PACK], BF16, name, buffer)
            interleave(engine_copy, dst[:], raw)
            return dst

        def quantise(codes, scales, values):
            nc.vector.quantize_mx(codes.bitcast(FP8X4), scales, values[:].rearrange("p c t -> p (c t)"))

        def quantised(name, q_bf, buffer=None):
            codes = tile([P, HALF], U32, name + "_codes", buffer)
            scales = tile([P, HALF], U8, name + "_scales")
            quantise(codes[:], scales[:], q_bf)
            return codes, scales

        def block(j):
            return slice(j * P, (j + 1) * P)

        def coarse(bank, o, u, q, start=False):
            nc.tensor.matmul_mx(
                bank, kw[:, o, block(u)].bitcast(FP4X4), ks[:, o, block(u)], q[0][:].bitcast(FP8X4), q[1][:], start=start, stop=False
            )

        def fine(bank, o, u, q, stop=False):
            nc.tensor.matmul_mx(
                bank, cw[o][:, block(u)].bitcast(FP8X4), cs[FINE_AT:P, o, block(u)], q[0][:].bitcast(FP8X4), q[1][:], start=False, stop=stop
            )

        warm = tile([P, 16], F32, "warm")
        nc.vector.memset(warm[:, 0:1], 0.0)
        nc.scalar.activation(warm[:, 8:9], warm[:, 0:1], SIGMOID)

        ks_pool = tile([P, T], U8, "ks_pool")
        load_scale_rows(ks_pool, COARSE_ROWS_AT, k_scales)
        offsets = sbuf.tile([P, N // 16], U16, name="offsets")
        nc.sync.dma_start(offsets[:], offs)
        cs_pool = tile([P, T], U8, "cs_pool")
        load_scale_rows(cs_pool, FINE_ROWS_AT, c_scales)
        q_front1 = tile([P, PACK, HALF], F32, "q_front1")
        load_q(1, 0, HALF, q_front1[:])
        th_rows = tile([P, P], F32, "th_rows")
        nc.gpsimd.memset(th_rows[:], 0.0)
        nc.sync.dma_start(th_rows[TH_AT : TH_AT + BLOCKS, :], th[0, 0].rearrange("(j p) -> j p", p=P))
        nc.gpsimd.memset(ks_pool[QUAD : 2 * QUAD, :].bitcast(I32), 0)
        nc.vector.memset(ks_pool[2 * QUAD : P, :].bitcast(I32), 0)
        nc.vector.memset(cs_pool[0 : 2 * QUAD, :].bitcast(I32), 0)
        nc.gpsimd.memset(cs_pool[3 * QUAD : P, :].bitcast(I32), 0)
        ident = tile([P, P], F32, "ident")
        nc.vector.memset(ident[:], 0.0)
        make_identity(nc, ident[:], nomemset=True)
        ks = tile([P, PASSES, N], U8, "ks")
        cs = tile([P, PASSES, N], U8, "cs")
        for planes in (ks, cs):
            nc.gpsimd.memset(planes[:].rearrange("p o s -> p (o s)").bitcast(I32), 0)
        kw_pool = load_words(tile([P, T], I32, "kw_pool"), k_words[0])
        q_pass0 = tile([P, PACK, NQ], F32, "q_pass0")
        load_q(0, 0, NQ, q_pass0[:])

        th_turned = psum.tile([P, P], F32, name="th_turned", tag="back0")
        nc.tensor.transpose(th_turned[:], th_rows[:], ident[:])
        th_cols = tile([P, BLOCKS], F32, "th_cols")
        nc.scalar.copy(th_cols[:], th_turned[:, TH_AT : TH_AT + BLOCKS])
        th_spread = psum.tile([P, NQ], F32, name="th_spread", tag="back1")
        for j in range(BLOCKS):
            nc.tensor.transpose(th_spread[:, block(j)], th_cols[:, j : j + 1].to_broadcast([P, P]), ident[:])
        bf_front1 = rounded("bf_front1", nc.scalar.copy, q_front1[:])
        th_all = tile([P, NQ], F32, "th_all")
        nc.scalar.copy(th_all[:], th_spread[:])

        front = [psum.tile([P, HALF], F32, name=f"front{u}")[:] for u in range(PACK)]
        back_pairs = [psum.tile([P, 2, HALF], F32, name=f"back{pair}") for pair in range(2)]
        back = [back_pairs[u // 2][:, u % 2, :] for u in range(PACK)]

        ks_dealt = tile([P, N], U8, "ks_dealt")
        gather_dealt(ks_dealt, ks_pool[:])
        move_scales(ks, 0, ks_dealt, COARSE_ROWS_AT)
        cw_pool0 = load_words(tile([P, T], I32, "cw_pool0", "ks_pool"), c_words[0])
        cs_dealt = tile([P, N], U8, "cs_dealt")
        gather_dealt(cs_dealt, cs_pool[:])
        cw_pool1 = load_words(tile([P, T], I32, "cw_pool1", "cs_pool"), c_words[1])
        move_scales(cs, FINE_AT, cs_dealt, FINE_ROWS_AT)

        kw_pair = tile([P, N], U32, "kw_pair")
        gather_dealt(kw_pair, kw_pool[:].bitcast(U32))
        kw = tile([P, PASSES, N], U16, "kw")
        nc.vector.tensor_copy(kw[:], kw_pair[:].bitcast(U16).rearrange("p (s o) -> p o s", o=PASSES))
        q_late = [tile([P, PACK, P], F32, f"q_late{j}", buffer) for j, buffer in enumerate(("kw_pool", "kw_pair"))]
        for j in range(2):
            load_q(1, HALF + j * P, P, q_late[j][:])
        bf_front0 = rounded("bf_front0", nc.scalar.copy, q_pass0[:, :, 0:HALF], "ks_dealt")
        bf_back0 = rounded("bf_back0", nc.vector.tensor_copy, q_pass0[:, :, HALF:NQ])
        q0_back = quantised("q0_back", bf_back0)
        for u in range(PACK):
            coarse(back[u], 0, u, q0_back, start=u % 2 == 0)
        q0_front = quantised("q0_front", bf_front0)
        for u in range(PACK):
            coarse(front[u], 0, u, q0_front, start=True)
        cw = [tile([P, N], U32, "cw0", "ks_dealt")]
        gather_dealt(cw[0], cw_pool0[:].bitcast(U32))
        q1_front = quantised("q1_front", bf_front1, "ks_pool")
        for u in range(PACK):
            coarse(front[u], 1, u, q1_front)
        cw.append(tile([P, N], U32, "cw1", "bf_front1"))
        gather_dealt(cw[1], cw_pool1[:].bitcast(U32))
        for u in range(PACK):
            fine(front[u], 0, u, q0_front)
        for u in range(2):
            fine(back[u], 0, u, q0_back)
        for u in range(PACK):
            fine(front[u], 1, u, q1_front, stop=True)
        for u in range(2, PACK):
            fine(back[u], 0, u, q0_back)

        y_scales = tile([P, NQ], U8, "y_scales")
        y_words = tile([P, NQ], I32, "y_words")
        rows_out = out_0.rearrange("(p u) q -> p u q", u=PACK)
        words_out = out_1[0].rearrange("p q t -> p (q t)").bitcast(I32)
        y_back = tile([P, PACK, HALF], F32, "y_back")
        z_back = tile([P, PACK, HALF], F32, "z_back")

        def sigmoid(dst, src):
            nc.scalar.activation(dst, src, SIGMOID)

        def quantise_y(cols, y_bf):
            quantise(y_words[:, cols], y_scales[:, cols], y_bf)
            nc.sync.dma_start(words_out[:, cols], y_words[:, cols])

        bf_late = [rounded(f"bf_late{j}", copy, q_late[j][:]) for j, copy in enumerate((nc.scalar.copy, nc.vector.tensor_copy))]
        q1_back = tile([P, HALF], U32, "q1_back_codes", "cs_pool"), tile([P, HALF], U8, "q1_back_scales")
        for j in range(2):
            quantise(q1_back[0][:, block(j)], q1_back[1][:, block(j)], bf_late[j])
        for u in range(PACK):
            coarse(back[u], 1, u, q1_back)
            fine(back[u], 1, u, q1_back, stop=u % 2 == 1)
        z_front = tile([P, PACK, HALF], F32, "z_front", "kw_pair")
        y_front = tile([P, PACK, HALF], F32, "y_front")
        for u in range(PACK):
            nc.vector.tensor_tensor(z_front[:, u, :], front[u], th_all[:, 0:HALF], SUBTRACT)
            sigmoid(y_front[:, u, :], z_front[:, u, :])
            nc.sync.dma_start(rows_out[:, u : u + 1, 0:HALF], y_front[:, u : u + 1, :])
        y_bf_back = tile([P, HALF, PACK], BF16, "y_bf_back")
        for pair in range(2):
            places = slice(2 * pair, 2 * pair + 2)
            for j in range(2):
                th_block = th_all[:, HALF + j * P : HALF + (j + 1) * P].unsqueeze(1).to_broadcast([P, 2, P])
                nc.vector.tensor_tensor(z_back[:, places, block(j)], back_pairs[pair][:, :, block(j)], th_block, SUBTRACT)
                sigmoid(y_back[:, places, block(j)], z_back[:, places, block(j)])
            nc.sync.dma_start(rows_out[:, places, HALF:NQ], y_back[:, places, :])
        y_bf_front = rounded("y_bf_front", nc.vector.tensor_copy, y_front[:])
        interleave(sigmoid, y_bf_back[:, SHARE:HALF, :], z_back[:, :, SHARE:HALF])
        for cols in (block(0), slice(P, SHARE)):
            interleave(nc.vector.tensor_copy, y_bf_back[:, cols, :], y_back[:, :, cols])
        quantise_y(slice(0, HALF), y_bf_front)
        quantise_y(slice(HALF, NQ), y_bf_back)
        for r in range(QUAD_ROWS):
            queue = nc.scalar if r % 2 == 0 else nc.sync
            queue.dma_start(out_2[0, r:ROWS:QUAD_ROWS, :].bitcast(I32), y_scales[r:P:QUAD, :].bitcast(I32))
